import numpy as np
import ml_dtypes


def mxq(x, axis, fmt="e4m3"):
    dtype, down = {"e4m3": (ml_dtypes.float8_e4m3fn, 7), "e5m2": (ml_dtypes.float8_e5m2, 14)}[fmt]
    v = np.moveaxis(np.asarray(x, np.float32).astype(ml_dtypes.bfloat16).astype(np.float64), axis, -1)
    blocks = v.reshape(v.shape[:-1] + (-1, 32))
    amax = np.abs(blocks).max(-1, keepdims=True)
    byte = np.maximum(np.where(amax > 0, np.frexp(amax)[1] - 1 + 127, 0) - down, 1)
    scale = np.exp2(byte - 127.0)
    codes = (blocks / scale).astype(np.float32).astype(dtype).astype(np.float64)
    return np.moveaxis((codes * scale).reshape(v.shape), -1, axis)


WIDE = False


def mx_kscale(k):
    if not WIDE:
        return np.ones(k)
    levels = np.array([10, -10, 5, -5, 0])
    if k % 512:
        return np.exp2(np.random.permutation(np.resize(levels, k // 32))).repeat(32)
    a = np.empty((k // 512, 16))
    for p in range(k // 512):
        a[p, :8] = np.random.permutation(np.resize(levels, 8))
        for g in range(8):
            far = levels[np.abs(levels - a[p, g]) >= 10]
            a[p, g + 8] = far[np.random.randint(len(far))]
    return np.exp2(a.ravel()).repeat(32)


def f64(x):
    return np.asarray(x).astype(np.float64)


def striped(idx):
    return np.tile(idx.reshape(-1, 16).T, (8, 1)).astype(np.uint16)


def unstriped(offs):
    return offs[:16].T.reshape(-1).astype(np.int64)


E2M1 = np.array([0.0, 0.5, 1.0, 1.5, 2.0, 3.0, 4.0, 6.0, -0.0, -0.5, -1.0, -1.5, -2.0, -3.0, -4.0, -6.0])


def pack_weight(w, fmt):
    k, n = w.shape
    w = f64(np.asarray(w, np.float32).astype(ml_dtypes.bfloat16)).reshape(k // 32, 32, n)
    amax = np.abs(w).max(1)
    if fmt == "e4m3":
        byte = np.frexp(amax)[1] - 1 + 127 - 7
    else:
        mant, ex = np.frexp(amax / 6.0)
        byte = np.where(mant > 0.5, ex, ex - 1) + 127
    byte = np.clip(np.where(amax > 0, byte, 1), 1, 254)
    scaled = (w * np.exp2(127.0 - byte)[:, None, :]).reshape(k, n).astype(np.float32)
    by_word = np.ascontiguousarray(scaled.reshape(k // 512, 128, 4, n).transpose(0, 1, 3, 2))
    if fmt == "e4m3":
        words = by_word.astype(ml_dtypes.float8_e4m3fn).view(np.uint8)
    else:
        c = by_word.astype(ml_dtypes.float4_e2m1fn).view(np.uint8) & 0xF
        words = (c[..., 0::2] | (c[..., 1::2] << 4)).reshape(k // 512, 128, 2 * n)
    return np.ascontiguousarray(words), np.ascontiguousarray(byte.astype(np.uint8).reshape(k // 512, 16, n))


def unpack_weight(words, scales, fmt):
    g, _, n = scales.shape
    words = np.ascontiguousarray(words).reshape(g, 128, n, -1)
    if fmt == "e4m3":
        vals = words.view(ml_dtypes.float8_e4m3fn).astype(np.float64)
    else:
        nib = np.empty((g, 128, n, 4), np.uint8)
        nib[..., 0::2] = words & 0xF
        nib[..., 1::2] = words >> 4
        vals = E2M1[nib]
    vals = vals * np.repeat(np.exp2(scales.astype(np.float64) - 127.0), 8, axis=1)[..., None]
    return vals.transpose(0, 1, 3, 2).reshape(g * 512, n)


def gelu(v):
    return 0.5 * v * (1.0 + np.tanh(np.sqrt(2.0 / np.pi) * (v + 0.044715 * v**3)))


def bf(x):
    return np.asarray(x, np.float32).astype(ml_dtypes.bfloat16)

def planes(Y):
    n, m = Y.shape
    b = f64(bf(Y)).reshape(n // 32, 32, m)
    amax = np.abs(b).max(1)
    byte = np.clip(np.where(amax > 0, np.frexp(amax)[1] - 1 + 127 - 7, 1), 1, 254)
    codes = (b * np.exp2(127.0 - byte)[:, None, :]).reshape(n, m).astype(np.float32).astype(ml_dtypes.float8_e4m3fn).view(np.uint8)
    words = codes.reshape(n // 512, 128, 4, m).transpose(0, 1, 3, 2)
    return np.ascontiguousarray(words), np.ascontiguousarray(byte.astype(np.uint8).reshape(n // 512, 16, m))


K, T, S, N, M = 1536, 2048, 1024, 1024, 512

def setup_inputs():
    n = np.random.standard_normal
    s = mx_kscale(K)[:, None]
    u = mx_kscale(S)
    idx = np.random.permutation(T)[:S]
    tab_words, tab_scales = pack_weight(n((K, T)) / np.sqrt(K) * s, "e4m3")
    x_words, x_scales = pack_weight(n((K, M)) / s, "e2m1")
    wdT = n((N, T)) / np.sqrt(S) * np.exp(0.8 * n((N, 1)))
    wdT[:, idx] /= u[None, :]
    return {
        "tab_words": tab_words, "tab_scales": tab_scales,
        "x_words": x_words, "x_scales": x_scales,
        "offs": striped(idx),
        "prev": n((S, M)).astype(np.float32),
        "leak": (0.5 + 0.4 * np.random.random(S)).astype(np.float32),
        "thr": (0.3 * np.exp(0.3 * n(S))).astype(np.float32),
        "g": (np.exp(0.3 * n(S)) * u).astype(np.float32),
        "wdT": wdT.astype(np.float32),
    }

def reference(tab_words, tab_scales, x_words, x_scales, offs, prev, leak, thr, g, wdT):
    v = unpack_weight(tab_words, tab_scales, "e4m3")[:, unstriped(offs)]
    x = unpack_weight(x_words, x_scales, "e2m1")
    pot = (v.T @ x) + f64(leak)[:, None] * f64(prev)
    h = np.maximum(pot - f64(thr)[:, None], 0.0) * f64(g)[:, None]
    wd = f64(wdT)[:, unstriped(offs)]
    y = mxq(wd, 1, "e4m3") @ mxq(h, 0, "e4m3")
    words, scales = planes(y)
    return y, words, scales

@@ -1,0 +1,207 @@
+from contextlib import ExitStack
+
+import concourse.mybir as mybir
+from concourse.masks import make_identity
+
+K, T, S, N, M = 1536, 2048, 1024, 1024, 512
+FLOPS = 2 * K * S * M + 2 * S * N * M
+
+F32 = mybir.dt.float32
+BF16 = mybir.dt.bfloat16
+I32 = mybir.dt.int32
+U32 = mybir.dt.uint32
+U16 = mybir.dt.uint16
+U8 = mybir.dt.uint8
+FP8X4 = mybir.dt.float8_e4m3fn_x4
+FP4X4 = mybir.dt.float4_e2m1fn_x4
+ALU = mybir.AluOpType
+ACT = mybir.ActivationFunctionType
+
+P = 128
+PACK = 4
+K_PASSES = K // (P * PACK)
+J_PASSES = S // (P * PACK)
+N_GROUPS = N // (P * PACK)
+QUADS = 4
+MOVED_ROWS = 112
+
+
+def tile_list_leaky_event_layer_kernel(
+    tc, tab_words, tab_scales, x_words, x_scales, offs, prev, leak, thr, g, wdT, out_0, out_1, out_2
+):
+    nc = tc.nc
+    with ExitStack() as ctx:
+        keep = ctx.enter_context(tc.tile_pool(name="keep", bufs=1))
+        ring = ctx.enter_context(tc.tile_pool(name="ring", bufs=3))
+        psum = ctx.enter_context(tc.psum_pool(name="psum", bufs=1))
+
+        offsets = keep.tile([P, S // 16], U16, name="offsets")
+        nc.sync.dma_start(offsets[:], offs)
+
+        tab_planes = keep.tile([P, T], U8, name="tab_planes", align_bytes=64)
+        nc.gpsimd.memset(tab_planes[:].bitcast(I32), 0)
+        for q in range(QUADS):
+            nc.gpsimd.dma_start(
+                out=tab_planes[32 * q : 32 * q + 4 * K_PASSES, :].bitcast(I32),
+                in_=tab_scales[:, 4 * q : 4 * q + 4, :].bitcast(I32),
+            )
+
+        x_planes = keep.tile([P, K_PASSES, M], U8, name="x_planes", align_bytes=64)
+        nc.vector.memset(x_planes[:].rearrange("p a m -> p (a m)").bitcast(I32), 0)
+        for q in range(QUADS):
+            nc.gpsimd.dma_start(
+                out=x_planes[32 * q : 32 * q + 4, :, :].bitcast(I32),
+                in_=x_scales[:, 4 * q : 4 * q + 4, :].rearrange("a r m -> r a m").bitcast(I32),
+            )
+        leak_sb = keep.tile([P, J_PASSES, PACK], F32, name="leak_sb")
+        thr_sb = keep.tile([P, J_PASSES, PACK], F32, name="thr_sb")
+        gain_sb = keep.tile([P, J_PASSES, PACK], F32, name="gain_sb")
+        v_planes = [keep.tile([P, S], U8, name="v_planes%d" % a, align_bytes=64) for a in range(K_PASSES)]
+        for a in range(1, K_PASSES):
+            nc.vector.memset(v_planes[a][:].bitcast(I32), 0)
+        identity = keep.tile([P, P], F32, name="identity")
+        make_identity(nc, identity[:])
+
+        tab_sb = [keep.tile([P, T], I32, name="tab_sb%d" % a) for a in range(K_PASSES)]
+        x_sb = keep.tile([P, K_PASSES, 2 * M], U8, name="x_sb", align_bytes=64)
+        prev_sb = [keep.tile([P, PACK, M], F32, name="prev_sb%d" % b) for b in range(J_PASSES)]
+        wd_sb = [keep.tile([P, T], F32, name="wd_sb%d" % i) for i in range(N_GROUPS * PACK)]
+        prev_rows = prev.rearrange("(b p t) m -> b p t m", b=J_PASSES, t=PACK)
+        wd_rows = wdT.rearrange("(c p t) j -> c t p j", c=N_GROUPS, t=PACK)
+
+        for a in range(K_PASSES):
+            nc.sync.dma_start(out=tab_sb[a][:], in_=tab_words[a].rearrange("p n t -> p (n t)").bitcast(I32))
+        nc.sync.dma_start(out=x_sb[:].bitcast(I32), in_=x_words.rearrange("a p n -> p a n").bitcast(I32))
+        for vec_sb, vec in ((leak_sb, leak), (thr_sb, thr), (gain_sb, g)):
+            nc.sync.dma_start(out=vec_sb[:], in_=vec.rearrange("(b p t) -> p b t", b=J_PASSES, t=PACK))
+        minus_thr = keep.tile([P, J_PASSES, PACK], F32, name="minus_thr")
+        nc.gpsimd.tensor_scalar(minus_thr[:], thr_sb[:], -1.0, 0.0, ALU.mult, ALU.add)
+        for i in range(N_GROUPS * PACK):
+            nc.sync.dma_start(out=wd_sb[i][:], in_=wd_rows[i // PACK, i % PACK])
+            if i < J_PASSES:
+                nc.sync.dma_start(out=prev_sb[i][:], in_=prev_rows[i])
+
+        picked_planes = keep.tile([P, S], U8, name="picked_planes", align_bytes=64)
+        nc.vector.tensor_copy(picked_planes[:], tab_planes[:].indirect(offsets[:]))
+        nc.vector.tensor_copy(
+            v_planes[0][:].rearrange("p (t s) -> p t s", t=PACK),
+            picked_planes[:].rearrange("p (s t) -> p t s", t=PACK),
+        )
+        for a in range(1, K_PASSES):
+            nc.scalar.dma_start(
+                out=v_planes[a][0:MOVED_ROWS, :].bitcast(I32),
+                in_=v_planes[0][4 * a : 4 * a + MOVED_ROWS, :].bitcast(I32),
+            )
+        v_words = [keep.tile([P, S], U32, name="v_words%d" % a, align_bytes=64) for a in range(K_PASSES)]
+        for a in range(K_PASSES):
+            nc.vector.tensor_copy(
+                v_words[a][:].rearrange("p (t s) -> p s t", t=PACK),
+                tab_sb[a][:].bitcast(U32).indirect(offsets[:]),
+            )
+
+        h_words = [keep.tile([P, M], U32, name="h_words%d" % b, align_bytes=64) for b in range(J_PASSES)]
+        h_planes = [keep.tile([P, M], U8, name="h_planes%d" % b, align_bytes=64) for b in range(J_PASSES)]
+
+        def make_h(b):
+            h_rows = keep.tile([P, PACK, M], BF16, name="h_rows%d" % b)
+            for t in range(PACK):
+                cols = slice(t * J_PASSES * P + b * P, t * J_PASSES * P + (b + 1) * P)
+                current = psum.tile([P, M], F32, name="current", bufs=3)
+                for a in range(K_PASSES):
+                    nc.tensor.matmul_mx(
+                        out=current[:],
+                        lhsT=v_words[a][:, cols].bitcast(FP8X4),
+                        lhsT_scale=v_planes[a][:, cols],
+                        rhs=x_sb[:, a, :].bitcast(FP4X4),
+                        rhs_scale=x_planes[:, a, :],
+                        start=(a == 0),
+                        stop=(a == K_PASSES - 1),
+                    )
+                pot = ring.tile([P, M], F32, name="pot")
+                nc.vector.scalar_tensor_tensor(
+                    pot[:], prev_sb[b][:, t, :], leak_sb[:, b, t : t + 1], current[:], ALU.mult, ALU.add
+                )
+                above = ring.tile([P, M], F32, name="above")
+                nc.scalar.activation(above[:], pot[:], ACT.Relu, bias=minus_thr[:, b, t : t + 1])
+                nc.scalar.activation(h_rows[:, t, :], above[:], ACT.Copy, scale=gain_sb[:, b, t : t + 1])
+            h_grouped = keep.tile([P, M, PACK], BF16, name="h_grouped%d" % b, align_bytes=64)
+            nc.scalar.copy(
+                h_grouped[:].rearrange("p (c i) t -> p c t i", i=4),
+                h_rows[:].rearrange("p t (c i) -> p c t i", i=4),
+            )
+            nc.vector.quantize_mx(
+                out=h_words[b][:].bitcast(FP8X4),
+                scales=h_planes[b][:],
+                in_=h_grouped[:].rearrange("p m t -> p (m t)"),
+            )
+
+        wd_words = [keep.tile([P, J_PASSES * P], U32, name="wd_words%d" % i, align_bytes=64) for i in range(N_GROUPS * PACK)]
+        wd_planes = [keep.tile([P, J_PASSES * P], U8, name="wd_planes%d" % i, align_bytes=64) for i in range(N_GROUPS * PACK)]
+
+        def make_wd(i):
+            picked = ring.tile([P, S], BF16, name="picked")
+            nc.vector.tensor_copy(picked[:], wd_sb[i][:].indirect(offsets[:]))
+            pairs = picked[:].bitcast(F32)
+            turned = psum.tile([P, J_PASSES, 2, P], F32, name="turned", bufs=2)
+            for b in range(J_PASSES):
+                for u in range(2):
+                    nc.tensor.transpose(turned[:, b, u, :], pairs[:, 2 * P * b + u : 2 * P * (b + 1) : 2], identity[:])
+            wd_grouped = ring.tile([P, J_PASSES * P * PACK], BF16, name="wd_grouped", align_bytes=64)
+            nc.scalar.copy(
+                wd_grouped[:].bitcast(F32).rearrange("p (b c u) -> p b c u", b=J_PASSES, u=2),
+                turned[:].rearrange("p b u c -> p b c u"),
+            )
+            nc.vector.quantize_mx(out=wd_words[i][:].bitcast(FP8X4), scales=wd_planes[i][:], in_=wd_grouped[:])
+
+        y_rows = out_0.rearrange("(c p t) m -> c p t m", c=N_GROUPS, t=PACK)
+        y_sb = [keep.tile([P, PACK, M], F32, name="y_sb%d" % c) for c in range(N_GROUPS)]
+        y_planes = keep.tile([P, N_GROUPS, M], U8, name="y_planes", align_bytes=64)
+
+        def make_y(i):
+            c, t = divmod(i, PACK)
+            acc = psum.tile([P, M], F32, name="acc", bufs=3)
+            for b in range(J_PASSES):
+                nc.tensor.matmul_mx(
+                    out=acc[:],
+                    lhsT=wd_words[i][:, b * P : (b + 1) * P].bitcast(FP8X4),
+                    lhsT_scale=wd_planes[i][:, b * P : (b + 1) * P],
+                    rhs=h_words[b][:].bitcast(FP8X4),
+                    rhs_scale=h_planes[b][:],
+                    start=(b == 0),
+                    stop=(b == J_PASSES - 1),
+                )
+            nc.scalar.copy(y_sb[c][:, t, :], acc[:])
+            nc.sync.dma_start(out=y_rows[c, :, t, :], in_=y_sb[c][:, t, :])
+
+        def make_y_planes(c, copy):
+            y_grouped = keep.tile([P, M, PACK], BF16, name="y_grouped%d" % c, align_bytes=64)
+            copy(
+                y_grouped[:].rearrange("p (c i) t -> p c t i", i=4),
+                y_sb[c][:].rearrange("p t (c i) -> p c t i", i=4),
+            )
+            y_words = keep.tile([P, M], I32, name="y_words%d" % c, align_bytes=64)
+            nc.vector.quantize_mx(
+                out=y_words[:].bitcast(FP8X4),
+                scales=y_planes[:, c, :],
+                in_=y_grouped[:].rearrange("p m t -> p (m t)"),
+            )
+            nc.sync.dma_start(out=out_1[c].rearrange("p m t -> p (m t)").bitcast(I32), in_=y_words[:])
+
+        make_wd(0)
+        make_h(0)
+        make_wd(1)
+        make_h(1)
+        for i in range(2, N_GROUPS * PACK):
+            make_wd(i)
+            make_y(i - 2)
+            if i - 2 == PACK - 1:
+                make_y_planes(0, nc.scalar.copy)
+        make_y(N_GROUPS * PACK - 2)
+        make_y(N_GROUPS * PACK - 1)
+        make_y_planes(1, nc.vector.tensor_copy)
+        for q in range(QUADS):
+            queue = nc.scalar if q % 2 else nc.sync
+            queue.dma_start(
+                out=out_2[:, 4 * q : 4 * q + 4, :].rearrange("c r m -> r c m").bitcast(I32),
+                in_=y_planes[32 * q : 32 * q + 4, :, :].bitcast(I32),
+            )

@@ -24,6 +24,11 @@ J_PASSES = S // (P * PACK)
 N_GROUPS = N // (P * PACK)
 QUADS = 4
 MOVED_ROWS = 112
+BIG = 3.0e38
+WINDOW_BYTES = 4 * T
+UNITS = [(i, 1) for i in range(8)]
+LOADS = [("tab", 0, 0), ("tab", 1, 0), ("tab_planes", 0, 0), ("tab", 2, 0), ("x_planes", 0, 0), ("x", 0, 0), ("wd", 0, 0), ("vec", 0, 0), ("vec", 1, 0), ("vec", 2, 0), ("prev", 0, 0)]
+LATER_LOADS = [("prev", 1, 0), ("wd", 1, 0), ("wd", 2, 0), ("wd", 3, 0), ("wd", 4, 0), ("wd", 5, 0), ("wd", 6, 0), ("wd", 7, 0)]
 
 
 def tile_list_leaky_event_layer_kernel(
@@ -32,99 +37,159 @@ def tile_list_leaky_event_layer_kernel(
     nc = tc.nc
     with ExitStack() as ctx:
         keep = ctx.enter_context(tc.tile_pool(name="keep", bufs=1))
+        placed = ctx.enter_context(tc.tile_pool(name="placed", bufs=1))
         ring = ctx.enter_context(tc.tile_pool(name="ring", bufs=3))
         psum = ctx.enter_context(tc.psum_pool(name="psum", bufs=1))
+
+        def over_window(k, at, shape, dtype, name):
+            if k is None:
+                return keep.tile(shape, dtype, name=name, align_bytes=64)
+            return placed.tile(shape, dtype, name=name, align_bytes=64, offset=k * WINDOW_BYTES + at)
+
+        bank_turn = [n % 8 for n in range(64)]
+
+        def next_bank(shape):
+            return psum.tile(shape, F32, name="bank%d" % bank_turn.pop(0))
 
         offsets = keep.tile([P, S // 16], U16, name="offsets")
         nc.sync.dma_start(offsets[:], offs)
 
         tab_planes = keep.tile([P, T], U8, name="tab_planes", align_bytes=64)
-        nc.gpsimd.memset(tab_planes[:].bitcast(I32), 0)
-        for q in range(QUADS):
-            nc.gpsimd.dma_start(
-                out=tab_planes[32 * q : 32 * q + 4 * K_PASSES, :].bitcast(I32),
-                in_=tab_scales[:, 4 * q : 4 * q + 4, :].bitcast(I32),
-            )
-
-        x_planes = keep.tile([P, K_PASSES, M], U8, name="x_planes", align_bytes=64)
-        nc.vector.memset(x_planes[:].rearrange("p a m -> p (a m)").bitcast(I32), 0)
-        for q in range(QUADS):
-            nc.gpsimd.dma_start(
-                out=x_planes[32 * q : 32 * q + 4, :, :].bitcast(I32),
-                in_=x_scales[:, 4 * q : 4 * q + 4, :].rearrange("a r m -> r a m").bitcast(I32),
-            )
-        leak_sb = keep.tile([P, J_PASSES, PACK], F32, name="leak_sb")
-        thr_sb = keep.tile([P, J_PASSES, PACK], F32, name="thr_sb")
-        gain_sb = keep.tile([P, J_PASSES, PACK], F32, name="gain_sb")
-        v_planes = [keep.tile([P, S], U8, name="v_planes%d" % a, align_bytes=64) for a in range(K_PASSES)]
-        for a in range(1, K_PASSES):
-            nc.vector.memset(v_planes[a][:].bitcast(I32), 0)
+        nc.vector.memset(tab_planes[:].bitcast(I32), 0)
         identity = keep.tile([P, P], F32, name="identity")
         make_identity(nc, identity[:])
 
+        x_planes = keep.tile([P, K_PASSES, M], U8, name="x_planes", align_bytes=64)
+        v_planes = [keep.tile([P, S], U8, name="v_planes%d" % a, align_bytes=64) for a in range(K_PASSES)]
+
+        leak_sb = keep.tile([P, J_PASSES * PACK], F32, name="leak_sb")
+        thr_sb = keep.tile([P, J_PASSES * PACK], F32, name="thr_sb")
+        gain_sb = keep.tile([P, J_PASSES * PACK], F32, name="gain_sb")
         tab_sb = [keep.tile([P, T], I32, name="tab_sb%d" % a) for a in range(K_PASSES)]
         x_sb = keep.tile([P, K_PASSES, 2 * M], U8, name="x_sb", align_bytes=64)
-        prev_sb = [keep.tile([P, PACK, M], F32, name="prev_sb%d" % b) for b in range(J_PASSES)]
-        wd_sb = [keep.tile([P, T], F32, name="wd_sb%d" % i) for i in range(N_GROUPS * PACK)]
+        prev_sb = [over_window((None, len(UNITS))[b], 0, [P, PACK, M], F32, "prev_sb%d" % b) for b in range(J_PASSES)]
         prev_rows = prev.rearrange("(b p t) m -> b p t m", b=J_PASSES, t=PACK)
-        wd_rows = wdT.rearrange("(c p t) j -> c t p j", c=N_GROUPS, t=PACK)
+        wd_rows = wdT.rearrange("(c p t) j -> c p t j", c=N_GROUPS, t=PACK)
+        windows = [over_window(k, 0, [P, T], F32 if n == 1 else U32, "window%d" % k) for k, (i, n) in enumerate(UNITS)]
 
-        for a in range(K_PASSES):
-            nc.sync.dma_start(out=tab_sb[a][:], in_=tab_words[a].rearrange("p n t -> p (n t)").bitcast(I32))
-        nc.sync.dma_start(out=x_sb[:].bitcast(I32), in_=x_words.rearrange("a p n -> p a n").bitcast(I32))
-        for vec_sb, vec in ((leak_sb, leak), (thr_sb, thr), (gain_sb, g)):
-            nc.sync.dma_start(out=vec_sb[:], in_=vec.rearrange("(b p t) -> p b t", b=J_PASSES, t=PACK))
-        minus_thr = keep.tile([P, J_PASSES, PACK], F32, name="minus_thr")
-        nc.gpsimd.tensor_scalar(minus_thr[:], thr_sb[:], -1.0, 0.0, ALU.mult, ALU.add)
-        for i in range(N_GROUPS * PACK):
-            nc.sync.dma_start(out=wd_sb[i][:], in_=wd_rows[i // PACK, i % PACK])
-            if i < J_PASSES:
-                nc.sync.dma_start(out=prev_sb[i][:], in_=prev_rows[i])
+        def load(kind, k, half):
+            if kind == "tab_planes":
+                for q in range(QUADS):
+                    nc.sync.dma_start(
+                        out=tab_planes[32 * q : 32 * q + 4 * K_PASSES, :].bitcast(I32),
+                        in_=tab_scales[:, 4 * q : 4 * q + 4, :].bitcast(I32),
+                    )
+            elif kind == "tab":
+                nc.sync.dma_start(out=tab_sb[k][:], in_=tab_words[k].rearrange("p n t -> p (n t)").bitcast(I32))
+            elif kind == "x":
+                nc.sync.dma_start(out=x_sb[:].bitcast(I32), in_=x_words.rearrange("a p n -> p a n").bitcast(I32))
+            elif kind == "x_planes":
+                for q in range(QUADS):
+                    nc.sync.dma_start(
+                        out=x_planes[32 * q : 32 * q + 4, :, :].bitcast(I32),
+                        in_=x_scales[:, 4 * q : 4 * q + 4, :].rearrange("a r m -> r a m").bitcast(I32),
+                    )
+            elif kind == "vec":
+                vec_sb, vec = ((gain_sb, g), (leak_sb, leak), (thr_sb, thr))[k]
+                nc.sync.dma_start(
+                    out=vec_sb[:].rearrange("p (b t) -> p b t", t=PACK),
+                    in_=vec.rearrange("(b p t) -> p b t", b=J_PASSES, t=PACK),
+                )
+            elif kind == "prev":
+                nc.sync.dma_start(out=prev_sb[k][:], in_=prev_rows[k])
+            elif kind == "wd":
+                c, t = divmod(UNITS[k][0], PACK)
+                nc.sync.dma_start(out=windows[k][:], in_=wd_rows[c, :, t, :])
+            else:
+                c, t = divmod(UNITS[k][0], PACK)
+                cols = slice(half * T // 2, (half + 1) * T // 2)
+                two_rows = ring.tile([P, 2, T // 2], F32, name="two_rows", bufs=2)
+                nc.sync.dma_start(out=two_rows[:], in_=wd_rows[c, :, t : t + 2, cols])
+                nc.scalar.copy(
+                    windows[k][:, cols].bitcast(BF16).rearrange("p (j e) -> p j e", e=2),
+                    two_rows[:].rearrange("p e j -> p j e"),
+                )
+
+        for item in LOADS:
+            load(*item)
+
+        gain_leak = keep.tile([P, J_PASSES * PACK], F32, name="gain_leak")
+        gain_thr = keep.tile([P, J_PASSES * PACK], F32, name="gain_thr")
+        minus_gain_thr = keep.tile([P, J_PASSES * PACK], F32, name="minus_gain_thr")
+        upper = keep.tile([P, J_PASSES * PACK], F32, name="upper")
+        lower = keep.tile([P, J_PASSES * PACK], F32, name="lower")
+        nc.gpsimd.tensor_tensor(gain_leak[:], gain_sb[:], leak_sb[:], ALU.mult)
+        nc.gpsimd.tensor_tensor(gain_thr[:], gain_sb[:], thr_sb[:], ALU.mult)
+        nc.gpsimd.tensor_scalar(minus_gain_thr[:], gain_thr[:], -1.0, 0.0, ALU.mult, ALU.add)
+        nc.gpsimd.tensor_scalar(upper[:], gain_sb[:], 0.0, BIG, ALU.is_ge, ALU.mult)
+        nc.gpsimd.tensor_scalar(lower[:], gain_sb[:], 0.0, -BIG, ALU.is_lt, ALU.mult)
 
         picked_planes = keep.tile([P, S], U8, name="picked_planes", align_bytes=64)
+        v_words = [keep.tile([P, S], U32, name="v_words%d" % a, align_bytes=64) for a in range(K_PASSES - 1)]
+
+        def pick_words(a):
+            nc.vector.tensor_copy(
+                v_words[a][:].rearrange("p (t s) -> p s t", t=PACK),
+                tab_sb[a][:].bitcast(U32).indirect(offsets[:]),
+            )
+
+        pick_words(0)
         nc.vector.tensor_copy(picked_planes[:], tab_planes[:].indirect(offsets[:]))
         nc.vector.tensor_copy(
             v_planes[0][:].rearrange("p (t s) -> p t s", t=PACK),
             picked_planes[:].rearrange("p (s t) -> p t s", t=PACK),
         )
         for a in range(1, K_PASSES):
-            nc.scalar.dma_start(
+            nc.sync.dma_start(
                 out=v_planes[a][0:MOVED_ROWS, :].bitcast(I32),
                 in_=v_planes[0][4 * a : 4 * a + MOVED_ROWS, :].bitcast(I32),
             )
-        v_words = [keep.tile([P, S], U32, name="v_words%d" % a, align_bytes=64) for a in range(K_PASSES)]
-        for a in range(K_PASSES):
+        for item in LATER_LOADS:
+            load(*item)
+        pick_words(1)
+        last_words = [keep.tile([P, S // J_PASSES], U32, name="last_words%d" % b, align_bytes=64) for b in range(J_PASSES)]
+        for b in range(J_PASSES):
             nc.vector.tensor_copy(
-                v_words[a][:].rearrange("p (t s) -> p s t", t=PACK),
-                tab_sb[a][:].bitcast(U32).indirect(offsets[:]),
+                last_words[b][:].rearrange("p (t s) -> p s t", t=PACK),
+                tab_sb[K_PASSES - 1][:].bitcast(U32).indirect(offsets[:, 32 * b : 32 * (b + 1)]),
             )
 
-        h_words = [keep.tile([P, M], U32, name="h_words%d" % b, align_bytes=64) for b in range(J_PASSES)]
+        h_words = [over_window((1, 2)[b], 4096, [P, M], U32, "h_words%d" % b) for b in range(J_PASSES)]
         h_planes = [keep.tile([P, M], U8, name="h_planes%d" % b, align_bytes=64) for b in range(J_PASSES)]
+
+        rests = [[keep.tile([P, M], F32, name="rest%d_%d" % (b, t)) for t in range(PACK)] for b in range(J_PASSES)]
+        for b in range(J_PASSES):
+            for t in range(PACK):
+                bt = slice(b * PACK + t, b * PACK + t + 1)
+                nc.scalar.activation(rests[b][t][:], prev_sb[b][:, t, :], ACT.Identity, bias=minus_gain_thr[:, bt], scale=gain_leak[:, bt])
 
         def make_h(b):
             h_rows = keep.tile([P, PACK, M], BF16, name="h_rows%d" % b)
+            rest = rests[b]
+            for t in range(0):
+                bt = slice(b * PACK + t, b * PACK + t + 1)
+                if ("scalar", "scalar")[b] == "scalar":
+                    nc.scalar.activation(rest[t][:], prev_sb[b][:, t, :], ACT.Identity, bias=minus_gain_thr[:, bt], scale=gain_leak[:, bt])
+                else:
+                    nc.gpsimd.tensor_scalar(rest[t][:], prev_sb[b][:, t, :], gain_leak[:, bt], minus_gain_thr[:, bt], ALU.mult, ALU.add)
             for t in range(PACK):
+                bt = slice(b * PACK + t, b * PACK + t + 1)
                 cols = slice(t * J_PASSES * P + b * P, t * J_PASSES * P + (b + 1) * P)
-                current = psum.tile([P, M], F32, name="current", bufs=3)
+                current = next_bank([P, M])
                 for a in range(K_PASSES):
                     nc.tensor.matmul_mx(
                         out=current[:],
-                        lhsT=v_words[a][:, cols].bitcast(FP8X4),
+                        lhsT=(v_words[a][:, cols] if a < K_PASSES - 1 else last_words[b][:, t * P : (t + 1) * P]).bitcast(FP8X4),
                         lhsT_scale=v_planes[a][:, cols],
                         rhs=x_sb[:, a, :].bitcast(FP4X4),
                         rhs_scale=x_planes[:, a, :],
                         start=(a == 0),
                         stop=(a == K_PASSES - 1),
                     )
-                pot = ring.tile([P, M], F32, name="pot")
-                nc.vector.scalar_tensor_tensor(
-                    pot[:], prev_sb[b][:, t, :], leak_sb[:, b, t : t + 1], current[:], ALU.mult, ALU.add
-                )
-                above = ring.tile([P, M], F32, name="above")
-                nc.scalar.activation(above[:], pot[:], ACT.Relu, bias=minus_thr[:, b, t : t + 1])
-                nc.scalar.activation(h_rows[:, t, :], above[:], ACT.Copy, scale=gain_sb[:, b, t : t + 1])
-            h_grouped = keep.tile([P, M, PACK], BF16, name="h_grouped%d" % b, align_bytes=64)
+                scaled = ring.tile([P, M], F32, name="scaled", bufs=4)
+                nc.vector.scalar_tensor_tensor(scaled[:], current[:], gain_sb[:, bt], rest[t][:], ALU.mult, ALU.add)
+                nc.gpsimd.tensor_scalar(h_rows[:, t, :], scaled[:], upper[:, bt], lower[:, bt], ALU.min, ALU.max)
+            h_grouped = over_window((len(UNITS), None)[b], 0, [P, M, PACK], BF16, "h_grouped%d" % b)
             nc.scalar.copy(
                 h_grouped[:].rearrange("p (c i) t -> p c t i", i=4),
                 h_rows[:].rearrange("p t (c i) -> p c t i", i=4),
@@ -135,70 +200,116 @@ def tile_list_leaky_event_layer_kernel(
                 in_=h_grouped[:].rearrange("p m t -> p (m t)"),
             )
 
-        wd_words = [keep.tile([P, J_PASSES * P], U32, name="wd_words%d" % i, align_bytes=64) for i in range(N_GROUPS * PACK)]
-        wd_planes = [keep.tile([P, J_PASSES * P], U8, name="wd_planes%d" % i, align_bytes=64) for i in range(N_GROUPS * PACK)]
+        wd_codes = {}
 
-        def make_wd(i):
-            picked = ring.tile([P, S], BF16, name="picked")
-            nc.vector.tensor_copy(picked[:], wd_sb[i][:].indirect(offsets[:]))
-            pairs = picked[:].bitcast(F32)
-            turned = psum.tile([P, J_PASSES, 2, P], F32, name="turned", bufs=2)
-            for b in range(J_PASSES):
-                for u in range(2):
-                    nc.tensor.transpose(turned[:, b, u, :], pairs[:, 2 * P * b + u : 2 * P * (b + 1) : 2], identity[:])
-            wd_grouped = ring.tile([P, J_PASSES * P * PACK], BF16, name="wd_grouped", align_bytes=64)
-            nc.scalar.copy(
-                wd_grouped[:].bitcast(F32).rearrange("p (b c u) -> p b c u", b=J_PASSES, u=2),
-                turned[:].rearrange("p b u c -> p b c u"),
-            )
-            nc.vector.quantize_mx(out=wd_words[i][:].bitcast(FP8X4), scales=wd_planes[i][:], in_=wd_grouped[:])
+        def make_wd(k):
+            first, n = UNITS[k]
+            last = k == len(UNITS) - 1
+            if n == 2:
+                words = over_window(k + 1, 0, [P, 2 * J_PASSES * P], U32, "wd_words%d" % k)
+                planes = keep.tile([P, 2 * J_PASSES * P], U8, name="wd_planes%d" % k, align_bytes=64)
+                picked = keep.tile([P, S], U32, name="picked_pairs%d" % k)
+                nc.vector.tensor_copy(
+                    picked[:].rearrange("p (t s) -> p s t", t=PACK), windows[k][:].indirect(offsets[:])
+                )
+                grouped = keep.tile([P, 2, J_PASSES, P, PACK], BF16, name="pair_grouped%d" % k, align_bytes=64)
+                for b in range(J_PASSES):
+                    turned = next_bank([P, PACK, P])
+                    for t in range(PACK):
+                        at = t * J_PASSES * P + b * P
+                        nc.tensor.transpose(turned[:, t, :], picked[:, at : at + P].bitcast(F32), identity[:])
+                    nc.scalar.copy(
+                        grouped[:, :, b, :, :],
+                        turned[:].bitcast(BF16).rearrange("p t (c e) -> p e c t", e=2),
+                    )
+                nc.vector.quantize_mx(
+                    out=words[:].bitcast(FP8X4), scales=planes[:], in_=grouped[:].rearrange("p e b c t -> p (e b c t)")
+                )
+                for e in range(2):
+                    for b in range(J_PASSES):
+                        at = (e * J_PASSES + b) * P
+                        wd_codes[first + e, b] = (words[:, at : at + P], planes[:, at : at + P])
+                return
+            parts = [[b] for b in range(J_PASSES)] if last else [list(range(J_PASSES))]
+            for part in parts:
+                nb = len(part)
+                name = "%d_%d" % (k, part[0])
+                words = over_window(None if last else k + 1, 0, [P, nb * P], U32, "wd_words" + name)
+                planes = keep.tile([P, nb * P], U8, name="wd_planes" + name, align_bytes=64)
+                picked = ring.tile([P, nb * P * PACK], BF16, name="picked")
+                lists = offsets[:, part[0] * 32 : (part[0] + nb) * 32]
+                nc.vector.tensor_copy(picked[:], windows[k][:].indirect(lists))
+                pairs = picked[:].bitcast(F32)
+                turned = next_bank([P, nb, 2, P])
+                for b in range(nb):
+                    for u in range(2):
+                        nc.tensor.transpose(turned[:, b, u, :], pairs[:, 2 * P * b + u : 2 * P * (b + 1) : 2], identity[:])
+                grouped = ring.tile([P, nb * P * PACK], BF16, name="wd_grouped", align_bytes=64)
+                nc.scalar.copy(
+                    grouped[:].bitcast(F32).rearrange("p (b c u) -> p b c u", b=nb, u=2),
+                    turned[:].rearrange("p b u c -> p b c u"),
+                )
+                nc.vector.quantize_mx(out=words[:].bitcast(FP8X4), scales=planes[:], in_=grouped[:])
+                for b in range(nb):
+                    wd_codes[first, part[b]] = (words[:, b * P : (b + 1) * P], planes[:, b * P : (b + 1) * P])
 
         y_rows = out_0.rearrange("(c p t) m -> c p t m", c=N_GROUPS, t=PACK)
         y_sb = [keep.tile([P, PACK, M], F32, name="y_sb%d" % c) for c in range(N_GROUPS)]
         y_planes = keep.tile([P, N_GROUPS, M], U8, name="y_planes", align_bytes=64)
 
-        def make_y(i):
+        def make_y(i, shares):
             c, t = divmod(i, PACK)
-            acc = psum.tile([P, M], F32, name="acc", bufs=3)
+            accs = [next_bank([P, m1 - m0]) for copy, m0, m1 in shares]
             for b in range(J_PASSES):
-                nc.tensor.matmul_mx(
-                    out=acc[:],
-                    lhsT=wd_words[i][:, b * P : (b + 1) * P].bitcast(FP8X4),
-                    lhsT_scale=wd_planes[i][:, b * P : (b + 1) * P],
-                    rhs=h_words[b][:].bitcast(FP8X4),
-                    rhs_scale=h_planes[b][:],
-                    start=(b == 0),
-                    stop=(b == J_PASSES - 1),
-                )
-            nc.scalar.copy(y_sb[c][:, t, :], acc[:])
+                words, planes = wd_codes[i, b]
+                for acc, (copy, m0, m1) in zip(accs, shares):
+                    nc.tensor.matmul_mx(
+                        out=acc[:],
+                        lhsT=words.bitcast(FP8X4),
+                        lhsT_scale=planes,
+                        rhs=h_words[b][:, m0:m1].bitcast(FP8X4),
+                        rhs_scale=h_planes[b][:, m0:m1],
+                        start=(b == 0),
+                        stop=(b == J_PASSES - 1),
+                    )
+            for acc, (copy, m0, m1) in zip(accs, shares):
+                copy(y_sb[c][:, t, m0:m1], acc[:])
             nc.sync.dma_start(out=y_rows[c, :, t, :], in_=y_sb[c][:, t, :])
 
-        def make_y_planes(c, copy):
-            y_grouped = keep.tile([P, M, PACK], BF16, name="y_grouped%d" % c, align_bytes=64)
-            copy(
-                y_grouped[:].rearrange("p (c i) t -> p c t i", i=4),
-                y_sb[c][:].rearrange("p t (c i) -> p c t i", i=4),
-            )
-            y_words = keep.tile([P, M], I32, name="y_words%d" % c, align_bytes=64)
-            nc.vector.quantize_mx(
-                out=y_words[:].bitcast(FP8X4),
-                scales=y_planes[:, c, :],
-                in_=y_grouped[:].rearrange("p m t -> p (m t)"),
-            )
-            nc.sync.dma_start(out=out_1[c].rearrange("p m t -> p (m t)").bitcast(I32), in_=y_words[:])
+        def make_y_planes(c, shares, hold):
+            for part, (copy, m0, m1) in enumerate(shares):
+                y_grouped = keep.tile([P, m1 - m0, PACK], BF16, name="y_grouped%d_%d" % (c, part), align_bytes=64)
+                copy(
+                    y_grouped[:].rearrange("p (c i) t -> p c t i", i=4),
+                    y_sb[c][:, :, m0:m1].rearrange("p t (c i) -> p c t i", i=4),
+                )
+                y_words = over_window(hold, 4096 + 2048, [P, m1 - m0], I32, "y_words%d_%d" % (c, part))
+                nc.vector.quantize_mx(
+                    out=y_words[:].bitcast(FP8X4),
+                    scales=y_planes[:, c, m0:m1],
+                    in_=y_grouped[:].rearrange("p m t -> p (m t)"),
+                )
+                (nc.scalar if part else nc.sync).dma_start(
+                    out=out_1[c, :, m0:m1, :].rearrange("p m t -> p (m t)").bitcast(I32), in_=y_words[:]
+                )
 
-        make_wd(0)
+        halves = [(nc.vector.tensor_copy, 0, M // 2), (nc.scalar.copy, M // 2, M)]
+
+        def make_ys(k):
+            first, n = UNITS[k]
+            for i in range(first, first + n):
+                make_y(i, halves if i == N_GROUPS * PACK - 1 else [(nc.scalar.copy, 0, M)])
+            if first + n == PACK:
+                make_y_planes(0, [(nc.scalar.copy, 0, M)], 6)
+
         make_h(0)
-        make_wd(1)
         make_h(1)
-        for i in range(2, N_GROUPS * PACK):
-            make_wd(i)
-            make_y(i - 2)
-            if i - 2 == PACK - 1:
-                make_y_planes(0, nc.scalar.copy)
-        make_y(N_GROUPS * PACK - 2)
-        make_y(N_GROUPS * PACK - 1)
-        make_y_planes(1, nc.vector.tensor_copy)
+        make_wd(0)
+        for k in range(1, len(UNITS)):
+            make_wd(k)
+            make_ys(k - 1)
+        make_ys(len(UNITS) - 1)
+        make_y_planes(1, halves, None)
         for q in range(QUADS):
             queue = nc.scalar if q % 2 else nc.sync
             queue.dma_start(

@@ -26,9 +26,9 @@ QUADS = 4
 MOVED_ROWS = 112
 BIG = 3.0e38
 WINDOW_BYTES = 4 * T
-UNITS = [(i, 1) for i in range(8)]
-LOADS = [("tab", 0, 0), ("tab", 1, 0), ("tab_planes", 0, 0), ("tab", 2, 0), ("x_planes", 0, 0), ("x", 0, 0), ("wd", 0, 0), ("vec", 0, 0), ("vec", 1, 0), ("vec", 2, 0), ("prev", 0, 0)]
-LATER_LOADS = [("prev", 1, 0), ("wd", 1, 0), ("wd", 2, 0), ("wd", 3, 0), ("wd", 4, 0), ("wd", 5, 0), ("wd", 6, 0), ("wd", 7, 0)]
+UNITS = [(0, 2)] + [(i, 1) for i in range(2, 8)]
+LOADS = [("tab", 0, 0), ("tab", 1, 0), ("tab_planes", 0, 0), ("pair", 0, 0), ("x_planes", 0, 0), ("pair", 0, 1), ("vec", 0, 0), ("vec", 1, 0), ("vec", 2, 0), ("tab", 2, 0), ("x", 0, 0), ("prev", 0, 0)]
+LATER_LOADS = [("prev", 1, 0), ("wd", 1, 0), ("wd", 2, 0), ("wd", 3, 0), ("wd", 4, 0), ("wd", 5, 0), ("wd", 6, 0)]
 
 
 def tile_list_leaky_event_layer_kernel(
@@ -300,7 +300,7 @@ def tile_list_leaky_event_layer_kernel(
             for i in range(first, first + n):
                 make_y(i, halves if i == N_GROUPS * PACK - 1 else [(nc.scalar.copy, 0, M)])
             if first + n == PACK:
-                make_y_planes(0, [(nc.scalar.copy, 0, M)], 6)
+                make_y_planes(0, [(nc.scalar.copy, 0, M)], 5)
 
         make_h(0)
         make_h(1)

@@ -27,7 +27,7 @@ MOVED_ROWS = 112
 BIG = 3.0e38
 WINDOW_BYTES = 4 * T
 UNITS = [(0, 2)] + [(i, 1) for i in range(2, 8)]
-LOADS = [("tab", 0, 0), ("tab", 1, 0), ("tab_planes", 0, 0), ("pair", 0, 0), ("x_planes", 0, 0), ("pair", 0, 1), ("vec", 0, 0), ("vec", 1, 0), ("vec", 2, 0), ("tab", 2, 0), ("x", 0, 0), ("prev", 0, 0)]
+LOADS = [("tab", 0, 0), ("tab", 1, 0), ("tab_planes", 0, 0), ("pair", 0, 0), ("tab", 2, 0), ("x_planes", 0, 0), ("x", 0, 0), ("pair", 0, 1), ("vec", 0, 0), ("vec", 1, 0), ("vec", 2, 0), ("prev", 0, 0)]
 LATER_LOADS = [("prev", 1, 0), ("wd", 1, 0), ("wd", 2, 0), ("wd", 3, 0), ("wd", 4, 0), ("wd", 5, 0), ("wd", 6, 0)]
 
 
@@ -125,12 +125,14 @@ def tile_list_leaky_event_layer_kernel(
         nc.gpsimd.tensor_scalar(lower[:], gain_sb[:], 0.0, -BIG, ALU.is_lt, ALU.mult)
 
         picked_planes = keep.tile([P, S], U8, name="picked_planes", align_bytes=64)
-        v_words = [keep.tile([P, S], U32, name="v_words%d" % a, align_bytes=64) for a in range(K_PASSES - 1)]
+        v_words = [keep.tile([P, S], U32, name="v_words%d" % a, align_bytes=64) for a in range(K_PASSES)]
 
         def pick_words(a):
+            listed = ring.tile([P, S], U32, name="listed_words", bufs=2)
+            nc.vector.tensor_copy(listed[:], tab_sb[a][:].bitcast(U32).indirect(offsets[:]))
             nc.vector.tensor_copy(
-                v_words[a][:].rearrange("p (t s) -> p s t", t=PACK),
-                tab_sb[a][:].bitcast(U32).indirect(offsets[:]),
+                v_words[a][:].bitcast(I32).rearrange("p (t c i) -> p c t i", t=PACK, i=4),
+                listed[:].bitcast(I32).rearrange("p (c i t) -> p c t i", t=PACK, i=4),
             )
 
         pick_words(0)
@@ -147,12 +149,7 @@ def tile_list_leaky_event_layer_kernel(
         for item in LATER_LOADS:
             load(*item)
         pick_words(1)
-        last_words = [keep.tile([P, S // J_PASSES], U32, name="last_words%d" % b, align_bytes=64) for b in range(J_PASSES)]
-        for b in range(J_PASSES):
-            nc.vector.tensor_copy(
-                last_words[b][:].rearrange("p (t s) -> p s t", t=PACK),
-                tab_sb[K_PASSES - 1][:].bitcast(U32).indirect(offsets[:, 32 * b : 32 * (b + 1)]),
-            )
+        pick_words(2)
 
         h_words = [over_window((1, 2)[b], 4096, [P, M], U32, "h_words%d" % b) for b in range(J_PASSES)]
         h_planes = [keep.tile([P, M], U8, name="h_planes%d" % b, align_bytes=64) for b in range(J_PASSES)]
@@ -179,7 +176,7 @@ def tile_list_leaky_event_layer_kernel(
                 for a in range(K_PASSES):
                     nc.tensor.matmul_mx(
                         out=current[:],
-                        lhsT=(v_words[a][:, cols] if a < K_PASSES - 1 else last_words[b][:, t * P : (t + 1) * P]).bitcast(FP8X4),
+                        lhsT=v_words[a][:, cols].bitcast(FP8X4),
                         lhsT_scale=v_planes[a][:, cols],
                         rhs=x_sb[:, a, :].bitcast(FP4X4),
                         rhs_scale=x_planes[:, a, :],
@@ -209,15 +206,12 @@ def tile_list_leaky_event_layer_kernel(
                 words = over_window(k + 1, 0, [P, 2 * J_PASSES * P], U32, "wd_words%d" % k)
                 planes = keep.tile([P, 2 * J_PASSES * P], U8, name="wd_planes%d" % k, align_bytes=64)
                 picked = keep.tile([P, S], U32, name="picked_pairs%d" % k)
-                nc.vector.tensor_copy(
-                    picked[:].rearrange("p (t s) -> p s t", t=PACK), windows[k][:].indirect(offsets[:])
-                )
+                nc.vector.tensor_copy(picked[:], windows[k][:].indirect(offsets[:]))
                 grouped = keep.tile([P, 2, J_PASSES, P, PACK], BF16, name="pair_grouped%d" % k, align_bytes=64)
                 for b in range(J_PASSES):
                     turned = next_bank([P, PACK, P])
                     for t in range(PACK):
-                        at = t * J_PASSES * P + b * P
-                        nc.tensor.transpose(turned[:, t, :], picked[:, at : at + P].bitcast(F32), identity[:])
+                        nc.tensor.transpose(turned[:, t, :], picked[:].bitcast(F32)[:, b * PACK * P + t : (b + 1) * PACK * P : PACK], identity[:])
                     nc.scalar.copy(
                         grouped[:, :, b, :, :],
                         turned[:].bitcast(BF16).rearrange("p t (c e) -> p e c t", e=2),

@@ -19,16 +19,19 @@ ACT = mybir.ActivationFunctionType
 
 P = 128
 PACK = 4
-K_PASSES = K // (P * PACK)
-J_PASSES = S // (P * PACK)
-N_GROUPS = N // (P * PACK)
+PASS = P * PACK
+K_PASSES = K // PASS
+J_PASSES = S // PASS
+N_GROUPS = N // PASS
+N_SLICES = N_GROUPS * PACK
+M_CHUNKS = M // P
 QUADS = 4
+BANKS = 8
 MOVED_ROWS = 112
 BIG = 3.0e38
 WINDOW_BYTES = 4 * T
-UNITS = [(0, 2)] + [(i, 1) for i in range(2, 8)]
-LOADS = [("tab", 0, 0), ("tab", 1, 0), ("tab_planes", 0, 0), ("pair", 0, 0), ("tab", 2, 0), ("x_planes", 0, 0), ("x", 0, 0), ("pair", 0, 1), ("vec", 0, 0), ("vec", 1, 0), ("vec", 2, 0), ("prev", 0, 0)]
-LATER_LOADS = [("prev", 1, 0), ("wd", 1, 0), ("wd", 2, 0), ("wd", 3, 0), ("wd", 4, 0), ("wd", 5, 0), ("wd", 6, 0)]
+PICKED_AT = 2048
+UNITS = [(i,) for i in range(N_SLICES)]
 
 
 def tile_list_leaky_event_layer_kernel(
@@ -41,228 +44,283 @@ def tile_list_leaky_event_layer_kernel(
         ring = ctx.enter_context(tc.tile_pool(name="ring", bufs=3))
         psum = ctx.enter_context(tc.psum_pool(name="psum", bufs=1))
 
-        def over_window(k, at, shape, dtype, name):
-            if k is None:
-                return keep.tile(shape, dtype, name=name, align_bytes=64)
-            return placed.tile(shape, dtype, name=name, align_bytes=64, offset=k * WINDOW_BYTES + at)
+        def on_window(w, at, shape, dtype, name):
+            return placed.tile(shape, dtype, name=name, align_bytes=64, offset=w * WINDOW_BYTES + at)
 
-        bank_turn = [n % 8 for n in range(64)]
+        def below_pick(k, columns, dtype, name):
+            return on_window(k, PICKED_AT + 64 - 4 * columns, [P, columns], dtype, name)
 
-        def next_bank(shape):
-            return psum.tile(shape, F32, name="bank%d" % bank_turn.pop(0))
+        def above_pick(k, columns, dtype, name):
+            return on_window(k, PICKED_AT + 2 * PASS - 64, [P, columns], dtype, name)
+
+        def bank(n, shape):
+            return psum.tile(shape, F32, name="bank%d" % n)
 
         offsets = keep.tile([P, S // 16], U16, name="offsets")
         nc.sync.dma_start(offsets[:], offs)
 
         tab_planes = keep.tile([P, T], U8, name="tab_planes", align_bytes=64)
         nc.vector.memset(tab_planes[:].bitcast(I32), 0)
+        for q in range(QUADS):
+            nc.scalar.dma_start(
+                out=tab_planes[32 * q : 32 * q + 4 * K_PASSES, :].bitcast(I32),
+                in_=tab_scales[:, 4 * q : 4 * q + 4, :].bitcast(I32),
+            )
+        x_planes = keep.tile([P, K_PASSES, M], U8, name="x_planes", align_bytes=64)
+        for q in range(QUADS):
+            nc.scalar.dma_start(
+                out=x_planes[32 * q : 32 * q + 4, :, :].bitcast(I32),
+                in_=x_scales[:, 4 * q : 4 * q + 4, :].rearrange("a r m -> r a m").bitcast(I32),
+            )
+        vec_rows = keep.tile([P, PASS], F32, name="vec_rows")
+        nc.vector.memset(vec_rows[:], 0.0)
+        for v, vec in enumerate((g, leak, thr)):
+            nc.scalar.dma_start(out=vec_rows[J_PASSES * v : J_PASSES * (v + 1), :], in_=vec.rearrange("(b j) -> b j", b=J_PASSES))
         identity = keep.tile([P, P], F32, name="identity")
         make_identity(nc, identity[:])
-
-        x_planes = keep.tile([P, K_PASSES, M], U8, name="x_planes", align_bytes=64)
-        v_planes = [keep.tile([P, S], U8, name="v_planes%d" % a, align_bytes=64) for a in range(K_PASSES)]
-
-        leak_sb = keep.tile([P, J_PASSES * PACK], F32, name="leak_sb")
-        thr_sb = keep.tile([P, J_PASSES * PACK], F32, name="thr_sb")
-        gain_sb = keep.tile([P, J_PASSES * PACK], F32, name="gain_sb")
-        tab_sb = [keep.tile([P, T], I32, name="tab_sb%d" % a) for a in range(K_PASSES)]
-        x_sb = keep.tile([P, K_PASSES, 2 * M], U8, name="x_sb", align_bytes=64)
-        prev_sb = [over_window((None, len(UNITS))[b], 0, [P, PACK, M], F32, "prev_sb%d" % b) for b in range(J_PASSES)]
-        prev_rows = prev.rearrange("(b p t) m -> b p t m", b=J_PASSES, t=PACK)
-        wd_rows = wdT.rearrange("(c p t) j -> c p t j", c=N_GROUPS, t=PACK)
-        windows = [over_window(k, 0, [P, T], F32 if n == 1 else U32, "window%d" % k) for k, (i, n) in enumerate(UNITS)]
-
-        def load(kind, k, half):
-            if kind == "tab_planes":
-                for q in range(QUADS):
-                    nc.sync.dma_start(
-                        out=tab_planes[32 * q : 32 * q + 4 * K_PASSES, :].bitcast(I32),
-                        in_=tab_scales[:, 4 * q : 4 * q + 4, :].bitcast(I32),
-                    )
-            elif kind == "tab":
-                nc.sync.dma_start(out=tab_sb[k][:], in_=tab_words[k].rearrange("p n t -> p (n t)").bitcast(I32))
-            elif kind == "x":
-                nc.sync.dma_start(out=x_sb[:].bitcast(I32), in_=x_words.rearrange("a p n -> p a n").bitcast(I32))
-            elif kind == "x_planes":
-                for q in range(QUADS):
-                    nc.sync.dma_start(
-                        out=x_planes[32 * q : 32 * q + 4, :, :].bitcast(I32),
-                        in_=x_scales[:, 4 * q : 4 * q + 4, :].rearrange("a r m -> r a m").bitcast(I32),
-                    )
-            elif kind == "vec":
-                vec_sb, vec = ((gain_sb, g), (leak_sb, leak), (thr_sb, thr))[k]
-                nc.sync.dma_start(
-                    out=vec_sb[:].rearrange("p (b t) -> p b t", t=PACK),
-                    in_=vec.rearrange("(b p t) -> p b t", b=J_PASSES, t=PACK),
-                )
-            elif kind == "prev":
-                nc.sync.dma_start(out=prev_sb[k][:], in_=prev_rows[k])
-            elif kind == "wd":
-                c, t = divmod(UNITS[k][0], PACK)
-                nc.sync.dma_start(out=windows[k][:], in_=wd_rows[c, :, t, :])
-            else:
-                c, t = divmod(UNITS[k][0], PACK)
-                cols = slice(half * T // 2, (half + 1) * T // 2)
-                two_rows = ring.tile([P, 2, T // 2], F32, name="two_rows", bufs=2)
-                nc.sync.dma_start(out=two_rows[:], in_=wd_rows[c, :, t : t + 2, cols])
-                nc.scalar.copy(
-                    windows[k][:, cols].bitcast(BF16).rearrange("p (j e) -> p j e", e=2),
-                    two_rows[:].rearrange("p e j -> p j e"),
-                )
-
-        for item in LOADS:
-            load(*item)
-
+        vec_turned = bank(BANKS - 1, [P, PACK, P])
+        for t in range(PACK):
+            nc.tensor.transpose(vec_turned[:, t, :], vec_rows[:, t::PACK], identity[:])
+        vecs = keep.tile([P, 3 * J_PASSES, PACK], F32, name="vecs")
+        nc.scalar.copy(vecs[:], vec_turned[:, :, 0 : 3 * J_PASSES].rearrange("p t r -> p r t"))
+        gain, leaks, thresholds = [
+            vecs[:, J_PASSES * v : J_PASSES * (v + 1), :].rearrange("p b t -> p (b t)") for v in range(3)
+        ]
         gain_leak = keep.tile([P, J_PASSES * PACK], F32, name="gain_leak")
         gain_thr = keep.tile([P, J_PASSES * PACK], F32, name="gain_thr")
         minus_gain_thr = keep.tile([P, J_PASSES * PACK], F32, name="minus_gain_thr")
         upper = keep.tile([P, J_PASSES * PACK], F32, name="upper")
         lower = keep.tile([P, J_PASSES * PACK], F32, name="lower")
-        nc.gpsimd.tensor_tensor(gain_leak[:], gain_sb[:], leak_sb[:], ALU.mult)
-        nc.gpsimd.tensor_tensor(gain_thr[:], gain_sb[:], thr_sb[:], ALU.mult)
+        nc.gpsimd.tensor_tensor(gain_leak[:], gain, leaks, ALU.mult)
+        nc.gpsimd.tensor_tensor(gain_thr[:], gain, thresholds, ALU.mult)
         nc.gpsimd.tensor_scalar(minus_gain_thr[:], gain_thr[:], -1.0, 0.0, ALU.mult, ALU.add)
-        nc.gpsimd.tensor_scalar(upper[:], gain_sb[:], 0.0, BIG, ALU.is_ge, ALU.mult)
-        nc.gpsimd.tensor_scalar(lower[:], gain_sb[:], 0.0, -BIG, ALU.is_lt, ALU.mult)
+        nc.gpsimd.tensor_scalar(upper[:], gain, 0.0, BIG, ALU.is_ge, ALU.mult)
+        nc.gpsimd.tensor_scalar(lower[:], gain, 0.0, -BIG, ALU.is_lt, ALU.mult)
 
-        picked_planes = keep.tile([P, S], U8, name="picked_planes", align_bytes=64)
-        v_words = [keep.tile([P, S], U32, name="v_words%d" % a, align_bytes=64) for a in range(K_PASSES)]
+        tab_sb = [on_window(a, 0, [P, T], I32, "tab_sb%d" % a) for a in range(K_PASSES)]
+        windows = [
+            on_window(K_PASSES + k, 0, [P, T], F32 if len(unit) == 1 else U32, "window%d" % k) for k, unit in enumerate(UNITS)
+        ]
+        x_sb = keep.tile([P, K_PASSES, 2 * M], U8, name="x_sb", align_bytes=64)
+        spare = K_PASSES + len(UNITS)
+        prev_sb = [
+            [keep.tile([P, 2, M], F32, name="prev_sb0_0"), keep.tile([P, 2, M], F32, name="prev_sb0_1")],
+            [keep.tile([P, 2, M], F32, name="prev_sb1_0"), on_window(spare, 4096 - 64, [P, 2, M], F32, "prev_sb1_1")],
+        ]
+        prev_rows = prev.rearrange("(b p t) m -> b p t m", b=J_PASSES, t=PACK)
+        wd_rows = wdT.rearrange("(c p t) j -> c p t j", c=N_GROUPS, t=PACK)
 
-        def pick_words(a):
-            listed = ring.tile([P, S], U32, name="listed_words", bufs=2)
-            nc.vector.tensor_copy(listed[:], tab_sb[a][:].bitcast(U32).indirect(offsets[:]))
-            nc.vector.tensor_copy(
-                v_words[a][:].bitcast(I32).rearrange("p (t c i) -> p c t i", t=PACK, i=4),
-                listed[:].bitcast(I32).rearrange("p (c i t) -> p c t i", t=PACK, i=4),
+        def load_tab(a):
+            nc.sync.dma_start(out=tab_sb[a][:], in_=tab_words[a].rearrange("p n t -> p (n t)").bitcast(I32))
+
+        def load_x():
+            nc.sync.dma_start(out=x_sb[:].bitcast(I32), in_=x_words.rearrange("a p n -> p a n").bitcast(I32))
+
+        def load_prev(b):
+            for u in range(2):
+                nc.sync.dma_start(out=prev_sb[b][u][:], in_=prev_rows[b, :, 2 * u : 2 * u + 2, :])
+
+        def load_wd(k):
+            c, t = divmod(UNITS[k][0], PACK)
+            nc.sync.dma_start(out=windows[k][:], in_=wd_rows[c, :, t, :])
+
+        def load_pair(k, part):
+            c, t = divmod(UNITS[k][0], PACK)
+            cols = slice(part * T // 2, (part + 1) * T // 2)
+            two_rows = ring.tile([P, 2, T // 2], F32, name="two_rows", bufs=2)
+            nc.sync.dma_start(out=two_rows[:], in_=wd_rows[c, :, t : t + 2, cols])
+            nc.scalar.copy(
+                windows[k][:, cols].bitcast(BF16).rearrange("p (j e) -> p j e", e=2),
+                two_rows[:].rearrange("p e j -> p j e"),
             )
 
-        pick_words(0)
-        nc.vector.tensor_copy(picked_planes[:], tab_planes[:].indirect(offsets[:]))
-        nc.vector.tensor_copy(
-            v_planes[0][:].rearrange("p (t s) -> p t s", t=PACK),
-            picked_planes[:].rearrange("p (s t) -> p t s", t=PACK),
-        )
+        def list_half(b):
+            return offsets[:, b * PASS // 16 : (b + 1) * PASS // 16]
+
+        v_words = [keep.tile([P, S], U32, name="v_words%d" % a, align_bytes=64) for a in range(K_PASSES)]
+        v_planes = [keep.tile([P, S], U8, name="v_planes%d" % a, align_bytes=64) for a in range(K_PASSES)]
+        load_tab(0)
+        load_tab(1)
+        load_x()
+        load_tab(2)
+        load_wd(0)
+
+        nc.vector.tensor_copy(v_words[0][:], tab_sb[0][:].bitcast(U32).indirect(offsets[:]))
+        nc.vector.tensor_copy(v_planes[0][:], tab_planes[:].indirect(offsets[:]))
         for a in range(1, K_PASSES):
             nc.sync.dma_start(
                 out=v_planes[a][0:MOVED_ROWS, :].bitcast(I32),
                 in_=v_planes[0][4 * a : 4 * a + MOVED_ROWS, :].bitcast(I32),
             )
-        for item in LATER_LOADS:
-            load(*item)
-        pick_words(1)
-        pick_words(2)
+        load_wd(1)
+        load_prev(0)
+        load_prev(1)
+        for k in range(2, len(UNITS)):
+            load_wd(k)
 
-        h_words = [over_window((1, 2)[b], 4096, [P, M], U32, "h_words%d" % b) for b in range(J_PASSES)]
-        h_planes = [keep.tile([P, M], U8, name="h_planes%d" % b, align_bytes=64) for b in range(J_PASSES)]
-
-        rests = [[keep.tile([P, M], F32, name="rest%d_%d" % (b, t)) for t in range(PACK)] for b in range(J_PASSES)]
+        nc.vector.tensor_copy(v_words[1][:], tab_sb[1][:].bitcast(U32).indirect(offsets[:]))
         for b in range(J_PASSES):
-            for t in range(PACK):
-                bt = slice(b * PACK + t, b * PACK + t + 1)
-                nc.scalar.activation(rests[b][t][:], prev_sb[b][:, t, :], ACT.Identity, bias=minus_gain_thr[:, bt], scale=gain_leak[:, bt])
+            nc.vector.tensor_copy(v_words[2][:, b * PASS : (b + 1) * PASS], tab_sb[2][:].bitcast(U32).indirect(list_half(b)))
 
-        def make_h(b):
-            h_rows = keep.tile([P, PACK, M], BF16, name="h_rows%d" % b)
-            rest = rests[b]
-            for t in range(0):
-                bt = slice(b * PACK + t, b * PACK + t + 1)
-                if ("scalar", "scalar")[b] == "scalar":
-                    nc.scalar.activation(rest[t][:], prev_sb[b][:, t, :], ACT.Identity, bias=minus_gain_thr[:, bt], scale=gain_leak[:, bt])
-                else:
-                    nc.gpsimd.tensor_scalar(rest[t][:], prev_sb[b][:, t, :], gain_leak[:, bt], minus_gain_thr[:, bt], ALU.mult, ALU.add)
-            for t in range(PACK):
-                bt = slice(b * PACK + t, b * PACK + t + 1)
-                cols = slice(t * J_PASSES * P + b * P, t * J_PASSES * P + (b + 1) * P)
-                current = next_bank([P, M])
-                for a in range(K_PASSES):
+        sums = [[bank(b * M_CHUNKS + mc, [P, PASS]) for mc in range(M_CHUNKS)] for b in range(J_PASSES)]
+        for b, passes in [(b, [0]) for b in range(J_PASSES)] + [(b, range(1, K_PASSES)) for b in range(J_PASSES)]:
+            for a in passes:
+                for mc in range(M_CHUNKS):
                     nc.tensor.matmul_mx(
-                        out=current[:],
-                        lhsT=v_words[a][:, cols].bitcast(FP8X4),
-                        lhsT_scale=v_planes[a][:, cols],
-                        rhs=x_sb[:, a, :].bitcast(FP4X4),
-                        rhs_scale=x_planes[:, a, :],
+                        out=sums[b][mc][:],
+                        lhsT=x_sb[:, a, 2 * mc * P : 2 * (mc + 1) * P].bitcast(FP4X4),
+                        lhsT_scale=x_planes[:, a, mc * P : (mc + 1) * P],
+                        rhs=v_words[a][:, b * PASS : (b + 1) * PASS].bitcast(FP8X4),
+                        rhs_scale=v_planes[a][:, b * PASS : (b + 1) * PASS],
                         start=(a == 0),
                         stop=(a == K_PASSES - 1),
                     )
-                scaled = ring.tile([P, M], F32, name="scaled", bufs=4)
-                nc.vector.scalar_tensor_tensor(scaled[:], current[:], gain_sb[:, bt], rest[t][:], ALU.mult, ALU.add)
-                nc.gpsimd.tensor_scalar(h_rows[:, t, :], scaled[:], upper[:, bt], lower[:, bt], ALU.min, ALU.max)
-            h_grouped = over_window((len(UNITS), None)[b], 0, [P, M, PACK], BF16, "h_grouped%d" % b)
+        currents = []
+        for b in range(J_PASSES):
+            dealt = [keep.tile([P, PACK, P], F32, name="dealt%d_%d" % (b, mc)) for mc in range(M_CHUNKS)]
+            for mc in range(M_CHUNKS):
+                nc.scalar.copy(dealt[mc][:], sums[b][mc][:].rearrange("m (p t) -> m t p", t=PACK))
+            turned = [bank(b * PACK + t, [P, M]) for t in range(PACK)]
+            for t in range(PACK):
+                for mc in range(M_CHUNKS):
+                    nc.tensor.transpose(turned[t][:, mc * P : (mc + 1) * P], dealt[mc][:, t, :], identity[:])
+            currents.append(turned)
+
+        banks = [n % BANKS for n in range(4 * N_SLICES)]
+        h_grouped = [on_window(spare, 0, [P, M, PACK], BF16, "h_grouped0"), keep.tile([P, M, PACK], BF16, name="h_grouped1", align_bytes=64)]
+        h_codes = {}
+
+        rests = {}
+
+        def make_rests(b):
+            for t in range(PACK):
+                bt = slice(b * PACK + t, b * PACK + t + 1)
+                if (b, t) == (J_PASSES - 1, PACK - 1):
+                    rest = on_window(2, PICKED_AT, [P, M], F32, "last_rest")
+                else:
+                    rest = keep.tile([P, M], F32, name="rest%d_%d" % (b, t))
+                if b == 0:
+                    nc.gpsimd.tensor_scalar(rest[:], prev_sb[b][t // 2][:, t % 2, :], gain_leak[:, bt], minus_gain_thr[:, bt], ALU.mult, ALU.add)
+                else:
+                    nc.scalar.activation(rest[:], prev_sb[b][t // 2][:, t % 2, :], ACT.Identity, bias=minus_gain_thr[:, bt], scale=gain_leak[:, bt])
+                rests[b, t] = rest
+
+        def make_h(b):
+            if b == 0:
+                rounded = on_window(K_PASSES + 1, WINDOW_BYTES // 2, [P, PACK, M], BF16, "rounded0")
+            else:
+                rounded = keep.tile([P, PACK, M], BF16, name="rounded1")
+            h_rows = keep.tile([P, PACK, M], BF16, name="h_rows%d" % b)
+            for t in range(PACK):
+                bt = slice(b * PACK + t, b * PACK + t + 1)
+                nc.vector.scalar_tensor_tensor(rounded[:, t, :], currents[b][t][:], gain[:, bt], rests[b, t][:], ALU.mult, ALU.add)
+            for t in range(PACK):
+                bt = slice(b * PACK + t, b * PACK + t + 1)
+                nc.vector.tensor_scalar(h_rows[:, t, :], rounded[:, t, :], upper[:, bt], lower[:, bt], ALU.min, ALU.max)
             nc.scalar.copy(
-                h_grouped[:].rearrange("p (c i) t -> p c t i", i=4),
+                h_grouped[b][:].rearrange("p (c i) t -> p c t i", i=4),
                 h_rows[:].rearrange("p t (c i) -> p c t i", i=4),
             )
-            nc.vector.quantize_mx(
-                out=h_words[b][:].bitcast(FP8X4),
-                scales=h_planes[b][:],
-                in_=h_grouped[:].rearrange("p m t -> p (m t)"),
-            )
 
+        def quantise_h(b, k):
+            words = above_pick(k, M, U32, "h_words%d" % b)
+            planes = keep.tile([P, M], U8, name="h_planes%d" % b, align_bytes=64)
+            nc.vector.quantize_mx(out=words[:].bitcast(FP8X4), scales=planes[:], in_=h_grouped[b][:].rearrange("p m t -> p (m t)"))
+            h_codes[b] = (words, planes)
+
+        picks = {}
         wd_codes = {}
 
-        def make_wd(k):
-            first, n = UNITS[k]
-            last = k == len(UNITS) - 1
-            if n == 2:
-                words = over_window(k + 1, 0, [P, 2 * J_PASSES * P], U32, "wd_words%d" % k)
-                planes = keep.tile([P, 2 * J_PASSES * P], U8, name="wd_planes%d" % k, align_bytes=64)
-                picked = keep.tile([P, S], U32, name="picked_pairs%d" % k)
-                nc.vector.tensor_copy(picked[:], windows[k][:].indirect(offsets[:]))
-                grouped = keep.tile([P, 2, J_PASSES, P, PACK], BF16, name="pair_grouped%d" % k, align_bytes=64)
+        def pick(k):
+            dtype = BF16 if len(UNITS[k]) == 1 else U32
+            picks[k] = [
+                on_window(k, PICKED_AT, [P, PASS], dtype, "picked%d" % k),
+                on_window(k, PICKED_AT + 2 * PASS, [P, PASS], dtype, "picked_last")
+                if k == len(UNITS) - 1
+                else ring.tile([P, PASS], dtype, name="picked"),
+            ]
+            for b in range(J_PASSES):
+                nc.vector.tensor_copy(picks[k][b][:], windows[k][:].indirect(list_half(b)))
+
+        def turn_single(k, halves, grouped):
+            turned = bank(banks.pop(0), [P, len(halves), 2, P])
+            for n, b in enumerate(halves):
+                for u in range(2):
+                    nc.tensor.transpose(turned[:, n, u, :], picks[k][b][:].bitcast(F32)[:, u::2], identity[:])
+            nc.scalar.copy(
+                grouped.bitcast(F32).rearrange("p (b c u) -> p b c u", b=len(halves), u=2),
+                turned[:].rearrange("p b u c -> p b c u"),
+            )
+
+        def turn_pair(k, grouped):
+            by_row = grouped.rearrange("p (e b c t) -> p e b c t", e=2, b=J_PASSES, t=PACK)
+            for b in range(J_PASSES):
+                turned = bank(banks.pop(0), [P, PACK, P])
+                for t in range(PACK):
+                    nc.tensor.transpose(turned[:, t, :], picks[k][b][:].bitcast(F32)[:, t::PACK], identity[:])
+                nc.scalar.copy(by_row[:, :, b, :, :], turned[:].bitcast(BF16).rearrange("p t (c e) -> p e c t", e=2))
+
+        turned_values = {}
+
+        def turn(ks):
+            slices = [i for k in ks for i in UNITS[k]]
+            if ks[0] == 0:
+                grouped = on_window(spare, 8192 - 128, [P, len(slices) * S], BF16, "wd_grouped0")
+            elif ks[0] == len(UNITS) - 2:
+                grouped = on_window(len(UNITS) - 1, PICKED_AT, [P, len(slices) * S], BF16, "wd_grouped_late")
+            else:
+                grouped = ring.tile([P, len(slices) * S], BF16, name="wd_grouped", align_bytes=64, bufs=2)
+            at = 0
+            for k in ks:
+                width = len(UNITS[k]) * S
+                if len(UNITS[k]) == 1:
+                    turn_single(k, range(J_PASSES), grouped[:, at : at + width])
+                else:
+                    turn_pair(k, grouped[:, at : at + width])
+                at = at + width
+            turned_values[ks[-1]] = (slices, grouped)
+
+        def quantise_wd(k, behind):
+            slices, grouped = turned_values[k]
+            columns = len(slices) * J_PASSES * P
+            if behind is None:
+                words = keep.tile([P, columns], U32, name="wd_words%d" % k, align_bytes=64)
+            else:
+                words = below_pick(behind, columns, U32, "wd_words%d" % k)
+            planes = keep.tile([P, columns], U8, name="wd_planes%d" % k, align_bytes=64)
+            nc.vector.quantize_mx(out=words[:].bitcast(FP8X4), scales=planes[:], in_=grouped[:])
+            for n, i in enumerate(slices):
                 for b in range(J_PASSES):
-                    turned = next_bank([P, PACK, P])
-                    for t in range(PACK):
-                        nc.tensor.transpose(turned[:, t, :], picked[:].bitcast(F32)[:, b * PACK * P + t : (b + 1) * PACK * P : PACK], identity[:])
-                    nc.scalar.copy(
-                        grouped[:, :, b, :, :],
-                        turned[:].bitcast(BF16).rearrange("p t (c e) -> p e c t", e=2),
-                    )
-                nc.vector.quantize_mx(
-                    out=words[:].bitcast(FP8X4), scales=planes[:], in_=grouped[:].rearrange("p e b c t -> p (e b c t)")
-                )
-                for e in range(2):
-                    for b in range(J_PASSES):
-                        at = (e * J_PASSES + b) * P
-                        wd_codes[first + e, b] = (words[:, at : at + P], planes[:, at : at + P])
-                return
-            parts = [[b] for b in range(J_PASSES)] if last else [list(range(J_PASSES))]
-            for part in parts:
-                nb = len(part)
-                name = "%d_%d" % (k, part[0])
-                words = over_window(None if last else k + 1, 0, [P, nb * P], U32, "wd_words" + name)
-                planes = keep.tile([P, nb * P], U8, name="wd_planes" + name, align_bytes=64)
-                picked = ring.tile([P, nb * P * PACK], BF16, name="picked")
-                lists = offsets[:, part[0] * 32 : (part[0] + nb) * 32]
-                nc.vector.tensor_copy(picked[:], windows[k][:].indirect(lists))
-                pairs = picked[:].bitcast(F32)
-                turned = next_bank([P, nb, 2, P])
-                for b in range(nb):
-                    for u in range(2):
-                        nc.tensor.transpose(turned[:, b, u, :], pairs[:, 2 * P * b + u : 2 * P * (b + 1) : 2], identity[:])
-                grouped = ring.tile([P, nb * P * PACK], BF16, name="wd_grouped", align_bytes=64)
-                nc.scalar.copy(
-                    grouped[:].bitcast(F32).rearrange("p (b c u) -> p b c u", b=nb, u=2),
-                    turned[:].rearrange("p b u c -> p b c u"),
-                )
-                nc.vector.quantize_mx(out=words[:].bitcast(FP8X4), scales=planes[:], in_=grouped[:])
-                for b in range(nb):
-                    wd_codes[first, part[b]] = (words[:, b * P : (b + 1) * P], planes[:, b * P : (b + 1) * P])
+                    at = (n * J_PASSES + b) * P
+                    wd_codes[i, b] = (words[:, at : at + P], planes[:, at : at + P])
+
+        def finish_last(k, b):
+            grouped = keep.tile([P, PASS], BF16, name="last_grouped%d" % b, align_bytes=64)
+            turn_single(k, [b], grouped[:])
+            words = keep.tile([P, P], U32, name="last_words%d" % b, align_bytes=64)
+            planes = keep.tile([P, P], U8, name="last_planes%d" % b, align_bytes=64)
+            nc.vector.quantize_mx(out=words[:].bitcast(FP8X4), scales=planes[:], in_=grouped[:])
+            wd_codes[UNITS[k][0], b] = (words[:], planes[:])
 
         y_rows = out_0.rearrange("(c p t) m -> c p t m", c=N_GROUPS, t=PACK)
         y_sb = [keep.tile([P, PACK, M], F32, name="y_sb%d" % c) for c in range(N_GROUPS)]
         y_planes = keep.tile([P, N_GROUPS, M], U8, name="y_planes", align_bytes=64)
+        whole = [(nc.scalar.copy, 0, M)]
+        halves = [(nc.vector.tensor_copy, 0, M // 2), (nc.scalar.copy, M // 2, M)]
 
         def make_y(i, shares):
             c, t = divmod(i, PACK)
-            accs = [next_bank([P, m1 - m0]) for copy, m0, m1 in shares]
+            accs = [bank(banks.pop(0), [P, m1 - m0]) for copy, m0, m1 in shares]
             for b in range(J_PASSES):
                 words, planes = wd_codes[i, b]
+                h_words, h_planes = h_codes[b]
                 for acc, (copy, m0, m1) in zip(accs, shares):
                     nc.tensor.matmul_mx(
                         out=acc[:],
                         lhsT=words.bitcast(FP8X4),
                         lhsT_scale=planes,
-                        rhs=h_words[b][:, m0:m1].bitcast(FP8X4),
-                        rhs_scale=h_planes[b][:, m0:m1],
+                        rhs=h_words[:, m0:m1].bitcast(FP8X4),
+                        rhs_scale=h_planes[:, m0:m1],
                         start=(b == 0),
                         stop=(b == J_PASSES - 1),
                     )
@@ -270,40 +328,58 @@ def tile_list_leaky_event_layer_kernel(
                 copy(y_sb[c][:, t, m0:m1], acc[:])
             nc.sync.dma_start(out=y_rows[c, :, t, :], in_=y_sb[c][:, t, :])
 
-        def make_y_planes(c, shares, hold):
-            for part, (copy, m0, m1) in enumerate(shares):
-                y_grouped = keep.tile([P, m1 - m0, PACK], BF16, name="y_grouped%d_%d" % (c, part), align_bytes=64)
-                copy(
-                    y_grouped[:].rearrange("p (c i) t -> p c t i", i=4),
-                    y_sb[c][:, :, m0:m1].rearrange("p t (c i) -> p c t i", i=4),
-                )
-                y_words = over_window(hold, 4096 + 2048, [P, m1 - m0], I32, "y_words%d_%d" % (c, part))
-                nc.vector.quantize_mx(
-                    out=y_words[:].bitcast(FP8X4),
-                    scales=y_planes[:, c, m0:m1],
-                    in_=y_grouped[:].rearrange("p m t -> p (m t)"),
-                )
-                (nc.scalar if part else nc.sync).dma_start(
-                    out=out_1[c, :, m0:m1, :].rearrange("p m t -> p (m t)").bitcast(I32), in_=y_words[:]
-                )
+        def group_y(c, copy, m0, m1):
+            grouped = keep.tile([P, m1 - m0, PACK], BF16, name="y_grouped%d_%d" % (c, m0), align_bytes=64)
+            copy(
+                grouped[:].rearrange("p (c i) t -> p c t i", i=4),
+                y_sb[c][:, :, m0:m1].rearrange("p t (c i) -> p c t i", i=4),
+            )
+            return grouped
 
-        halves = [(nc.vector.tensor_copy, 0, M // 2), (nc.scalar.copy, M // 2, M)]
+        def quantise_y(c, m0, m1, grouped, words, queue):
+            nc.vector.quantize_mx(
+                out=words[:].bitcast(FP8X4), scales=y_planes[:, c, m0:m1], in_=grouped[:].rearrange("p m t -> p (m t)")
+            )
+            queue.dma_start(out=out_1[c, :, m0:m1, :].rearrange("p m t -> p (m t)").bitcast(I32), in_=words[:])
 
-        def make_ys(k):
-            first, n = UNITS[k]
-            for i in range(first, first + n):
-                make_y(i, halves if i == N_GROUPS * PACK - 1 else [(nc.scalar.copy, 0, M)])
-            if first + n == PACK:
-                make_y_planes(0, [(nc.scalar.copy, 0, M)], 5)
-
+        pick(0)
+        pick(1)
+        make_rests(0)
+        make_rests(1)
         make_h(0)
         make_h(1)
-        make_wd(0)
-        for k in range(1, len(UNITS)):
-            make_wd(k)
-            make_ys(k - 1)
-        make_ys(len(UNITS) - 1)
-        make_y_planes(1, halves, None)
+        turn([0, 1])
+        pick(2)
+        quantise_h(0, 2)
+        pick(3)
+        turn([2, 3])
+        quantise_h(1, 3)
+        quantise_wd(1, 3)
+        quantise_wd(3, None)
+        for i in range(PACK):
+            make_y(i, whole)
+        y_grouped0 = group_y(0, nc.scalar.copy, 0, M)
+        pick(4)
+        turn([4])
+        pick(5)
+        turn([5])
+        quantise_wd(4, 5)
+        make_y(4, whole)
+        pick(6)
+        turn([6])
+        quantise_y(0, 0, M, y_grouped0, above_pick(6, M, I32, "y_words0"), nc.sync)
+        quantise_wd(5, 6)
+        make_y(5, whole)
+        quantise_wd(6, None)
+        make_y(6, whole)
+        pick(7)
+        finish_last(7, 0)
+        finish_last(7, 1)
+
+        make_y(N_SLICES - 1, halves)
+        for (copy, m0, m1), queue in zip(halves, (nc.sync, nc.scalar)):
+            words = keep.tile([P, m1 - m0], I32, name="y_words1_%d" % m0, align_bytes=64)
+            quantise_y(1, m0, m1, group_y(1, copy, m0, m1), words, queue)
         for q in range(QUADS):
             queue = nc.scalar if q % 2 else nc.sync
             queue.dma_start(

@@ -31,7 +31,8 @@ MOVED_ROWS = 112
 BIG = 3.0e38
 WINDOW_BYTES = 4 * T
 PICKED_AT = 2048
-UNITS = [(i,) for i in range(N_SLICES)]
+GROUP_PARTS = 2
+UNITS = [(0,), (1,), (2,), (3,), (4, 5), (6,), (7,)]
 
 
 def tile_list_leaky_event_layer_kernel(
@@ -48,10 +49,10 @@ def tile_list_leaky_event_layer_kernel(
             return placed.tile(shape, dtype, name=name, align_bytes=64, offset=w * WINDOW_BYTES + at)
 
         def below_pick(k, columns, dtype, name):
-            return on_window(k, PICKED_AT + 64 - 4 * columns, [P, columns], dtype, name)
+            return on_window(K_PASSES + k, 0, [P, columns], dtype, name)
 
         def above_pick(k, columns, dtype, name):
-            return on_window(k, PICKED_AT + 2 * PASS - 64, [P, columns], dtype, name)
+            return on_window(K_PASSES + k, WINDOW_BYTES // 2, [P, columns], dtype, name)
 
         def bank(n, shape):
             return psum.tile(shape, F32, name="bank%d" % n)
@@ -61,21 +62,16 @@ def tile_list_leaky_event_layer_kernel(
 
         tab_planes = keep.tile([P, T], U8, name="tab_planes", align_bytes=64)
         nc.vector.memset(tab_planes[:].bitcast(I32), 0)
-        for q in range(QUADS):
-            nc.scalar.dma_start(
-                out=tab_planes[32 * q : 32 * q + 4 * K_PASSES, :].bitcast(I32),
-                in_=tab_scales[:, 4 * q : 4 * q + 4, :].bitcast(I32),
-            )
         x_planes = keep.tile([P, K_PASSES, M], U8, name="x_planes", align_bytes=64)
         for q in range(QUADS):
-            nc.scalar.dma_start(
+            nc.gpsimd.dma_start(
                 out=x_planes[32 * q : 32 * q + 4, :, :].bitcast(I32),
                 in_=x_scales[:, 4 * q : 4 * q + 4, :].rearrange("a r m -> r a m").bitcast(I32),
             )
         vec_rows = keep.tile([P, PASS], F32, name="vec_rows")
         nc.vector.memset(vec_rows[:], 0.0)
         for v, vec in enumerate((g, leak, thr)):
-            nc.scalar.dma_start(out=vec_rows[J_PASSES * v : J_PASSES * (v + 1), :], in_=vec.rearrange("(b j) -> b j", b=J_PASSES))
+            nc.gpsimd.dma_start(out=vec_rows[J_PASSES * v : J_PASSES * (v + 1), :], in_=vec.rearrange("(b j) -> b j", b=J_PASSES))
         identity = keep.tile([P, P], F32, name="identity")
         make_identity(nc, identity[:])
         vec_turned = bank(BANKS - 1, [P, PACK, P])
@@ -126,8 +122,8 @@ def tile_list_leaky_event_layer_kernel(
 
         def load_pair(k, part):
             c, t = divmod(UNITS[k][0], PACK)
-            cols = slice(part * T // 2, (part + 1) * T // 2)
-            two_rows = ring.tile([P, 2, T // 2], F32, name="two_rows", bufs=2)
+            cols = slice(part * T // 4, (part + 1) * T // 4)
+            two_rows = on_window(K_PASSES + len(UNITS) + 2, 4096 * part, [P, 2, T // 4], F32, "two_rows%d" % part)
             nc.sync.dma_start(out=two_rows[:], in_=wd_rows[c, :, t : t + 2, cols])
             nc.scalar.copy(
                 windows[k][:, cols].bitcast(BF16).rearrange("p (j e) -> p j e", e=2),
@@ -140,6 +136,11 @@ def tile_list_leaky_event_layer_kernel(
         v_words = [keep.tile([P, S], U32, name="v_words%d" % a, align_bytes=64) for a in range(K_PASSES)]
         v_planes = [keep.tile([P, S], U8, name="v_planes%d" % a, align_bytes=64) for a in range(K_PASSES)]
         load_tab(0)
+        for q in range(QUADS):
+            nc.sync.dma_start(
+                out=tab_planes[32 * q : 32 * q + 4 * K_PASSES, :].bitcast(I32),
+                in_=tab_scales[:, 4 * q : 4 * q + 4, :].bitcast(I32),
+            )
         load_tab(1)
         load_x()
         load_tab(2)
@@ -155,8 +156,12 @@ def tile_list_leaky_event_layer_kernel(
         load_wd(1)
         load_prev(0)
         load_prev(1)
-        for k in range(2, len(UNITS)):
-            load_wd(k)
+        load_wd(2)
+        load_wd(3)
+        for part in range(4):
+            load_pair(4, part)
+        load_wd(5)
+        load_wd(6)
 
         nc.vector.tensor_copy(v_words[1][:], tab_sb[1][:].bitcast(U32).indirect(offsets[:]))
         for b in range(J_PASSES):
@@ -189,6 +194,7 @@ def tile_list_leaky_event_layer_kernel(
         banks = [n % BANKS for n in range(4 * N_SLICES)]
         h_grouped = [on_window(spare, 0, [P, M, PACK], BF16, "h_grouped0"), keep.tile([P, M, PACK], BF16, name="h_grouped1", align_bytes=64)]
         h_codes = {}
+        clamped = {}
 
         rests = {}
 
@@ -216,14 +222,30 @@ def tile_list_leaky_event_layer_kernel(
                 nc.vector.scalar_tensor_tensor(rounded[:, t, :], currents[b][t][:], gain[:, bt], rests[b, t][:], ALU.mult, ALU.add)
             for t in range(PACK):
                 bt = slice(b * PACK + t, b * PACK + t + 1)
-                nc.vector.tensor_scalar(h_rows[:, t, :], rounded[:, t, :], upper[:, bt], lower[:, bt], ALU.min, ALU.max)
-            nc.scalar.copy(
-                h_grouped[b][:].rearrange("p (c i) t -> p c t i", i=4),
-                h_rows[:].rearrange("p t (c i) -> p c t i", i=4),
-            )
+                nc.gpsimd.tensor_scalar(h_rows[:, t, :], rounded[:, t, :], upper[:, bt], lower[:, bt], ALU.min, ALU.max)
+            clamped[b] = h_rows
+
+        def group_h(b):
+            h_rows = clamped[b]
+            if b == 0:
+                nc.scalar.copy(
+                    h_grouped[b][:].rearrange("p (c i) t -> p c t i", i=4),
+                    h_rows[:].rearrange("p t (c i) -> p c t i", i=4),
+                )
+                return
+            for part in range(GROUP_PARTS):
+                cols = slice(part * M // GROUP_PARTS, (part + 1) * M // GROUP_PARTS)
+                nc.gpsimd.tensor_scalar(
+                    h_grouped[b][:, cols, :],
+                    h_rows[:, :, cols].rearrange("p t m -> p m t"),
+                    1.0,
+                    0.0,
+                    ALU.mult,
+                    ALU.add,
+                )
 
         def quantise_h(b, k):
-            words = above_pick(k, M, U32, "h_words%d" % b)
+            words = on_window(K_PASSES + k, WINDOW_BYTES // 2 + 2048 * b, [P, M], U32, "h_words%d" % b)
             planes = keep.tile([P, M], U8, name="h_planes%d" % b, align_bytes=64)
             nc.vector.quantize_mx(out=words[:].bitcast(FP8X4), scales=planes[:], in_=h_grouped[b][:].rearrange("p m t -> p (m t)"))
             h_codes[b] = (words, planes)
@@ -233,20 +255,25 @@ def tile_list_leaky_event_layer_kernel(
 
         def pick(k):
             dtype = BF16 if len(UNITS[k]) == 1 else U32
-            picks[k] = [
-                on_window(k, PICKED_AT, [P, PASS], dtype, "picked%d" % k),
-                on_window(k, PICKED_AT + 2 * PASS, [P, PASS], dtype, "picked_last")
-                if k == len(UNITS) - 1
-                else ring.tile([P, PASS], dtype, name="picked"),
-            ]
-            for b in range(J_PASSES):
-                nc.vector.tensor_copy(picks[k][b][:], windows[k][:].indirect(list_half(b)))
+            if k == len(UNITS) - 1 or len(UNITS[k]) == 2:
+                picks[k] = [on_window(k if len(UNITS[k]) == 1 else spare + 4, PICKED_AT * (2 - len(UNITS[k])) + 2 * len(UNITS[k]) * PASS * b, [P, PASS], dtype, "picked_half%d_%d" % (k, b))[:] for b in range(J_PASSES)]
+                for b in range(J_PASSES):
+                    nc.vector.tensor_copy(picks[k][b], windows[k][:].indirect(list_half(b)))
+                return
+            if k == 2:
+                picked = on_window(k, PICKED_AT, [P, S], dtype, "picked2")
+            elif k == 5:
+                picked = on_window(K_PASSES + 4, WINDOW_BYTES // 2, [P, S], dtype, "picked5")
+            else:
+                picked = ring.tile([P, S], dtype, name="picked", bufs=2)
+            nc.vector.tensor_copy(picked[:], windows[k][:].indirect(offsets[:]))
+            picks[k] = [picked[:, b * PASS : (b + 1) * PASS] for b in range(J_PASSES)]
 
         def turn_single(k, halves, grouped):
             turned = bank(banks.pop(0), [P, len(halves), 2, P])
             for n, b in enumerate(halves):
                 for u in range(2):
-                    nc.tensor.transpose(turned[:, n, u, :], picks[k][b][:].bitcast(F32)[:, u::2], identity[:])
+                    nc.tensor.transpose(turned[:, n, u, :], picks[k][b].bitcast(F32)[:, u::2], identity[:])
             nc.scalar.copy(
                 grouped.bitcast(F32).rearrange("p (b c u) -> p b c u", b=len(halves), u=2),
                 turned[:].rearrange("p b u c -> p b c u"),
@@ -257,7 +284,7 @@ def tile_list_leaky_event_layer_kernel(
             for b in range(J_PASSES):
                 turned = bank(banks.pop(0), [P, PACK, P])
                 for t in range(PACK):
-                    nc.tensor.transpose(turned[:, t, :], picks[k][b][:].bitcast(F32)[:, t::PACK], identity[:])
+                    nc.tensor.transpose(turned[:, t, :], picks[k][b].bitcast(F32)[:, t::PACK], identity[:])
                 nc.scalar.copy(by_row[:, :, b, :, :], turned[:].bitcast(BF16).rearrange("p t (c e) -> p e c t", e=2))
 
         turned_values = {}
@@ -266,8 +293,10 @@ def tile_list_leaky_event_layer_kernel(
             slices = [i for k in ks for i in UNITS[k]]
             if ks[0] == 0:
                 grouped = on_window(spare, 8192 - 128, [P, len(slices) * S], BF16, "wd_grouped0")
-            elif ks[0] == len(UNITS) - 2:
-                grouped = on_window(len(UNITS) - 1, PICKED_AT, [P, len(slices) * S], BF16, "wd_grouped_late")
+            elif ks[0] == 2:
+                grouped = on_window(spare + 4, -64, [P, len(slices) * S], BF16, "wd_grouped23")
+            elif ks[0] == 4:
+                grouped = on_window(len(UNITS) - 1, 0, [P, len(slices) * S], BF16, "wd_grouped45")
             else:
                 grouped = ring.tile([P, len(slices) * S], BF16, name="wd_grouped", align_bytes=64, bufs=2)
             at = 0
@@ -303,7 +332,7 @@ def tile_list_leaky_event_layer_kernel(
             wd_codes[UNITS[k][0], b] = (words[:], planes[:])
 
         y_rows = out_0.rearrange("(c p t) m -> c p t m", c=N_GROUPS, t=PACK)
-        y_sb = [keep.tile([P, PACK, M], F32, name="y_sb%d" % c) for c in range(N_GROUPS)]
+        y_sb = [on_window(spare + 3, -64, [P, PACK, M], F32, "y_sb0"), keep.tile([P, PACK, M], F32, name="y_sb1")]
         y_planes = keep.tile([P, N_GROUPS, M], U8, name="y_planes", align_bytes=64)
         whole = [(nc.scalar.copy, 0, M)]
         halves = [(nc.vector.tensor_copy, 0, M // 2), (nc.scalar.copy, M // 2, M)]
@@ -336,6 +365,18 @@ def tile_list_leaky_event_layer_kernel(
             )
             return grouped
 
+        def group_on_gpsimd(out, in_):
+            for part in range(GROUP_PARTS):
+                cols = slice(part * M // 4 // GROUP_PARTS, (part + 1) * M // 4 // GROUP_PARTS)
+                nc.gpsimd.tensor_scalar(
+                    out[:, cols, :, :].rearrange("p c t i -> p (c i) t"),
+                    in_[:, cols, :, :].rearrange("p c t i -> p (c i) t"),
+                    1.0,
+                    0.0,
+                    ALU.mult,
+                    ALU.add,
+                )
+
         def quantise_y(c, m0, m1, grouped, words, queue):
             nc.vector.quantize_mx(
                 out=words[:].bitcast(FP8X4), scales=y_planes[:, c, m0:m1], in_=grouped[:].rearrange("p m t -> p (m t)")
@@ -349,32 +390,31 @@ def tile_list_leaky_event_layer_kernel(
         make_h(0)
         make_h(1)
         turn([0, 1])
+        group_h(0)
+        group_h(1)
         pick(2)
-        quantise_h(0, 2)
+        quantise_wd(1, 2)
         pick(3)
-        turn([2, 3])
+        quantise_h(0, 3)
         quantise_h(1, 3)
-        quantise_wd(1, 3)
+        turn([2, 3])
         quantise_wd(3, None)
         for i in range(PACK):
             make_y(i, whole)
-        y_grouped0 = group_y(0, nc.scalar.copy, 0, M)
+        y_grouped0 = group_y(0, group_on_gpsimd, 0, M)
         pick(4)
         turn([4])
         pick(5)
-        turn([5])
         quantise_wd(4, 5)
+        turn([5])
         make_y(4, whole)
-        pick(6)
-        turn([6])
-        quantise_y(0, 0, M, y_grouped0, above_pick(6, M, I32, "y_words0"), nc.sync)
-        quantise_wd(5, 6)
         make_y(5, whole)
-        quantise_wd(6, None)
+        pick(6)
+        quantise_wd(5, 6)
+        finish_last(6, 0)
+        quantise_y(0, 0, M, y_grouped0, above_pick(6, M, I32, "y_words0"), nc.sync)
+        finish_last(6, 1)
         make_y(6, whole)
-        pick(7)
-        finish_last(7, 0)
-        finish_last(7, 1)
 
         make_y(N_SLICES - 1, halves)
         for (copy, m0, m1), queue in zip(halves, (nc.sync, nc.scalar)):

@@ -63,11 +63,6 @@ def tile_list_leaky_event_layer_kernel(
         tab_planes = keep.tile([P, T], U8, name="tab_planes", align_bytes=64)
         nc.vector.memset(tab_planes[:].bitcast(I32), 0)
         x_planes = keep.tile([P, K_PASSES, M], U8, name="x_planes", align_bytes=64)
-        for q in range(QUADS):
-            nc.gpsimd.dma_start(
-                out=x_planes[32 * q : 32 * q + 4, :, :].bitcast(I32),
-                in_=x_scales[:, 4 * q : 4 * q + 4, :].rearrange("a r m -> r a m").bitcast(I32),
-            )
         vec_rows = keep.tile([P, PASS], F32, name="vec_rows")
         nc.vector.memset(vec_rows[:], 0.0)
         for v, vec in enumerate((g, leak, thr)):
@@ -143,6 +138,11 @@ def tile_list_leaky_event_layer_kernel(
             )
         load_tab(1)
         load_x()
+        for q in range(QUADS):
+            nc.sync.dma_start(
+                out=x_planes[32 * q : 32 * q + 4, :, :].bitcast(I32),
+                in_=x_scales[:, 4 * q : 4 * q + 4, :].rearrange("a r m -> r a m").bitcast(I32),
+            )
         load_tab(2)
         load_wd(0)
 

@@ -63,31 +63,8 @@ def tile_list_leaky_event_layer_kernel(
         tab_planes = keep.tile([P, T], U8, name="tab_planes", align_bytes=64)
         nc.vector.memset(tab_planes[:].bitcast(I32), 0)
         x_planes = keep.tile([P, K_PASSES, M], U8, name="x_planes", align_bytes=64)
-        vec_rows = keep.tile([P, PASS], F32, name="vec_rows")
-        nc.vector.memset(vec_rows[:], 0.0)
-        for v, vec in enumerate((g, leak, thr)):
-            nc.gpsimd.dma_start(out=vec_rows[J_PASSES * v : J_PASSES * (v + 1), :], in_=vec.rearrange("(b j) -> b j", b=J_PASSES))
         identity = keep.tile([P, P], F32, name="identity")
         make_identity(nc, identity[:])
-        vec_turned = bank(BANKS - 1, [P, PACK, P])
-        for t in range(PACK):
-            nc.tensor.transpose(vec_turned[:, t, :], vec_rows[:, t::PACK], identity[:])
-        vecs = keep.tile([P, 3 * J_PASSES, PACK], F32, name="vecs")
-        nc.scalar.copy(vecs[:], vec_turned[:, :, 0 : 3 * J_PASSES].rearrange("p t r -> p r t"))
-        gain, leaks, thresholds = [
-            vecs[:, J_PASSES * v : J_PASSES * (v + 1), :].rearrange("p b t -> p (b t)") for v in range(3)
-        ]
-        gain_leak = keep.tile([P, J_PASSES * PACK], F32, name="gain_leak")
-        gain_thr = keep.tile([P, J_PASSES * PACK], F32, name="gain_thr")
-        minus_gain_thr = keep.tile([P, J_PASSES * PACK], F32, name="minus_gain_thr")
-        upper = keep.tile([P, J_PASSES * PACK], F32, name="upper")
-        lower = keep.tile([P, J_PASSES * PACK], F32, name="lower")
-        nc.gpsimd.tensor_tensor(gain_leak[:], gain, leaks, ALU.mult)
-        nc.gpsimd.tensor_tensor(gain_thr[:], gain, thresholds, ALU.mult)
-        nc.gpsimd.tensor_scalar(minus_gain_thr[:], gain_thr[:], -1.0, 0.0, ALU.mult, ALU.add)
-        nc.gpsimd.tensor_scalar(upper[:], gain, 0.0, BIG, ALU.is_ge, ALU.mult)
-        nc.gpsimd.tensor_scalar(lower[:], gain, 0.0, -BIG, ALU.is_lt, ALU.mult)
-
         tab_sb = [on_window(a, 0, [P, T], I32, "tab_sb%d" % a) for a in range(K_PASSES)]
         windows = [
             on_window(K_PASSES + k, 0, [P, T], F32 if len(unit) == 1 else U32, "window%d" % k) for k, unit in enumerate(UNITS)
@@ -132,7 +109,7 @@ def tile_list_leaky_event_layer_kernel(
         v_planes = [keep.tile([P, S], U8, name="v_planes%d" % a, align_bytes=64) for a in range(K_PASSES)]
         load_tab(0)
         for q in range(QUADS):
-            nc.sync.dma_start(
+            (nc.sync if q < 2 else nc.scalar).dma_start(
                 out=tab_planes[32 * q : 32 * q + 4 * K_PASSES, :].bitcast(I32),
                 in_=tab_scales[:, 4 * q : 4 * q + 4, :].bitcast(I32),
             )
@@ -154,6 +131,24 @@ def tile_list_leaky_event_layer_kernel(
                 in_=v_planes[0][4 * a : 4 * a + MOVED_ROWS, :].bitcast(I32),
             )
         load_wd(1)
+        vecs = [keep.tile([P, J_PASSES * PACK], F32, name="vec%d" % v) for v in range(3)]
+        for vec_sb, vec in zip(vecs, (g, leak, thr)):
+            nc.sync.dma_start(
+                out=vec_sb[:].rearrange("p (b t) -> p b t", t=PACK),
+                in_=vec.rearrange("(b p t) -> p b t", b=J_PASSES, t=PACK),
+            )
+        gain, leaks, thresholds = [vec_sb[:] for vec_sb in vecs]
+        gain_leak = keep.tile([P, J_PASSES * PACK], F32, name="gain_leak")
+        gain_thr = keep.tile([P, J_PASSES * PACK], F32, name="gain_thr")
+        minus_gain_thr = keep.tile([P, J_PASSES * PACK], F32, name="minus_gain_thr")
+        upper = keep.tile([P, J_PASSES * PACK], F32, name="upper")
+        lower = keep.tile([P, J_PASSES * PACK], F32, name="lower")
+        nc.gpsimd.tensor_tensor(gain_leak[:], gain, leaks, ALU.mult)
+        nc.gpsimd.tensor_tensor(gain_thr[:], gain, thresholds, ALU.mult)
+        nc.gpsimd.tensor_scalar(minus_gain_thr[:], gain_thr[:], -1.0, 0.0, ALU.mult, ALU.add)
+        nc.gpsimd.tensor_scalar(upper[:], gain, 0.0, BIG, ALU.is_ge, ALU.mult)
+        nc.gpsimd.tensor_scalar(lower[:], gain, 0.0, -BIG, ALU.is_lt, ALU.mult)
+
         load_prev(0)
         load_prev(1)
         load_wd(2)
@@ -222,7 +217,7 @@ def tile_list_leaky_event_layer_kernel(
                 nc.vector.scalar_tensor_tensor(rounded[:, t, :], currents[b][t][:], gain[:, bt], rests[b, t][:], ALU.mult, ALU.add)
             for t in range(PACK):
                 bt = slice(b * PACK + t, b * PACK + t + 1)
-                nc.gpsimd.tensor_scalar(h_rows[:, t, :], rounded[:, t, :], upper[:, bt], lower[:, bt], ALU.min, ALU.max)
+                (nc.gpsimd if b else nc.vector).tensor_scalar(h_rows[:, t, :], rounded[:, t, :], upper[:, bt], lower[:, bt], ALU.min, ALU.max)
             clamped[b] = h_rows
 
         def group_h(b):

@@ -187,7 +187,7 @@ def tile_list_leaky_event_layer_kernel(
             currents.append(turned)
 
         banks = [n % BANKS for n in range(4 * N_SLICES)]
-        h_grouped = [on_window(spare, 0, [P, M, PACK], BF16, "h_grouped0"), keep.tile([P, M, PACK], BF16, name="h_grouped1", align_bytes=64)]
+        h_grouped = [on_window(spare, 0, [P, M, PACK], BF16, "h_grouped0"), on_window(1, 0, [P, M, PACK], BF16, "h_grouped1")]
         h_codes = {}
         clamped = {}
 
@@ -208,7 +208,7 @@ def tile_list_leaky_event_layer_kernel(
 
         def make_h(b):
             if b == 0:
-                rounded = on_window(K_PASSES + 1, WINDOW_BYTES // 2, [P, PACK, M], BF16, "rounded0")
+                rounded = keep.tile([P, PACK, M], BF16, name="rounded0")
             else:
                 rounded = keep.tile([P, PACK, M], BF16, name="rounded1")
             h_rows = keep.tile([P, PACK, M], BF16, name="h_rows%d" % b)
@@ -217,30 +217,19 @@ def tile_list_leaky_event_layer_kernel(
                 nc.vector.scalar_tensor_tensor(rounded[:, t, :], currents[b][t][:], gain[:, bt], rests[b, t][:], ALU.mult, ALU.add)
             for t in range(PACK):
                 bt = slice(b * PACK + t, b * PACK + t + 1)
-                (nc.gpsimd if b else nc.vector).tensor_scalar(h_rows[:, t, :], rounded[:, t, :], upper[:, bt], lower[:, bt], ALU.min, ALU.max)
+                nc.vector.tensor_scalar(h_rows[:, t, :], rounded[:, t, :], upper[:, bt], lower[:, bt], ALU.min, ALU.max)
             clamped[b] = h_rows
 
         def group_h(b):
             h_rows = clamped[b]
-            if b == 0:
+            if True:
                 nc.scalar.copy(
                     h_grouped[b][:].rearrange("p (c i) t -> p c t i", i=4),
                     h_rows[:].rearrange("p t (c i) -> p c t i", i=4),
                 )
-                return
-            for part in range(GROUP_PARTS):
-                cols = slice(part * M // GROUP_PARTS, (part + 1) * M // GROUP_PARTS)
-                nc.gpsimd.tensor_scalar(
-                    h_grouped[b][:, cols, :],
-                    h_rows[:, :, cols].rearrange("p t m -> p m t"),
-                    1.0,
-                    0.0,
-                    ALU.mult,
-                    ALU.add,
-                )
 
         def quantise_h(b, k):
-            words = on_window(K_PASSES + k, WINDOW_BYTES // 2 + 2048 * b, [P, M], U32, "h_words%d" % b)
+            words = keep.tile([P, M], U32, name="h_words%d" % b, align_bytes=64)
             planes = keep.tile([P, M], U8, name="h_planes%d" % b, align_bytes=64)
             nc.vector.quantize_mx(out=words[:].bitcast(FP8X4), scales=planes[:], in_=h_grouped[b][:].rearrange("p m t -> p (m t)"))
             h_codes[b] = (words, planes)
@@ -251,14 +240,16 @@ def tile_list_leaky_event_layer_kernel(
         def pick(k):
             dtype = BF16 if len(UNITS[k]) == 1 else U32
             if k == len(UNITS) - 1 or len(UNITS[k]) == 2:
-                picks[k] = [on_window(k if len(UNITS[k]) == 1 else spare + 4, PICKED_AT * (2 - len(UNITS[k])) + 2 * len(UNITS[k]) * PASS * b, [P, PASS], dtype, "picked_half%d_%d" % (k, b))[:] for b in range(J_PASSES)]
+                picks[k] = [on_window(k, PICKED_AT * (2 - len(UNITS[k])) + 2 * len(UNITS[k]) * PASS * b, [P, PASS], dtype, "picked_half%d_%d" % (k, b))[:] for b in range(J_PASSES)]
                 for b in range(J_PASSES):
                     nc.vector.tensor_copy(picks[k][b], windows[k][:].indirect(list_half(b)))
                 return
             if k == 2:
                 picked = on_window(k, PICKED_AT, [P, S], dtype, "picked2")
+            elif k == 3:
+                picked = on_window(1, 0, [P, S], dtype, "picked3")
             elif k == 5:
-                picked = on_window(K_PASSES + 4, WINDOW_BYTES // 2, [P, S], dtype, "picked5")
+                picked = on_window(spare + 4, 0, [P, S], dtype, "picked5")
             else:
                 picked = ring.tile([P, S], dtype, name="picked", bufs=2)
             nc.vector.tensor_copy(picked[:], windows[k][:].indirect(offsets[:]))
@@ -310,7 +301,7 @@ def tile_list_leaky_event_layer_kernel(
             if behind is None:
                 words = keep.tile([P, columns], U32, name="wd_words%d" % k, align_bytes=64)
             else:
-                words = below_pick(behind, columns, U32, "wd_words%d" % k)
+                words = on_window(behind, PICKED_AT + 64 - 4 * columns, [P, columns], U32, "wd_words%d" % k) if behind == 6 else below_pick(behind, columns, U32, "wd_words%d" % k)
             planes = keep.tile([P, columns], U8, name="wd_planes%d" % k, align_bytes=64)
             nc.vector.quantize_mx(out=words[:].bitcast(FP8X4), scales=planes[:], in_=grouped[:])
             for n, i in enumerate(slices):
@@ -319,7 +310,7 @@ def tile_list_leaky_event_layer_kernel(
                     wd_codes[i, b] = (words[:, at : at + P], planes[:, at : at + P])
 
         def finish_last(k, b):
-            grouped = keep.tile([P, PASS], BF16, name="last_grouped%d" % b, align_bytes=64)
+            grouped = on_window(2, 2 * PASS * (1 - b) + 4 * M * (1 - b), [P, PASS], BF16, "last_grouped%d" % b)
             turn_single(k, [b], grouped[:])
             words = keep.tile([P, P], U32, name="last_words%d" % b, align_bytes=64)
             planes = keep.tile([P, P], U8, name="last_planes%d" % b, align_bytes=64)
@@ -360,17 +351,17 @@ def tile_list_leaky_event_layer_kernel(
             )
             return grouped
 
-        def group_on_gpsimd(out, in_):
-            for part in range(GROUP_PARTS):
-                cols = slice(part * M // 4 // GROUP_PARTS, (part + 1) * M // 4 // GROUP_PARTS)
-                nc.gpsimd.tensor_scalar(
-                    out[:, cols, :, :].rearrange("p c t i -> p (c i) t"),
-                    in_[:, cols, :, :].rearrange("p c t i -> p (c i) t"),
-                    1.0,
-                    0.0,
-                    ALU.mult,
-                    ALU.add,
-                )
+        def group_shared(out, in_):
+            split = 256 // 4
+            nc.gpsimd.tensor_scalar(
+                out[:, split:, :, :].rearrange("p c t i -> p (c i) t"),
+                in_[:, split:, :, :].rearrange("p c t i -> p (c i) t"),
+                1.0,
+                0.0,
+                ALU.mult,
+                ALU.add,
+            )
+            nc.scalar.copy(out[:, :split, :, :], in_[:, :split, :, :])
 
         def quantise_y(c, m0, m1, grouped, words, queue):
             nc.vector.quantize_mx(
@@ -388,27 +379,29 @@ def tile_list_leaky_event_layer_kernel(
         group_h(0)
         group_h(1)
         pick(2)
-        quantise_wd(1, 2)
+        quantise_wd(1, None)
+        quantise_h(0, 2)
+        quantise_h(1, 2)
+        make_y(0, whole)
+        make_y(1, whole)
         pick(3)
-        quantise_h(0, 3)
-        quantise_h(1, 3)
-        turn([2, 3])
-        quantise_wd(3, None)
-        for i in range(PACK):
-            make_y(i, whole)
-        y_grouped0 = group_y(0, group_on_gpsimd, 0, M)
         pick(4)
+        turn([2, 3])
         turn([4])
+        quantise_wd(3, None)
+        make_y(2, whole)
+        make_y(3, whole)
+        y_grouped0 = group_y(0, group_shared, 0, M)
         pick(5)
-        quantise_wd(4, 5)
+        quantise_wd(4, None)
         turn([5])
         make_y(4, whole)
         make_y(5, whole)
         pick(6)
         quantise_wd(5, 6)
         finish_last(6, 0)
-        quantise_y(0, 0, M, y_grouped0, above_pick(6, M, I32, "y_words0"), nc.sync)
         finish_last(6, 1)
+        quantise_y(0, 0, M, y_grouped0, on_window(2, 0, [P, M], I32, "y_words0"), nc.sync)
         make_y(6, whole)
 
         make_y(N_SLICES - 1, halves)

@@ -72,7 +72,7 @@ def tile_list_leaky_event_layer_kernel(
         x_sb = keep.tile([P, K_PASSES, 2 * M], U8, name="x_sb", align_bytes=64)
         spare = K_PASSES + len(UNITS)
         prev_sb = [
-            [keep.tile([P, 2, M], F32, name="prev_sb0_0"), keep.tile([P, 2, M], F32, name="prev_sb0_1")],
+            [keep.tile([P, 2, M], F32, name="prev_sb0_0"), on_window(spare + 5, 0, [P, 2, M], F32, "prev_sb0_1")],
             [keep.tile([P, 2, M], F32, name="prev_sb1_0"), on_window(spare, 4096 - 64, [P, 2, M], F32, "prev_sb1_1")],
         ]
         prev_rows = prev.rearrange("(b p t) m -> b p t m", b=J_PASSES, t=PACK)
@@ -211,7 +211,7 @@ def tile_list_leaky_event_layer_kernel(
                 rounded = keep.tile([P, PACK, M], BF16, name="rounded0")
             else:
                 rounded = keep.tile([P, PACK, M], BF16, name="rounded1")
-            h_rows = keep.tile([P, PACK, M], BF16, name="h_rows%d" % b)
+            h_rows = on_window(spare + 5, 4096 * b, [P, PACK, M], BF16, "h_rows%d" % b)
             for t in range(PACK):
                 bt = slice(b * PACK + t, b * PACK + t + 1)
                 nc.vector.scalar_tensor_tensor(rounded[:, t, :], currents[b][t][:], gain[:, bt], rests[b, t][:], ALU.mult, ALU.add)
@@ -222,10 +222,14 @@ def tile_list_leaky_event_layer_kernel(
 
         def group_h(b):
             h_rows = clamped[b]
-            if True:
-                nc.scalar.copy(
-                    h_grouped[b][:].rearrange("p (c i) t -> p c t i", i=4),
-                    h_rows[:].rearrange("p t (c i) -> p c t i", i=4),
+            split = M if b == 0 else 320
+            nc.scalar.copy(
+                h_grouped[b][:, :split, :].rearrange("p (c i) t -> p c t i", i=4),
+                h_rows[:, :, :split].rearrange("p t (c i) -> p c t i", i=4),
+            )
+            if split < M:
+                nc.gpsimd.tensor_scalar(
+                    h_grouped[b][:, split:, :], h_rows[:, :, split:].rearrange("p t m -> p m t"), 1.0, 0.0, ALU.mult, ALU.add
                 )
 
         def quantise_h(b, k):

@@ -31,8 +31,11 @@ MOVED_ROWS = 112
 BIG = 3.0e38
 WINDOW_BYTES = 4 * T
 PICKED_AT = 2048
-GROUP_PARTS = 2
+PAIR_PARTS = 4
+SCALAR_COLUMNS = (M, 320)
 UNITS = [(0,), (1,), (2,), (3,), (4, 5), (6,), (7,)]
+PAIR = 4
+LAST = len(UNITS) - 1
 
 
 def tile_list_leaky_event_layer_kernel(
@@ -42,17 +45,11 @@ def tile_list_leaky_event_layer_kernel(
     with ExitStack() as ctx:
         keep = ctx.enter_context(tc.tile_pool(name="keep", bufs=1))
         placed = ctx.enter_context(tc.tile_pool(name="placed", bufs=1))
-        ring = ctx.enter_context(tc.tile_pool(name="ring", bufs=3))
+        ring = ctx.enter_context(tc.tile_pool(name="ring", bufs=2))
         psum = ctx.enter_context(tc.psum_pool(name="psum", bufs=1))
 
         def on_window(w, at, shape, dtype, name):
             return placed.tile(shape, dtype, name=name, align_bytes=64, offset=w * WINDOW_BYTES + at)
-
-        def below_pick(k, columns, dtype, name):
-            return on_window(K_PASSES + k, 0, [P, columns], dtype, name)
-
-        def above_pick(k, columns, dtype, name):
-            return on_window(K_PASSES + k, WINDOW_BYTES // 2, [P, columns], dtype, name)
 
         def bank(n, shape):
             return psum.tile(shape, F32, name="bank%d" % n)
@@ -94,8 +91,9 @@ def tile_list_leaky_event_layer_kernel(
 
         def load_pair(k, part):
             c, t = divmod(UNITS[k][0], PACK)
-            cols = slice(part * T // 4, (part + 1) * T // 4)
-            two_rows = on_window(K_PASSES + len(UNITS) + 2, 4096 * part, [P, 2, T // 4], F32, "two_rows%d" % part)
+            width = T // PAIR_PARTS
+            cols = slice(part * width, (part + 1) * width)
+            two_rows = on_window(spare + 2, 8 * width * part, [P, 2, width], F32, "two_rows%d" % part)
             nc.sync.dma_start(out=two_rows[:], in_=wd_rows[c, :, t : t + 2, cols])
             nc.scalar.copy(
                 windows[k][:, cols].bitcast(BF16).rearrange("p (j e) -> p j e", e=2),
@@ -153,8 +151,8 @@ def tile_list_leaky_event_layer_kernel(
         load_prev(1)
         load_wd(2)
         load_wd(3)
-        for part in range(4):
-            load_pair(4, part)
+        for part in range(PAIR_PARTS):
+            load_pair(PAIR, part)
         load_wd(5)
         load_wd(6)
 
@@ -187,10 +185,12 @@ def tile_list_leaky_event_layer_kernel(
             currents.append(turned)
 
         banks = [n % BANKS for n in range(4 * N_SLICES)]
-        h_grouped = [on_window(spare, 0, [P, M, PACK], BF16, "h_grouped0"), on_window(1, 0, [P, M, PACK], BF16, "h_grouped1")]
+        h_grouped = [
+            on_window(spare, 0, [P, M, PACK], BF16, "h_grouped0"),
+            on_window(1, 0, [P, M, PACK], BF16, "h_grouped1"),
+        ]
         h_codes = {}
         clamped = {}
-
         rests = {}
 
         def make_rests(b):
@@ -200,17 +200,15 @@ def tile_list_leaky_event_layer_kernel(
                     rest = on_window(2, PICKED_AT, [P, M], F32, "last_rest")
                 else:
                     rest = keep.tile([P, M], F32, name="rest%d_%d" % (b, t))
-                if b == 0:
-                    nc.gpsimd.tensor_scalar(rest[:], prev_sb[b][t // 2][:, t % 2, :], gain_leak[:, bt], minus_gain_thr[:, bt], ALU.mult, ALU.add)
+                rows = prev_sb[b][t // 2][:, t % 2, :]
+                if b == 0 and t < 2:
+                    nc.gpsimd.tensor_scalar(rest[:], rows, gain_leak[:, bt], minus_gain_thr[:, bt], ALU.mult, ALU.add)
                 else:
-                    nc.scalar.activation(rest[:], prev_sb[b][t // 2][:, t % 2, :], ACT.Identity, bias=minus_gain_thr[:, bt], scale=gain_leak[:, bt])
+                    nc.scalar.activation(rest[:], rows, ACT.Identity, bias=minus_gain_thr[:, bt], scale=gain_leak[:, bt])
                 rests[b, t] = rest
 
         def make_h(b):
-            if b == 0:
-                rounded = keep.tile([P, PACK, M], BF16, name="rounded0")
-            else:
-                rounded = keep.tile([P, PACK, M], BF16, name="rounded1")
+            rounded = keep.tile([P, PACK, M], BF16, name="rounded%d" % b)
             h_rows = on_window(spare + 5, 4096 * b, [P, PACK, M], BF16, "h_rows%d" % b)
             for t in range(PACK):
                 bt = slice(b * PACK + t, b * PACK + t + 1)
@@ -222,7 +220,7 @@ def tile_list_leaky_event_layer_kernel(
 
         def group_h(b):
             h_rows = clamped[b]
-            split = M if b == 0 else 320
+            split = SCALAR_COLUMNS[b]
             nc.scalar.copy(
                 h_grouped[b][:, :split, :].rearrange("p (c i) t -> p c t i", i=4),
                 h_rows[:, :, :split].rearrange("p t (c i) -> p c t i", i=4),
@@ -232,7 +230,7 @@ def tile_list_leaky_event_layer_kernel(
                     h_grouped[b][:, split:, :], h_rows[:, :, split:].rearrange("p t m -> p m t"), 1.0, 0.0, ALU.mult, ALU.add
                 )
 
-        def quantise_h(b, k):
+        def quantise_h(b):
             words = keep.tile([P, M], U32, name="h_words%d" % b, align_bytes=64)
             planes = keep.tile([P, M], U8, name="h_planes%d" % b, align_bytes=64)
             nc.vector.quantize_mx(out=words[:].bitcast(FP8X4), scales=planes[:], in_=h_grouped[b][:].rearrange("p m t -> p (m t)"))
@@ -243,8 +241,11 @@ def tile_list_leaky_event_layer_kernel(
 
         def pick(k):
             dtype = BF16 if len(UNITS[k]) == 1 else U32
-            if k == len(UNITS) - 1 or len(UNITS[k]) == 2:
-                picks[k] = [on_window(k, PICKED_AT * (2 - len(UNITS[k])) + 2 * len(UNITS[k]) * PASS * b, [P, PASS], dtype, "picked_half%d_%d" % (k, b))[:] for b in range(J_PASSES)]
+            if k in (PAIR, LAST):
+                first, size = (0, 4 * PASS) if k == PAIR else (PICKED_AT, 2 * PASS)
+                picks[k] = [
+                    on_window(k, first + size * b, [P, PASS], dtype, "picked_half%d_%d" % (k, b))[:] for b in range(J_PASSES)
+                ]
                 for b in range(J_PASSES):
                     nc.vector.tensor_copy(picks[k][b], windows[k][:].indirect(list_half(b)))
                 return
@@ -255,7 +256,7 @@ def tile_list_leaky_event_layer_kernel(
             elif k == 5:
                 picked = on_window(spare + 4, 0, [P, S], dtype, "picked5")
             else:
-                picked = ring.tile([P, S], dtype, name="picked", bufs=2)
+                picked = ring.tile([P, S], dtype, name="picked")
             nc.vector.tensor_copy(picked[:], windows[k][:].indirect(offsets[:]))
             picks[k] = [picked[:, b * PASS : (b + 1) * PASS] for b in range(J_PASSES)]
 
@@ -285,10 +286,10 @@ def tile_list_leaky_event_layer_kernel(
                 grouped = on_window(spare, 8192 - 128, [P, len(slices) * S], BF16, "wd_grouped0")
             elif ks[0] == 2:
                 grouped = on_window(spare + 4, -64, [P, len(slices) * S], BF16, "wd_grouped23")
-            elif ks[0] == 4:
-                grouped = on_window(len(UNITS) - 1, 0, [P, len(slices) * S], BF16, "wd_grouped45")
+            elif ks[0] == PAIR:
+                grouped = on_window(LAST, 0, [P, len(slices) * S], BF16, "wd_grouped45")
             else:
-                grouped = ring.tile([P, len(slices) * S], BF16, name="wd_grouped", align_bytes=64, bufs=2)
+                grouped = keep.tile([P, len(slices) * S], BF16, name="wd_grouped6", align_bytes=64)
             at = 0
             for k in ks:
                 width = len(UNITS[k]) * S
@@ -299,13 +300,13 @@ def tile_list_leaky_event_layer_kernel(
                 at = at + width
             turned_values[ks[-1]] = (slices, grouped)
 
-        def quantise_wd(k, behind):
+        def quantise_wd(k):
             slices, grouped = turned_values[k]
             columns = len(slices) * J_PASSES * P
-            if behind is None:
-                words = keep.tile([P, columns], U32, name="wd_words%d" % k, align_bytes=64)
+            if k == LAST - 1:
+                words = on_window(LAST, PICKED_AT + 64 - 4 * columns, [P, columns], U32, "wd_words%d" % k)
             else:
-                words = on_window(behind, PICKED_AT + 64 - 4 * columns, [P, columns], U32, "wd_words%d" % k) if behind == 6 else below_pick(behind, columns, U32, "wd_words%d" % k)
+                words = keep.tile([P, columns], U32, name="wd_words%d" % k, align_bytes=64)
             planes = keep.tile([P, columns], U8, name="wd_planes%d" % k, align_bytes=64)
             nc.vector.quantize_mx(out=words[:].bitcast(FP8X4), scales=planes[:], in_=grouped[:])
             for n, i in enumerate(slices):
@@ -314,7 +315,7 @@ def tile_list_leaky_event_layer_kernel(
                     wd_codes[i, b] = (words[:, at : at + P], planes[:, at : at + P])
 
         def finish_last(k, b):
-            grouped = on_window(2, 2 * PASS * (1 - b) + 4 * M * (1 - b), [P, PASS], BF16, "last_grouped%d" % b)
+            grouped = on_window(2, (2 * PASS + 4 * M) * (1 - b), [P, PASS], BF16, "last_grouped%d" % b)
             turn_single(k, [b], grouped[:])
             words = keep.tile([P, P], U32, name="last_words%d" % b, align_bytes=64)
             planes = keep.tile([P, P], U8, name="last_planes%d" % b, align_bytes=64)
@@ -356,7 +357,7 @@ def tile_list_leaky_event_layer_kernel(
             return grouped
 
         def group_shared(out, in_):
-            split = 256 // 4
+            split = M // 2 // 4
             nc.gpsimd.tensor_scalar(
                 out[:, split:, :, :].rearrange("p c t i -> p (c i) t"),
                 in_[:, split:, :, :].rearrange("p c t i -> p (c i) t"),
@@ -383,31 +384,30 @@ def tile_list_leaky_event_layer_kernel(
         group_h(0)
         group_h(1)
         pick(2)
-        quantise_wd(1, None)
-        quantise_h(0, 2)
-        quantise_h(1, 2)
+        quantise_wd(1)
+        quantise_h(0)
+        quantise_h(1)
         make_y(0, whole)
         make_y(1, whole)
         pick(3)
-        pick(4)
+        pick(PAIR)
         turn([2, 3])
-        turn([4])
-        quantise_wd(3, None)
+        turn([PAIR])
+        quantise_wd(3)
         make_y(2, whole)
         make_y(3, whole)
         y_grouped0 = group_y(0, group_shared, 0, M)
         pick(5)
-        quantise_wd(4, None)
+        quantise_wd(PAIR)
         turn([5])
         make_y(4, whole)
         make_y(5, whole)
-        pick(6)
-        quantise_wd(5, 6)
-        finish_last(6, 0)
-        finish_last(6, 1)
+        pick(LAST)
+        quantise_wd(5)
+        finish_last(LAST, 0)
+        finish_last(LAST, 1)
         quantise_y(0, 0, M, y_grouped0, on_window(2, 0, [P, M], I32, "y_words0"), nc.sync)
         make_y(6, whole)
-
         make_y(N_SLICES - 1, halves)
         for (copy, m0, m1), queue in zip(halves, (nc.sync, nc.scalar)):
             words = keep.tile([P, m1 - m0], I32, name="y_words1_%d" % m0, align_bytes=64)

@@ -24,18 +24,22 @@ K_PASSES = K // PASS
 J_PASSES = S // PASS
 N_GROUPS = N // PASS
 N_SLICES = N_GROUPS * PACK
-M_CHUNKS = M // P
 QUADS = 4
 BANKS = 8
-MOVED_ROWS = 112
+MOVED_ROWS = 100
 BIG = 3.0e38
+KB = 1024
 WINDOW_BYTES = 4 * T
-PICKED_AT = 2048
 PAIR_PARTS = 4
-SCALAR_COLUMNS = (M, 320)
-UNITS = [(0,), (1,), (2,), (3,), (4, 5), (6,), (7,)]
-PAIR = 4
+UNITS = [(0,), (1,), (4,), (2, 3), (5,), (6,), (7,)]
+PAIR = 3
 LAST = len(UNITS) - 1
+
+TAB_AT = 0
+WD_AT = TAB_AT + K_PASSES * WINDOW_BYTES
+ROWS_AT = WD_AT + len(UNITS) * WINDOW_BYTES
+PREV_AT = ROWS_AT + 2 * WINDOW_BYTES + 4 * KB
+EARLY_AT = PREV_AT + 24 * KB
 
 
 def tile_list_leaky_event_layer_kernel(
@@ -45,11 +49,10 @@ def tile_list_leaky_event_layer_kernel(
     with ExitStack() as ctx:
         keep = ctx.enter_context(tc.tile_pool(name="keep", bufs=1))
         placed = ctx.enter_context(tc.tile_pool(name="placed", bufs=1))
-        ring = ctx.enter_context(tc.tile_pool(name="ring", bufs=2))
         psum = ctx.enter_context(tc.psum_pool(name="psum", bufs=1))
 
-        def on_window(w, at, shape, dtype, name):
-            return placed.tile(shape, dtype, name=name, align_bytes=64, offset=w * WINDOW_BYTES + at)
+        def place(at, shape, dtype, name):
+            return placed.tile(shape, dtype, name=name, align_bytes=64, offset=at)
 
         def bank(n, shape):
             return psum.tile(shape, F32, name="bank%d" % n)
@@ -62,48 +65,42 @@ def tile_list_leaky_event_layer_kernel(
         x_planes = keep.tile([P, K_PASSES, M], U8, name="x_planes", align_bytes=64)
         identity = keep.tile([P, P], F32, name="identity")
         make_identity(nc, identity[:])
-        tab_sb = [on_window(a, 0, [P, T], I32, "tab_sb%d" % a) for a in range(K_PASSES)]
+        tab_sb = [place(TAB_AT + a * WINDOW_BYTES, [P, T], I32, "tab_sb%d" % a) for a in range(K_PASSES)]
         windows = [
-            on_window(K_PASSES + k, 0, [P, T], F32 if len(unit) == 1 else U32, "window%d" % k) for k, unit in enumerate(UNITS)
+            place(WD_AT + k * WINDOW_BYTES, [P, T], F32 if len(unit) == 1 else U32, "window%d" % k) for k, unit in enumerate(UNITS)
         ]
         x_sb = keep.tile([P, K_PASSES, 2 * M], U8, name="x_sb", align_bytes=64)
-        spare = K_PASSES + len(UNITS)
-        prev_sb = [
-            [keep.tile([P, 2, M], F32, name="prev_sb0_0"), on_window(spare + 5, 0, [P, 2, M], F32, "prev_sb0_1")],
-            [keep.tile([P, 2, M], F32, name="prev_sb1_0"), on_window(spare, 4096 - 64, [P, 2, M], F32, "prev_sb1_1")],
-        ]
+        prev_at = [[PREV_AT + 4 * KB * (2 * b + u) for u in range(2)] for b in range(J_PASSES)]
+        prev_sb = [[place(prev_at[b][u], [P, 2, M], F32, "prev_sb%d_%d" % (b, u)) for u in range(2)] for b in range(J_PASSES)]
         prev_rows = prev.rearrange("(b p t) m -> b p t m", b=J_PASSES, t=PACK)
         wd_rows = wdT.rearrange("(c p t) j -> c p t j", c=N_GROUPS, t=PACK)
 
         def load_tab(a):
             nc.sync.dma_start(out=tab_sb[a][:], in_=tab_words[a].rearrange("p n t -> p (n t)").bitcast(I32))
 
-        def load_x():
-            nc.sync.dma_start(out=x_sb[:].bitcast(I32), in_=x_words.rearrange("a p n -> p a n").bitcast(I32))
+        def load_prev(b, u):
+            nc.sync.dma_start(out=prev_sb[b][u][:], in_=prev_rows[b, :, 2 * u : 2 * u + 2, :])
 
-        def load_prev(b):
-            for u in range(2):
-                nc.sync.dma_start(out=prev_sb[b][u][:], in_=prev_rows[b, :, 2 * u : 2 * u + 2, :])
-
-        def load_wd(k):
+        def load_unit(k):
             c, t = divmod(UNITS[k][0], PACK)
-            nc.sync.dma_start(out=windows[k][:], in_=wd_rows[c, :, t, :])
-
-        def load_pair(k, part):
-            c, t = divmod(UNITS[k][0], PACK)
+            if len(UNITS[k]) == 1:
+                nc.sync.dma_start(out=windows[k][:], in_=wd_rows[c, :, t, :])
+                return
             width = T // PAIR_PARTS
-            cols = slice(part * width, (part + 1) * width)
-            two_rows = on_window(spare + 2, 8 * width * part, [P, 2, width], F32, "two_rows%d" % part)
-            nc.sync.dma_start(out=two_rows[:], in_=wd_rows[c, :, t : t + 2, cols])
-            nc.scalar.copy(
-                windows[k][:, cols].bitcast(BF16).rearrange("p (j e) -> p j e", e=2),
-                two_rows[:].rearrange("p e j -> p j e"),
-            )
+            for part in range(PAIR_PARTS):
+                cols = slice(part * width, (part + 1) * width)
+                two_rows = place(ROWS_AT + 8 * width * part, [P, 2, width], F32, "two_rows%d" % part)
+                nc.sync.dma_start(out=two_rows[:], in_=wd_rows[c, :, t : t + 2, cols])
+                nc.scalar.copy(
+                    windows[k][:, cols].bitcast(BF16).rearrange("p (j e) -> p j e", e=2),
+                    two_rows[:].rearrange("p e j -> p j e"),
+                )
 
         def list_half(b):
             return offsets[:, b * PASS // 16 : (b + 1) * PASS // 16]
 
-        v_words = [keep.tile([P, S], U32, name="v_words%d" % a, align_bytes=64) for a in range(K_PASSES)]
+        whole_words = [keep.tile([P, PACK, J_PASSES * P], U32, name="v_words%d" % a, align_bytes=64) for a in range(K_PASSES - 1)]
+        half_words = [keep.tile([P, PACK, P], U32, name="v_words_half%d" % b, align_bytes=64) for b in range(J_PASSES)]
         v_planes = [keep.tile([P, S], U8, name="v_planes%d" % a, align_bytes=64) for a in range(K_PASSES)]
         load_tab(0)
         for q in range(QUADS):
@@ -112,28 +109,27 @@ def tile_list_leaky_event_layer_kernel(
                 in_=tab_scales[:, 4 * q : 4 * q + 4, :].bitcast(I32),
             )
         load_tab(1)
-        load_x()
+        nc.sync.dma_start(out=x_sb[:].bitcast(I32), in_=x_words.rearrange("a p n -> p a n").bitcast(I32))
         for q in range(QUADS):
             nc.sync.dma_start(
                 out=x_planes[32 * q : 32 * q + 4, :, :].bitcast(I32),
                 in_=x_scales[:, 4 * q : 4 * q + 4, :].rearrange("a r m -> r a m").bitcast(I32),
             )
         load_tab(2)
-        load_wd(0)
-
-        nc.vector.tensor_copy(v_words[0][:], tab_sb[0][:].bitcast(U32).indirect(offsets[:]))
-        nc.vector.tensor_copy(v_planes[0][:], tab_planes[:].indirect(offsets[:]))
-        for a in range(1, K_PASSES):
-            nc.sync.dma_start(
-                out=v_planes[a][0:MOVED_ROWS, :].bitcast(I32),
-                in_=v_planes[0][4 * a : 4 * a + MOVED_ROWS, :].bitcast(I32),
-            )
-        load_wd(1)
         vecs = [keep.tile([P, J_PASSES * PACK], F32, name="vec%d" % v) for v in range(3)]
         for vec_sb, vec in zip(vecs, (g, leak, thr)):
             nc.sync.dma_start(
                 out=vec_sb[:].rearrange("p (b t) -> p b t", t=PACK),
                 in_=vec.rearrange("(b p t) -> p b t", b=J_PASSES, t=PACK),
+            )
+        load_prev(0, 0)
+
+        nc.vector.tensor_copy(whole_words[0][:].rearrange("p t c -> p c t"), tab_sb[0][:].bitcast(U32).indirect(offsets[:]))
+        nc.vector.tensor_copy(v_planes[0][:].rearrange("p (t c) -> p c t", t=PACK), tab_planes[:].indirect(offsets[:]))
+        for a in range(1, K_PASSES):
+            nc.sync.dma_start(
+                out=v_planes[a][0:MOVED_ROWS, :].bitcast(I32),
+                in_=v_planes[0][4 * a : 4 * a + MOVED_ROWS, :].bitcast(I32),
             )
         gain, leaks, thresholds = [vec_sb[:] for vec_sb in vecs]
         gain_leak = keep.tile([P, J_PASSES * PACK], F32, name="gain_leak")
@@ -147,69 +143,66 @@ def tile_list_leaky_event_layer_kernel(
         nc.gpsimd.tensor_scalar(upper[:], gain, 0.0, BIG, ALU.is_ge, ALU.mult)
         nc.gpsimd.tensor_scalar(lower[:], gain, 0.0, -BIG, ALU.is_lt, ALU.mult)
 
-        load_prev(0)
-        load_prev(1)
-        load_wd(2)
-        load_wd(3)
-        for part in range(PAIR_PARTS):
-            load_pair(PAIR, part)
-        load_wd(5)
-        load_wd(6)
+        load_prev(0, 1)
+        load_prev(1, 0)
+        load_prev(1, 1)
+        for k in range(len(UNITS)):
+            load_unit(k)
 
-        nc.vector.tensor_copy(v_words[1][:], tab_sb[1][:].bitcast(U32).indirect(offsets[:]))
+        nc.vector.tensor_copy(whole_words[1][:].rearrange("p t c -> p c t"), tab_sb[1][:].bitcast(U32).indirect(offsets[:]))
         for b in range(J_PASSES):
-            nc.vector.tensor_copy(v_words[2][:, b * PASS : (b + 1) * PASS], tab_sb[2][:].bitcast(U32).indirect(list_half(b)))
+            nc.vector.tensor_copy(half_words[b][:].rearrange("p t c -> p c t"), tab_sb[2][:].bitcast(U32).indirect(list_half(b)))
 
-        sums = [[bank(b * M_CHUNKS + mc, [P, PASS]) for mc in range(M_CHUNKS)] for b in range(J_PASSES)]
-        for b, passes in [(b, [0]) for b in range(J_PASSES)] + [(b, range(1, K_PASSES)) for b in range(J_PASSES)]:
-            for a in passes:
-                for mc in range(M_CHUNKS):
-                    nc.tensor.matmul_mx(
-                        out=sums[b][mc][:],
-                        lhsT=x_sb[:, a, 2 * mc * P : 2 * (mc + 1) * P].bitcast(FP4X4),
-                        lhsT_scale=x_planes[:, a, mc * P : (mc + 1) * P],
-                        rhs=v_words[a][:, b * PASS : (b + 1) * PASS].bitcast(FP8X4),
-                        rhs_scale=v_planes[a][:, b * PASS : (b + 1) * PASS],
-                        start=(a == 0),
-                        stop=(a == K_PASSES - 1),
-                    )
-        currents = []
+        currents = [[bank(b * PACK + t, [P, M]) for t in range(PACK)] for b in range(J_PASSES)]
+
+        def first_pass(a, b, t):
+            if a < K_PASSES - 1:
+                words = whole_words[a][:, t, b * P : (b + 1) * P]
+            else:
+                words = half_words[b][:, t, :]
+            at = (t * J_PASSES + b) * P
+            nc.tensor.matmul_mx(
+                out=currents[b][t][:],
+                lhsT=words.bitcast(FP8X4),
+                lhsT_scale=v_planes[a][:, at : at + P],
+                rhs=x_sb[:, a, :].bitcast(FP4X4),
+                rhs_scale=x_planes[:, a, :],
+                start=(a == 0),
+                stop=(a == K_PASSES - 1),
+            )
+
         for b in range(J_PASSES):
-            dealt = [keep.tile([P, PACK, P], F32, name="dealt%d_%d" % (b, mc)) for mc in range(M_CHUNKS)]
-            for mc in range(M_CHUNKS):
-                nc.scalar.copy(dealt[mc][:], sums[b][mc][:].rearrange("m (p t) -> m t p", t=PACK))
-            turned = [bank(b * PACK + t, [P, M]) for t in range(PACK)]
             for t in range(PACK):
-                for mc in range(M_CHUNKS):
-                    nc.tensor.transpose(turned[t][:, mc * P : (mc + 1) * P], dealt[mc][:, t, :], identity[:])
-            currents.append(turned)
+                first_pass(0, b, t)
+        for b in range(J_PASSES):
+            for t in range(PACK):
+                for a in range(1, K_PASSES):
+                    first_pass(a, b, t)
 
-        banks = [n % BANKS for n in range(4 * N_SLICES)]
-        h_grouped = [
-            on_window(spare, 0, [P, M, PACK], BF16, "h_grouped0"),
-            on_window(1, 0, [P, M, PACK], BF16, "h_grouped1"),
-        ]
+        banks = [0, 1] + [n % BANKS for n in range(1, 4 * N_SLICES)]
         h_codes = {}
         clamped = {}
         rests = {}
+        h_grouped = {}
+
+        def slot(k):
+            if k == PAIR + 1:
+                return ROWS_AT + 2 * WINDOW_BYTES - 2 * KB
+            if k < 2:
+                return EARLY_AT + k * WINDOW_BYTES
+            return WD_AT + (k - 2) * WINDOW_BYTES
 
         def make_rests(b):
             for t in range(PACK):
                 bt = slice(b * PACK + t, b * PACK + t + 1)
-                if (b, t) == (J_PASSES - 1, PACK - 1):
-                    rest = on_window(2, PICKED_AT, [P, M], F32, "last_rest")
-                else:
-                    rest = keep.tile([P, M], F32, name="rest%d_%d" % (b, t))
+                rest = place(TAB_AT + b * WINDOW_BYTES + 2 * KB * t, [P, M], F32, "rest%d_%d" % (b, t))
                 rows = prev_sb[b][t // 2][:, t % 2, :]
-                if b == 0 and t < 2:
-                    nc.gpsimd.tensor_scalar(rest[:], rows, gain_leak[:, bt], minus_gain_thr[:, bt], ALU.mult, ALU.add)
-                else:
-                    nc.scalar.activation(rest[:], rows, ACT.Identity, bias=minus_gain_thr[:, bt], scale=gain_leak[:, bt])
+                nc.scalar.activation(rest[:], rows, ACT.Identity, bias=minus_gain_thr[:, bt], scale=gain_leak[:, bt])
                 rests[b, t] = rest
 
         def make_h(b):
             rounded = keep.tile([P, PACK, M], BF16, name="rounded%d" % b)
-            h_rows = on_window(spare + 5, 4096 * b, [P, PACK, M], BF16, "h_rows%d" % b)
+            h_rows = place(prev_at[b][1] - 64 * b, [P, PACK, M], BF16, "h_rows%d" % b)
             for t in range(PACK):
                 bt = slice(b * PACK + t, b * PACK + t + 1)
                 nc.vector.scalar_tensor_tensor(rounded[:, t, :], currents[b][t][:], gain[:, bt], rests[b, t][:], ALU.mult, ALU.add)
@@ -219,52 +212,47 @@ def tile_list_leaky_event_layer_kernel(
             clamped[b] = h_rows
 
         def group_h(b):
-            h_rows = clamped[b]
-            split = SCALAR_COLUMNS[b]
+            at = prev_at[1][1] + 4 * KB - 64 if b == 0 else TAB_AT + 2 * WINDOW_BYTES
+            h_grouped[b] = place(at, [P, M, PACK], BF16, "h_grouped%d" % b)
             nc.scalar.copy(
-                h_grouped[b][:, :split, :].rearrange("p (c i) t -> p c t i", i=4),
-                h_rows[:, :, :split].rearrange("p t (c i) -> p c t i", i=4),
+                h_grouped[b][:].rearrange("p (c i) t -> p c t i", i=4),
+                clamped[b][:].rearrange("p t (c i) -> p c t i", i=4),
             )
-            if split < M:
-                nc.gpsimd.tensor_scalar(
-                    h_grouped[b][:, split:, :], h_rows[:, :, split:].rearrange("p t m -> p m t"), 1.0, 0.0, ALU.mult, ALU.add
-                )
 
         def quantise_h(b):
-            words = keep.tile([P, M], U32, name="h_words%d" % b, align_bytes=64)
+            if b == 0:
+                words = keep.tile([P, M], U32, name="h_words0", align_bytes=64)
+            else:
+                words = place(slot(0) + 2 * KB - 64, [P, M], U32, "h_words1")
             planes = keep.tile([P, M], U8, name="h_planes%d" % b, align_bytes=64)
             nc.vector.quantize_mx(out=words[:].bitcast(FP8X4), scales=planes[:], in_=h_grouped[b][:].rearrange("p m t -> p (m t)"))
             h_codes[b] = (words, planes)
 
         picks = {}
         wd_codes = {}
+        turned_values = {}
 
         def pick(k):
-            dtype = BF16 if len(UNITS[k]) == 1 else U32
-            if k in (PAIR, LAST):
-                first, size = (0, 4 * PASS) if k == PAIR else (PICKED_AT, 2 * PASS)
-                picks[k] = [
-                    on_window(k, first + size * b, [P, PASS], dtype, "picked_half%d_%d" % (k, b))[:] for b in range(J_PASSES)
-                ]
-                for b in range(J_PASSES):
-                    nc.vector.tensor_copy(picks[k][b], windows[k][:].indirect(list_half(b)))
-                return
-            if k == 2:
-                picked = on_window(k, PICKED_AT, [P, S], dtype, "picked2")
-            elif k == 3:
-                picked = on_window(1, 0, [P, S], dtype, "picked3")
-            elif k == 5:
-                picked = on_window(spare + 4, 0, [P, S], dtype, "picked5")
-            else:
-                picked = ring.tile([P, S], dtype, name="picked")
-            nc.vector.tensor_copy(picked[:], windows[k][:].indirect(offsets[:]))
-            picks[k] = [picked[:, b * PASS : (b + 1) * PASS] for b in range(J_PASSES)]
+            picks[k] = []
+            for b in range(J_PASSES):
+                size = len(UNITS[k]) * KB
+                at = slot(k) + (2 * KB - size if b == 0 else 4 * KB)
+                if k == PAIR + 1 and b == 1:
+                    at = WD_AT + (k - 2) * WINDOW_BYTES
+                if len(UNITS[k]) == 1:
+                    picked = place(at, [P, 2, 2 * P], BF16, "picked%d_%d" % (k, b))
+                    dealt = picked[:].rearrange("p u (c e) -> p c u e", e=2)
+                else:
+                    picked = place(at, [P, PACK, P], U32, "picked%d_%d" % (k, b))
+                    dealt = picked[:].rearrange("p t c -> p c t")
+                nc.vector.tensor_copy(dealt, windows[k][:].indirect(list_half(b)))
+                picks[k].append(picked)
 
         def turn_single(k, halves, grouped):
             turned = bank(banks.pop(0), [P, len(halves), 2, P])
             for n, b in enumerate(halves):
                 for u in range(2):
-                    nc.tensor.transpose(turned[:, n, u, :], picks[k][b].bitcast(F32)[:, u::2], identity[:])
+                    nc.tensor.transpose(turned[:, n, u, :], picks[k][b][:, u, :].bitcast(F32), identity[:])
             nc.scalar.copy(
                 grouped.bitcast(F32).rearrange("p (b c u) -> p b c u", b=len(halves), u=2),
                 turned[:].rearrange("p b u c -> p b c u"),
@@ -275,47 +263,32 @@ def tile_list_leaky_event_layer_kernel(
             for b in range(J_PASSES):
                 turned = bank(banks.pop(0), [P, PACK, P])
                 for t in range(PACK):
-                    nc.tensor.transpose(turned[:, t, :], picks[k][b].bitcast(F32)[:, t::PACK], identity[:])
+                    nc.tensor.transpose(turned[:, t, :], picks[k][b][:, t, :].bitcast(F32), identity[:])
                 nc.scalar.copy(by_row[:, :, b, :, :], turned[:].bitcast(BF16).rearrange("p t (c e) -> p e c t", e=2))
 
-        turned_values = {}
-
-        def turn(ks):
-            slices = [i for k in ks for i in UNITS[k]]
-            if ks[0] == 0:
-                grouped = on_window(spare, 8192 - 128, [P, len(slices) * S], BF16, "wd_grouped0")
-            elif ks[0] == 2:
-                grouped = on_window(spare + 4, -64, [P, len(slices) * S], BF16, "wd_grouped23")
-            elif ks[0] == PAIR:
-                grouped = on_window(LAST, 0, [P, len(slices) * S], BF16, "wd_grouped45")
+        def turn(k):
+            if k < PAIR:
+                grouped = place(ROWS_AT + (8 * KB + 64 + 2 * KB * k if k else 0), [P, S], BF16, "wd_grouped%d" % k)
             else:
-                grouped = keep.tile([P, len(slices) * S], BF16, name="wd_grouped6", align_bytes=64)
-            at = 0
-            for k in ks:
-                width = len(UNITS[k]) * S
-                if len(UNITS[k]) == 1:
-                    turn_single(k, range(J_PASSES), grouped[:, at : at + width])
-                else:
-                    turn_pair(k, grouped[:, at : at + width])
-                at = at + width
-            turned_values[ks[-1]] = (slices, grouped)
+                grouped = keep.tile([P, len(UNITS[k]) * S], BF16, name="wd_grouped%d" % k, align_bytes=64)
+            if len(UNITS[k]) == 1:
+                turn_single(k, range(J_PASSES), grouped[:])
+            else:
+                turn_pair(k, grouped[:])
+            turned_values[k] = grouped
 
         def quantise_wd(k):
-            slices, grouped = turned_values[k]
-            columns = len(slices) * J_PASSES * P
-            if k == LAST - 1:
-                words = on_window(LAST, PICKED_AT + 64 - 4 * columns, [P, columns], U32, "wd_words%d" % k)
-            else:
-                words = keep.tile([P, columns], U32, name="wd_words%d" % k, align_bytes=64)
+            columns = len(UNITS[k]) * J_PASSES * P
+            words = place(slot(k + 1) + 2 * KB - 64, [P, columns], U32, "wd_words%d" % k)
             planes = keep.tile([P, columns], U8, name="wd_planes%d" % k, align_bytes=64)
-            nc.vector.quantize_mx(out=words[:].bitcast(FP8X4), scales=planes[:], in_=grouped[:])
-            for n, i in enumerate(slices):
+            nc.vector.quantize_mx(out=words[:].bitcast(FP8X4), scales=planes[:], in_=turned_values[k][:])
+            for n, i in enumerate(UNITS[k]):
                 for b in range(J_PASSES):
                     at = (n * J_PASSES + b) * P
                     wd_codes[i, b] = (words[:, at : at + P], planes[:, at : at + P])
 
         def finish_last(k, b):
-            grouped = on_window(2, (2 * PASS + 4 * M) * (1 - b), [P, PASS], BF16, "last_grouped%d" % b)
+            grouped = place(EARLY_AT + b * WINDOW_BYTES, [P, PASS], BF16, "last_grouped%d" % b)
             turn_single(k, [b], grouped[:])
             words = keep.tile([P, P], U32, name="last_words%d" % b, align_bytes=64)
             planes = keep.tile([P, P], U8, name="last_planes%d" % b, align_bytes=64)
@@ -323,7 +296,7 @@ def tile_list_leaky_event_layer_kernel(
             wd_codes[UNITS[k][0], b] = (words[:], planes[:])
 
         y_rows = out_0.rearrange("(c p t) m -> c p t m", c=N_GROUPS, t=PACK)
-        y_sb = [on_window(spare + 3, -64, [P, PACK, M], F32, "y_sb0"), keep.tile([P, PACK, M], F32, name="y_sb1")]
+        y_sb = [keep.tile([P, PACK, M], F32, name="y_sb%d" % c) for c in range(N_GROUPS)]
         y_planes = keep.tile([P, N_GROUPS, M], U8, name="y_planes", align_bytes=64)
         whole = [(nc.scalar.copy, 0, M)]
         halves = [(nc.vector.tensor_copy, 0, M // 2), (nc.scalar.copy, M // 2, M)]
@@ -349,24 +322,15 @@ def tile_list_leaky_event_layer_kernel(
             nc.sync.dma_start(out=y_rows[c, :, t, :], in_=y_sb[c][:, t, :])
 
         def group_y(c, copy, m0, m1):
-            grouped = keep.tile([P, m1 - m0, PACK], BF16, name="y_grouped%d_%d" % (c, m0), align_bytes=64)
+            if (c, m0) == (0, M // 2):
+                grouped = place(WD_AT + LAST * WINDOW_BYTES, [P, m1 - m0, PACK], BF16, "y_grouped0_late")
+            else:
+                grouped = keep.tile([P, m1 - m0, PACK], BF16, name="y_grouped%d_%d" % (c, m0), align_bytes=64)
             copy(
                 grouped[:].rearrange("p (c i) t -> p c t i", i=4),
                 y_sb[c][:, :, m0:m1].rearrange("p t (c i) -> p c t i", i=4),
             )
             return grouped
-
-        def group_shared(out, in_):
-            split = M // 2 // 4
-            nc.gpsimd.tensor_scalar(
-                out[:, split:, :, :].rearrange("p c t i -> p (c i) t"),
-                in_[:, split:, :, :].rearrange("p c t i -> p (c i) t"),
-                1.0,
-                0.0,
-                ALU.mult,
-                ALU.add,
-            )
-            nc.scalar.copy(out[:, :split, :, :], in_[:, :split, :, :])
 
         def quantise_y(c, m0, m1, grouped, words, queue):
             nc.vector.quantize_mx(
@@ -374,40 +338,34 @@ def tile_list_leaky_event_layer_kernel(
             )
             queue.dma_start(out=out_1[c, :, m0:m1, :].rearrange("p m t -> p (m t)").bitcast(I32), in_=words[:])
 
-        pick(0)
-        pick(1)
         make_rests(0)
         make_rests(1)
         make_h(0)
         make_h(1)
-        turn([0, 1])
         group_h(0)
         group_h(1)
-        pick(2)
-        quantise_wd(1)
         quantise_h(0)
+        pick(0)
+        turn(0)
         quantise_h(1)
-        make_y(0, whole)
-        make_y(1, whole)
-        pick(3)
-        pick(PAIR)
-        turn([2, 3])
-        turn([PAIR])
-        quantise_wd(3)
-        make_y(2, whole)
-        make_y(3, whole)
-        y_grouped0 = group_y(0, group_shared, 0, M)
-        pick(5)
-        quantise_wd(PAIR)
-        turn([5])
-        make_y(4, whole)
-        make_y(5, whole)
+        y_grouped0 = None
+        for k in range(1, LAST):
+            pick(k)
+            turn(k)
+            quantise_wd(k - 1)
+            for i in UNITS[k - 1]:
+                make_y(i, whole)
+            if k - 1 == PAIR:
+                y_grouped0 = group_y(0, nc.scalar.copy, 0, M // 2)
         pick(LAST)
-        quantise_wd(5)
         finish_last(LAST, 0)
+        quantise_wd(LAST - 1)
+        make_y(UNITS[LAST - 1][0], whole)
+        y_grouped0_late = group_y(0, nc.vector.tensor_copy, M // 2, M)
         finish_last(LAST, 1)
-        quantise_y(0, 0, M, y_grouped0, on_window(2, 0, [P, M], I32, "y_words0"), nc.sync)
-        make_y(6, whole)
+        for n, grouped in enumerate((y_grouped0, y_grouped0_late)):
+            words = place(EARLY_AT + WINDOW_BYTES + (KB - 64) * (2 * n - 1), [P, M // 2], I32, "y_words0_%d" % n)
+            quantise_y(0, n * M // 2, (n + 1) * M // 2, grouped, words, nc.sync)
         make_y(N_SLICES - 1, halves)
         for (copy, m0, m1), queue in zip(halves, (nc.sync, nc.scalar)):
             words = keep.tile([P, m1 - m0], I32, name="y_words1_%d" % m0, align_bytes=64)

@@ -117,7 +117,7 @@ def tile_list_leaky_event_layer_kernel(
             )
         load_tab(2)
         vecs = [keep.tile([P, J_PASSES * PACK], F32, name="vec%d" % v) for v in range(3)]
-        for vec_sb, vec in zip(vecs, (g, leak, thr)):
+        for vec_sb, vec in zip(vecs, (thr, g, leak)):
             nc.sync.dma_start(
                 out=vec_sb[:].rearrange("p (b t) -> p b t", t=PACK),
                 in_=vec.rearrange("(b p t) -> p b t", b=J_PASSES, t=PACK),
@@ -131,15 +131,15 @@ def tile_list_leaky_event_layer_kernel(
                 out=v_planes[a][0:MOVED_ROWS, :].bitcast(I32),
                 in_=v_planes[0][4 * a : 4 * a + MOVED_ROWS, :].bitcast(I32),
             )
-        gain, leaks, thresholds = [vec_sb[:] for vec_sb in vecs]
+        thresholds, gain, leaks = [vec_sb[:] for vec_sb in vecs]
         gain_leak = keep.tile([P, J_PASSES * PACK], F32, name="gain_leak")
-        gain_thr = keep.tile([P, J_PASSES * PACK], F32, name="gain_thr")
+        minus_thr = keep.tile([P, J_PASSES * PACK], F32, name="minus_thr")
         minus_gain_thr = keep.tile([P, J_PASSES * PACK], F32, name="minus_gain_thr")
         upper = keep.tile([P, J_PASSES * PACK], F32, name="upper")
         lower = keep.tile([P, J_PASSES * PACK], F32, name="lower")
         nc.gpsimd.tensor_tensor(gain_leak[:], gain, leaks, ALU.mult)
-        nc.gpsimd.tensor_tensor(gain_thr[:], gain, thresholds, ALU.mult)
-        nc.gpsimd.tensor_scalar(minus_gain_thr[:], gain_thr[:], -1.0, 0.0, ALU.mult, ALU.add)
+        nc.scalar.activation(minus_thr[:], thresholds, ACT.Identity, scale=-1.0)
+        nc.gpsimd.tensor_tensor(minus_gain_thr[:], gain, minus_thr[:], ALU.mult)
         nc.gpsimd.tensor_scalar(upper[:], gain, 0.0, BIG, ALU.is_ge, ALU.mult)
         nc.gpsimd.tensor_scalar(lower[:], gain, 0.0, -BIG, ALU.is_lt, ALU.mult)
 
@@ -240,8 +240,8 @@ def tile_list_leaky_event_layer_kernel(
                 if k == PAIR + 1 and b == 1:
                     at = WD_AT + (k - 2) * WINDOW_BYTES
                 if len(UNITS[k]) == 1:
-                    picked = place(at, [P, 2, 2 * P], BF16, "picked%d_%d" % (k, b))
-                    dealt = picked[:].rearrange("p u (c e) -> p c u e", e=2)
+                    picked = place(at, [P, PASS], BF16, "picked%d_%d" % (k, b))
+                    dealt = picked[:]
                 else:
                     picked = place(at, [P, PACK, P], U32, "picked%d_%d" % (k, b))
                     dealt = picked[:].rearrange("p t c -> p c t")
@@ -252,7 +252,7 @@ def tile_list_leaky_event_layer_kernel(
             turned = bank(banks.pop(0), [P, len(halves), 2, P])
             for n, b in enumerate(halves):
                 for u in range(2):
-                    nc.tensor.transpose(turned[:, n, u, :], picks[k][b][:, u, :].bitcast(F32), identity[:])
+                    nc.tensor.transpose(turned[:, n, u, :], picks[k][b][:].bitcast(F32)[:, u::2], identity[:])
             nc.scalar.copy(
                 grouped.bitcast(F32).rearrange("p (b c u) -> p b c u", b=len(halves), u=2),
                 turned[:].rearrange("p b u c -> p b c u"),

@@ -30,16 +30,20 @@ MOVED_ROWS = 100
 BIG = 3.0e38
 KB = 1024
 WINDOW_BYTES = 4 * T
-PAIR_PARTS = 4
-UNITS = [(0,), (1,), (4,), (2, 3), (5,), (6,), (7,)]
-PAIR = 3
+UNITS = [(0,), (1,), (2,), (3,), (4, 5), (6,), (7,)]
+PAIR = 4
 LAST = len(UNITS) - 1
+PAIR_CUTS = (0, 512, 1024, 1536, T)
+GPSIMD_GROUP = 384
 
 TAB_AT = 0
-WD_AT = TAB_AT + K_PASSES * WINDOW_BYTES
-ROWS_AT = WD_AT + len(UNITS) * WINDOW_BYTES
-PREV_AT = ROWS_AT + 2 * WINDOW_BYTES + 4 * KB
-EARLY_AT = PREV_AT + 24 * KB
+PREV_AT = TAB_AT + K_PASSES * WINDOW_BYTES
+ROWS_AT = PREV_AT + 24 * KB
+EARLY_AT = ROWS_AT + 24 * KB
+SINGLES_AT = EARLY_AT + 4 * WINDOW_BYTES
+WINDOW_AT = [SINGLES_AT + WINDOW_BYTES * k for k in range(len(UNITS))]
+LATE_PICKS_AT = [(64 - 2 * KB, 256), (192 - 2 * KB, 192 - KB)]
+LAST_PART_AT = ROWS_AT + 8 * PAIR_CUTS[-2]
 
 
 def tile_list_leaky_event_layer_kernel(
@@ -66,9 +70,7 @@ def tile_list_leaky_event_layer_kernel(
         identity = keep.tile([P, P], F32, name="identity")
         make_identity(nc, identity[:])
         tab_sb = [place(TAB_AT + a * WINDOW_BYTES, [P, T], I32, "tab_sb%d" % a) for a in range(K_PASSES)]
-        windows = [
-            place(WD_AT + k * WINDOW_BYTES, [P, T], F32 if len(unit) == 1 else U32, "window%d" % k) for k, unit in enumerate(UNITS)
-        ]
+        windows = [place(WINDOW_AT[k], [P, T], F32 if len(unit) == 1 else U32, "window%d" % k) for k, unit in enumerate(UNITS)]
         x_sb = keep.tile([P, K_PASSES, 2 * M], U8, name="x_sb", align_bytes=64)
         prev_at = [[PREV_AT + 4 * KB * (2 * b + u) for u in range(2)] for b in range(J_PASSES)]
         prev_sb = [[place(prev_at[b][u], [P, 2, M], F32, "prev_sb%d_%d" % (b, u)) for u in range(2)] for b in range(J_PASSES)]
@@ -81,20 +83,23 @@ def tile_list_leaky_event_layer_kernel(
         def load_prev(b, u):
             nc.sync.dma_start(out=prev_sb[b][u][:], in_=prev_rows[b, :, 2 * u : 2 * u + 2, :])
 
+        staged = []
+
         def load_unit(k):
             c, t = divmod(UNITS[k][0], PACK)
             if len(UNITS[k]) == 1:
                 nc.sync.dma_start(out=windows[k][:], in_=wd_rows[c, :, t, :])
                 return
-            width = T // PAIR_PARTS
-            for part in range(PAIR_PARTS):
-                cols = slice(part * width, (part + 1) * width)
-                two_rows = place(ROWS_AT + 8 * width * part, [P, 2, width], F32, "two_rows%d" % part)
-                nc.sync.dma_start(out=two_rows[:], in_=wd_rows[c, :, t : t + 2, cols])
-                nc.scalar.copy(
-                    windows[k][:, cols].bitcast(BF16).rearrange("p (j e) -> p j e", e=2),
-                    two_rows[:].rearrange("p e j -> p j e"),
-                )
+            for j0, j1 in zip(PAIR_CUTS, PAIR_CUTS[1:]):
+                two_rows = place(ROWS_AT + 8 * j0, [P, 2, j1 - j0], F32, "two_rows%d" % j0)
+                nc.sync.dma_start(out=two_rows[:], in_=wd_rows[c, :, t : t + 2, j0:j1])
+                staged.append(two_rows)
+
+        def cast_part(n):
+            nc.scalar.copy(
+                windows[PAIR][:, PAIR_CUTS[n] : PAIR_CUTS[n + 1]].bitcast(BF16).rearrange("p (j e) -> p j e", e=2),
+                staged[n][:].rearrange("p e j -> p j e"),
+            )
 
         def list_half(b):
             return offsets[:, b * PASS // 16 : (b + 1) * PASS // 16]
@@ -179,18 +184,14 @@ def tile_list_leaky_event_layer_kernel(
                 for a in range(1, K_PASSES):
                     first_pass(a, b, t)
 
-        banks = [0, 1] + [n % BANKS for n in range(1, 4 * N_SLICES)]
         h_codes = {}
         clamped = {}
         rests = {}
-        h_grouped = {}
 
         def slot(k):
-            if k == PAIR + 1:
-                return ROWS_AT + 2 * WINDOW_BYTES - 2 * KB
-            if k < 2:
-                return EARLY_AT + k * WINDOW_BYTES
-            return WD_AT + (k - 2) * WINDOW_BYTES
+            if k < 3:
+                return EARLY_AT + (k + 1) * WINDOW_BYTES
+            return WINDOW_AT[k - 2]
 
         def make_rests(b):
             for t in range(PACK):
@@ -200,111 +201,113 @@ def tile_list_leaky_event_layer_kernel(
                 nc.scalar.activation(rest[:], rows, ACT.Identity, bias=minus_gain_thr[:, bt], scale=gain_leak[:, bt])
                 rests[b, t] = rest
 
-        def make_h(b):
-            rounded = keep.tile([P, PACK, M], BF16, name="rounded%d" % b)
-            h_rows = place(prev_at[b][1] - 64 * b, [P, PACK, M], BF16, "h_rows%d" % b)
+        rounded = [keep.tile([P, PACK, M], BF16, name="rounded%d" % b) for b in range(J_PASSES)]
+
+        def add_current(b):
             for t in range(PACK):
                 bt = slice(b * PACK + t, b * PACK + t + 1)
-                nc.vector.scalar_tensor_tensor(rounded[:, t, :], currents[b][t][:], gain[:, bt], rests[b, t][:], ALU.mult, ALU.add)
+                nc.vector.scalar_tensor_tensor(rounded[b][:, t, :], currents[b][t][:], gain[:, bt], rests[b, t][:], ALU.mult, ALU.add)
+
+        def clamp(b):
+            at = prev_at[0][1] if b == 0 else TAB_AT + WINDOW_BYTES + 4 * KB
+            h_rows = place(at, [P, PACK, M], BF16, "h_rows%d" % b)
             for t in range(PACK):
                 bt = slice(b * PACK + t, b * PACK + t + 1)
-                nc.vector.tensor_scalar(h_rows[:, t, :], rounded[:, t, :], upper[:, bt], lower[:, bt], ALU.min, ALU.max)
+                engine = nc.vector if b == 0 else nc.gpsimd
+                engine.tensor_scalar(h_rows[:, t, :], rounded[b][:, t, :], upper[:, bt], lower[:, bt], ALU.min, ALU.max)
             clamped[b] = h_rows
 
+        h_grouped = {}
+
         def group_h(b):
-            at = prev_at[1][1] + 4 * KB - 64 if b == 0 else TAB_AT + 2 * WINDOW_BYTES
-            h_grouped[b] = place(at, [P, M, PACK], BF16, "h_grouped%d" % b)
+            h_grouped[b] = place(prev_at[1][1] if b == 0 else slot(0) + 64, [P, M, PACK], BF16, "h_grouped%d" % b)
             nc.scalar.copy(
                 h_grouped[b][:].rearrange("p (c i) t -> p c t i", i=4),
                 clamped[b][:].rearrange("p t (c i) -> p c t i", i=4),
             )
 
         def quantise_h(b):
-            if b == 0:
-                words = keep.tile([P, M], U32, name="h_words0", align_bytes=64)
-            else:
-                words = place(slot(0) + 2 * KB - 64, [P, M], U32, "h_words1")
+            words = place(slot(b + 1) + 64 - KB, [P, M], U32, "h_words%d" % b)
             planes = keep.tile([P, M], U8, name="h_planes%d" % b, align_bytes=64)
             nc.vector.quantize_mx(out=words[:].bitcast(FP8X4), scales=planes[:], in_=h_grouped[b][:].rearrange("p m t -> p (m t)"))
             h_codes[b] = (words, planes)
 
         picks = {}
         wd_codes = {}
-        turned_values = {}
+        turned = {}
+        wd_grouped = {}
 
-        def pick(k):
-            picks[k] = []
-            for b in range(J_PASSES):
-                size = len(UNITS[k]) * KB
-                at = slot(k) + (2 * KB - size if b == 0 else 4 * KB)
-                if k == PAIR + 1 and b == 1:
-                    at = WD_AT + (k - 2) * WINDOW_BYTES
-                if len(UNITS[k]) == 1:
-                    picked = place(at, [P, PASS], BF16, "picked%d_%d" % (k, b))
-                    dealt = picked[:]
-                else:
-                    picked = place(at, [P, PACK, P], U32, "picked%d_%d" % (k, b))
-                    dealt = picked[:].rearrange("p t c -> p c t")
-                nc.vector.tensor_copy(dealt, windows[k][:].indirect(list_half(b)))
-                picks[k].append(picked)
+        def pick(k, b):
+            size = len(UNITS[k]) * KB
+            at = slot(k) + (2 * KB - size if b == 0 else 4 * KB)
+            if k > PAIR:
+                at = slot(PAIR) + LATE_PICKS_AT[k - PAIR - 1][b]
+            if len(UNITS[k]) == 1:
+                room = 2 * PASS if (k, b) == (PAIR + 1, 0) else PASS
+                picked = place(at, [P, room], BF16, "picked%d_%d" % (k, b))
+                dealt = picked[:, :PASS]
+            else:
+                picked = place(at, [P, PACK, P], U32, "picked%d_%d" % (k, b))
+                dealt = picked[:].rearrange("p t c -> p c t")
+            nc.vector.tensor_copy(dealt, windows[k][:].indirect(list_half(b)))
+            picks[k, b] = picked
 
-        def turn_single(k, halves, grouped):
-            turned = bank(banks.pop(0), [P, len(halves), 2, P])
-            for n, b in enumerate(halves):
-                for u in range(2):
-                    nc.tensor.transpose(turned[:, n, u, :], picks[k][b][:].bitcast(F32)[:, u::2], identity[:])
+        def turn(k, b, n):
+            if len(UNITS[k]) == 2 or k == LAST:
+                turned[k, b] = bank(n, [P, 2 * len(UNITS[k]), P])[:]
+            else:
+                if b == 0:
+                    turned[k] = bank(n, [P, J_PASSES, 2, P])
+                turned[k, b] = turned[k][:, b, :, :]
+            for u in range(2 * len(UNITS[k])):
+                words = picks[k, b][:, u, :].bitcast(F32) if k == PAIR else picks[k, b][:, :PASS].bitcast(F32)[:, u::2]
+                nc.tensor.transpose(turned[k, b][:, u, :], words, identity[:])
+
+        def group_single(k, grouped):
             nc.scalar.copy(
-                grouped.bitcast(F32).rearrange("p (b c u) -> p b c u", b=len(halves), u=2),
-                turned[:].rearrange("p b u c -> p b c u"),
+                grouped.bitcast(F32).rearrange("p (b c u) -> p b c u", b=J_PASSES, u=2),
+                turned[k][:].rearrange("p b u c -> p b c u"),
             )
 
-        def turn_pair(k, grouped):
+        def group_pair(b, grouped):
             by_row = grouped.rearrange("p (e b c t) -> p e b c t", e=2, b=J_PASSES, t=PACK)
-            for b in range(J_PASSES):
-                turned = bank(banks.pop(0), [P, PACK, P])
-                for t in range(PACK):
-                    nc.tensor.transpose(turned[:, t, :], picks[k][b][:, t, :].bitcast(F32), identity[:])
-                nc.scalar.copy(by_row[:, :, b, :, :], turned[:].bitcast(BF16).rearrange("p t (c e) -> p e c t", e=2))
+            nc.scalar.copy(by_row[:, :, b, :, :], turned[PAIR, b].bitcast(BF16).rearrange("p t (c e) -> p e c t", e=2))
 
-        def turn(k):
-            if k < PAIR:
-                grouped = place(ROWS_AT + (8 * KB + 64 + 2 * KB * k if k else 0), [P, S], BF16, "wd_grouped%d" % k)
-            else:
-                grouped = keep.tile([P, len(UNITS[k]) * S], BF16, name="wd_grouped%d" % k, align_bytes=64)
-            if len(UNITS[k]) == 1:
-                turn_single(k, range(J_PASSES), grouped[:])
-            else:
-                turn_pair(k, grouped[:])
-            turned_values[k] = grouped
-
-        def quantise_wd(k):
-            columns = len(UNITS[k]) * J_PASSES * P
-            words = place(slot(k + 1) + 2 * KB - 64, [P, columns], U32, "wd_words%d" % k)
-            planes = keep.tile([P, columns], U8, name="wd_planes%d" % k, align_bytes=64)
-            nc.vector.quantize_mx(out=words[:].bitcast(FP8X4), scales=planes[:], in_=turned_values[k][:])
-            for n, i in enumerate(UNITS[k]):
+        def quantise_wd(slices, grouped, at):
+            columns = len(slices) * J_PASSES * P
+            words = place(at, [P, columns], U32, "wd_words%d" % slices[0])
+            planes = keep.tile([P, columns], U8, name="wd_planes%d" % slices[0], align_bytes=64)
+            nc.vector.quantize_mx(out=words[:].bitcast(FP8X4), scales=planes[:], in_=grouped)
+            for n, i in enumerate(slices):
                 for b in range(J_PASSES):
                     at = (n * J_PASSES + b) * P
                     wd_codes[i, b] = (words[:, at : at + P], planes[:, at : at + P])
 
-        def finish_last(k, b):
-            grouped = place(EARLY_AT + b * WINDOW_BYTES, [P, PASS], BF16, "last_grouped%d" % b)
-            turn_single(k, [b], grouped[:])
+        def group_last(b):
+            wd_grouped[LAST, b] = place(EARLY_AT + b * 4 * KB, [P, PASS], BF16, "last_grouped%d" % b)
+            nc.scalar.copy(
+                wd_grouped[LAST, b][:].bitcast(F32).rearrange("p (c u) -> p c u", u=2), turned[LAST, b].rearrange("p u c -> p c u")
+            )
+
+        def quantise_last(b):
             words = keep.tile([P, P], U32, name="last_words%d" % b, align_bytes=64)
             planes = keep.tile([P, P], U8, name="last_planes%d" % b, align_bytes=64)
-            nc.vector.quantize_mx(out=words[:].bitcast(FP8X4), scales=planes[:], in_=grouped[:])
-            wd_codes[UNITS[k][0], b] = (words[:], planes[:])
+            nc.vector.quantize_mx(out=words[:].bitcast(FP8X4), scales=planes[:], in_=wd_grouped[LAST, b][:])
+            wd_codes[UNITS[LAST][0], b] = (words[:], planes[:])
 
         y_rows = out_0.rearrange("(c p t) m -> c p t m", c=N_GROUPS, t=PACK)
-        y_sb = [keep.tile([P, PACK, M], F32, name="y_sb%d" % c) for c in range(N_GROUPS)]
+        y_sb = [place(LAST_PART_AT + 64 - 8 * KB, [P, PACK, M], F32, "y_sb0"), keep.tile([P, PACK, M], F32, name="y_sb1")]
         y_planes = keep.tile([P, N_GROUPS, M], U8, name="y_planes", align_bytes=64)
         whole = [(nc.scalar.copy, 0, M)]
         halves = [(nc.vector.tensor_copy, 0, M // 2), (nc.scalar.copy, M // 2, M)]
 
-        def make_y(i, shares):
-            c, t = divmod(i, PACK)
-            accs = [bank(banks.pop(0), [P, m1 - m0]) for copy, m0, m1 in shares]
-            for b in range(J_PASSES):
+        sums = {}
+
+        def multiply(i, shares, banks, passes):
+            if passes[0] == 0:
+                sums[i] = [bank(n, [P, m1 - m0]) for n, (copy, m0, m1) in zip(banks, shares)]
+            accs = sums[i]
+            for b in passes:
                 words, planes = wd_codes[i, b]
                 h_words, h_planes = h_codes[b]
                 for acc, (copy, m0, m1) in zip(accs, shares):
@@ -317,20 +320,18 @@ def tile_list_leaky_event_layer_kernel(
                         start=(b == 0),
                         stop=(b == J_PASSES - 1),
                     )
-            for acc, (copy, m0, m1) in zip(accs, shares):
+
+        def store_y(i, shares):
+            c, t = divmod(i, PACK)
+            for acc, (copy, m0, m1) in zip(sums[i], shares):
                 copy(y_sb[c][:, t, m0:m1], acc[:])
             nc.sync.dma_start(out=y_rows[c, :, t, :], in_=y_sb[c][:, t, :])
 
-        def group_y(c, copy, m0, m1):
-            if (c, m0) == (0, M // 2):
-                grouped = place(WD_AT + LAST * WINDOW_BYTES, [P, m1 - m0, PACK], BF16, "y_grouped0_late")
-            else:
-                grouped = keep.tile([P, m1 - m0, PACK], BF16, name="y_grouped%d_%d" % (c, m0), align_bytes=64)
+        def group_y(c, copy, m0, m1, grouped):
             copy(
-                grouped[:].rearrange("p (c i) t -> p c t i", i=4),
+                grouped.rearrange("p (c i) t -> p c t i", i=4),
                 y_sb[c][:, :, m0:m1].rearrange("p t (c i) -> p c t i", i=4),
             )
-            return grouped
 
         def quantise_y(c, m0, m1, grouped, words, queue):
             nc.vector.quantize_mx(
@@ -338,38 +339,98 @@ def tile_list_leaky_event_layer_kernel(
             )
             queue.dma_start(out=out_1[c, :, m0:m1, :].rearrange("p m t -> p (m t)").bitcast(I32), in_=words[:])
 
+        both = [0, 1]
+
+        def unit(k, n0, n1):
+            pick(k, 0)
+            turn(k, 0, n0)
+            pick(k, 1)
+            turn(k, 1, n1)
+
+        def make_y(i, n):
+            multiply(i, whole, [n], both)
+            store_y(i, whole)
+
+        def behind_turn(k):
+            return slot(k) + 2 * KB - 64
+
+        def single(k, at):
+            wd_grouped[k] = place(at, [P, S], BF16, "wd_grouped%d" % k)
+            group_single(k, wd_grouped[k][:])
+
         make_rests(0)
         make_rests(1)
-        make_h(0)
-        make_h(1)
+        add_current(0)
+        clamp(0)
+        add_current(1)
+        clamp(1)
         group_h(0)
+        unit(0, 0, 0)
+        single(0, TAB_AT)
         group_h(1)
+        unit(1, 1, 1)
         quantise_h(0)
-        pick(0)
-        turn(0)
+        quantise_wd([0], wd_grouped[0][:], behind_turn(1))
+        single(1, TAB_AT + 2 * KB)
+        multiply(0, whole, [3], [0])
+        cast_part(0)
+        cast_part(1)
+        unit(2, 2, 2)
         quantise_h(1)
-        y_grouped0 = None
-        for k in range(1, LAST):
-            pick(k)
-            turn(k)
-            quantise_wd(k - 1)
-            for i in UNITS[k - 1]:
-                make_y(i, whole)
-            if k - 1 == PAIR:
-                y_grouped0 = group_y(0, nc.scalar.copy, 0, M // 2)
-        pick(LAST)
-        finish_last(LAST, 0)
-        quantise_wd(LAST - 1)
-        make_y(UNITS[LAST - 1][0], whole)
-        y_grouped0_late = group_y(0, nc.vector.tensor_copy, M // 2, M)
-        finish_last(LAST, 1)
-        for n, grouped in enumerate((y_grouped0, y_grouped0_late)):
-            words = place(EARLY_AT + WINDOW_BYTES + (KB - 64) * (2 * n - 1), [P, M // 2], I32, "y_words0_%d" % n)
-            quantise_y(0, n * M // 2, (n + 1) * M // 2, grouped, words, nc.sync)
-        make_y(N_SLICES - 1, halves)
+        quantise_wd([1], wd_grouped[1][:], behind_turn(2))
+        single(2, ROWS_AT + 4 * KB)
+        cast_part(2)
+        cast_part(3)
+        multiply(0, whole, [3], [1])
+        multiply(1, whole, [4], both)
+        unit(3, 5, 5)
+        quantise_wd([2], wd_grouped[2][:], behind_turn(3))
+        multiply(2, whole, [6], both)
+        single(3, LAST_PART_AT + 64)
+        store_y(0, whole)
+        store_y(1, whole)
+        unit(PAIR, 5, 0)
+        quantise_wd([3], wd_grouped[3][:], behind_turn(PAIR))
+        multiply(3, whole, [1], both)
+        paired = place(TAB_AT + 8 * KB, [P, 2 * S], BF16, "wd_grouped45")
+        group_pair(0, paired[:])
+        group_pair(1, paired[:])
+        store_y(2, whole)
+        store_y(3, whole)
+        unit(5, 0, 0)
+        quantise_wd([4, 5], paired[:], slot(PAIR) + 128 - 4 * KB)
+        single(5, TAB_AT + 12 * KB)
+        y_early = place(TAB_AT + 8 * KB, [P, GPSIMD_GROUP, PACK], BF16, "y_grouped0_early")
+        nc.gpsimd.tensor_copy(y_early[:], y_sb[0][:, :, :GPSIMD_GROUP].rearrange("p t m -> p m t"))
+        make_y(4, 3)
+        make_y(5, 4)
+        pick(LAST, 0)
+        turn(LAST, 0, 5)
+        pick(LAST, 1)
+        turn(LAST, 1, 6)
+        group_last(0)
+        group_last(1)
+        quantise_wd([6], wd_grouped[5][:], WINDOW_AT[LAST] + 4 * KB)
+        quantise_last(0)
+        multiply(6, whole, [7], both)
+        multiply(7, halves, [0, 1], [0])
+        y_late = place(WINDOW_AT[LAST], [P, M - GPSIMD_GROUP, PACK], BF16, "y_grouped0_late")
+        group_y(0, nc.vector.tensor_copy, GPSIMD_GROUP, M, y_late[:])
+        quantise_last(1)
+        multiply(7, halves, [0, 1], [1])
+        store_y(6, whole)
+        y_words0 = place(EARLY_AT + 4 * KB, [P, M], I32, "y_words0")
+        for grouped, m0, m1 in ((y_early, 0, GPSIMD_GROUP), (y_late, GPSIMD_GROUP, M)):
+            nc.vector.quantize_mx(
+                out=y_words0[:, m0:m1].bitcast(FP8X4), scales=y_planes[:, 0, m0:m1], in_=grouped[:].rearrange("p m t -> p (m t)")
+            )
+        nc.sync.dma_start(out=out_1[0].rearrange("p m t -> p (m t)").bitcast(I32), in_=y_words0[:])
+        store_y(7, halves)
         for (copy, m0, m1), queue in zip(halves, (nc.sync, nc.scalar)):
             words = keep.tile([P, m1 - m0], I32, name="y_words1_%d" % m0, align_bytes=64)
-            quantise_y(1, m0, m1, group_y(1, copy, m0, m1), words, queue)
+            grouped = keep.tile([P, m1 - m0, PACK], BF16, name="y_grouped1_%d" % m0, align_bytes=64)
+            group_y(1, copy, m0, m1, grouped[:])
+            quantise_y(1, m0, m1, grouped, words, queue)
         for q in range(QUADS):
             queue = nc.scalar if q % 2 else nc.sync
             queue.dma_start(

@@ -34,7 +34,7 @@ UNITS = [(0,), (1,), (2,), (3,), (4, 5), (6,), (7,)]
 PAIR = 4
 LAST = len(UNITS) - 1
 PAIR_CUTS = (0, 512, 1024, 1536, T)
-GPSIMD_GROUP = 384
+SCALAR_GROUP = 256
 
 TAB_AT = 0
 PREV_AT = TAB_AT + K_PASSES * WINDOW_BYTES
@@ -209,25 +209,27 @@ def tile_list_leaky_event_layer_kernel(
                 nc.vector.scalar_tensor_tensor(rounded[b][:, t, :], currents[b][t][:], gain[:, bt], rests[b, t][:], ALU.mult, ALU.add)
 
         def clamp(b):
-            at = prev_at[0][1] if b == 0 else TAB_AT + WINDOW_BYTES + 4 * KB
+            at = prev_at[b][1] - 64 * b
             h_rows = place(at, [P, PACK, M], BF16, "h_rows%d" % b)
             for t in range(PACK):
                 bt = slice(b * PACK + t, b * PACK + t + 1)
-                engine = nc.vector if b == 0 else nc.gpsimd
-                engine.tensor_scalar(h_rows[:, t, :], rounded[b][:, t, :], upper[:, bt], lower[:, bt], ALU.min, ALU.max)
+                nc.vector.tensor_scalar(h_rows[:, t, :], rounded[b][:, t, :], upper[:, bt], lower[:, bt], ALU.min, ALU.max)
             clamped[b] = h_rows
 
         h_grouped = {}
 
         def group_h(b):
-            h_grouped[b] = place(prev_at[1][1] if b == 0 else slot(0) + 64, [P, M, PACK], BF16, "h_grouped%d" % b)
+            h_grouped[b] = place(prev_at[1][1] + 4 * KB * (b + 1) - 64, [P, M, PACK], BF16, "h_grouped%d" % b)
             nc.scalar.copy(
                 h_grouped[b][:].rearrange("p (c i) t -> p c t i", i=4),
                 clamped[b][:].rearrange("p t (c i) -> p c t i", i=4),
             )
 
         def quantise_h(b):
-            words = place(slot(b + 1) + 64 - KB, [P, M], U32, "h_words%d" % b)
+            if b == 0:
+                words = keep.tile([P, M], U32, name="h_words0", align_bytes=64)
+            else:
+                words = place(behind_turn(0), [P, M], U32, "h_words1")
             planes = keep.tile([P, M], U8, name="h_planes%d" % b, align_bytes=64)
             nc.vector.quantize_mx(out=words[:].bitcast(FP8X4), scales=planes[:], in_=h_grouped[b][:].rearrange("p m t -> p (m t)"))
             h_codes[b] = (words, planes)
@@ -296,7 +298,7 @@ def tile_list_leaky_event_layer_kernel(
             wd_codes[UNITS[LAST][0], b] = (words[:], planes[:])
 
         y_rows = out_0.rearrange("(c p t) m -> c p t m", c=N_GROUPS, t=PACK)
-        y_sb = [place(LAST_PART_AT + 64 - 8 * KB, [P, PACK, M], F32, "y_sb0"), keep.tile([P, PACK, M], F32, name="y_sb1")]
+        y_sb = [place(LAST_PART_AT + 4 * KB - 64, [P, PACK, M], F32, "y_sb0"), keep.tile([P, PACK, M], F32, name="y_sb1")]
         y_planes = keep.tile([P, N_GROUPS, M], U8, name="y_planes", align_bytes=64)
         whole = [(nc.scalar.copy, 0, M)]
         halves = [(nc.vector.tensor_copy, 0, M // 2), (nc.scalar.copy, M // 2, M)]
@@ -365,62 +367,61 @@ def tile_list_leaky_event_layer_kernel(
         add_current(1)
         clamp(1)
         group_h(0)
+        group_h(1)
+        quantise_h(0)
         unit(0, 0, 0)
         single(0, TAB_AT)
-        group_h(1)
-        unit(1, 1, 1)
-        quantise_h(0)
-        quantise_wd([0], wd_grouped[0][:], behind_turn(1))
-        single(1, TAB_AT + 2 * KB)
-        multiply(0, whole, [3], [0])
-        cast_part(0)
-        cast_part(1)
-        unit(2, 2, 2)
         quantise_h(1)
-        quantise_wd([1], wd_grouped[1][:], behind_turn(2))
-        single(2, ROWS_AT + 4 * KB)
+        cast_part(0)
+        unit(1, 1, 1)
+        quantise_wd([0], wd_grouped[0][:], behind_turn(1))
+        multiply(0, whole, [3], both)
+        single(1, ROWS_AT)
+        cast_part(1)
         cast_part(2)
-        cast_part(3)
-        multiply(0, whole, [3], [1])
+        unit(2, 2, 2)
+        quantise_wd([1], wd_grouped[1][:], behind_turn(2))
         multiply(1, whole, [4], both)
+        cast_part(3)
+        single(2, LAST_PART_AT + 64 - 2 * KB)
         unit(3, 5, 5)
-        quantise_wd([2], wd_grouped[2][:], behind_turn(3))
-        multiply(2, whole, [6], both)
         single(3, LAST_PART_AT + 64)
         store_y(0, whole)
         store_y(1, whole)
-        unit(PAIR, 5, 0)
+        unit(PAIR, 5, 3)
+        quantise_wd([2], wd_grouped[2][:], TAB_AT + 4 * KB)
         quantise_wd([3], wd_grouped[3][:], behind_turn(PAIR))
+        multiply(2, whole, [4], both)
         multiply(3, whole, [1], both)
         paired = place(TAB_AT + 8 * KB, [P, 2 * S], BF16, "wd_grouped45")
         group_pair(0, paired[:])
         group_pair(1, paired[:])
         store_y(2, whole)
         store_y(3, whole)
-        unit(5, 0, 0)
-        quantise_wd([4, 5], paired[:], slot(PAIR) + 128 - 4 * KB)
+        y_early = keep.tile([P, SCALAR_GROUP, PACK], BF16, name="y_grouped0_early", align_bytes=64)
+        group_y(0, nc.scalar.copy, 0, SCALAR_GROUP, y_early[:])
+        unit(5, 3, 3)
+        quantise_wd([4, 5], paired[:], TAB_AT + 16 * KB)
         single(5, TAB_AT + 12 * KB)
-        y_early = place(TAB_AT + 8 * KB, [P, GPSIMD_GROUP, PACK], BF16, "y_grouped0_early")
-        nc.gpsimd.tensor_copy(y_early[:], y_sb[0][:, :, :GPSIMD_GROUP].rearrange("p t m -> p m t"))
-        make_y(4, 3)
-        make_y(5, 4)
+        make_y(4, 0)
+        make_y(5, 6)
         pick(LAST, 0)
         turn(LAST, 0, 5)
         pick(LAST, 1)
-        turn(LAST, 1, 6)
+        turn(LAST, 1, 2)
         group_last(0)
         group_last(1)
-        quantise_wd([6], wd_grouped[5][:], WINDOW_AT[LAST] + 4 * KB)
+        quantise_wd([6], wd_grouped[5][:], TAB_AT + 20 * KB)
         quantise_last(0)
         multiply(6, whole, [7], both)
         multiply(7, halves, [0, 1], [0])
-        y_late = place(WINDOW_AT[LAST], [P, M - GPSIMD_GROUP, PACK], BF16, "y_grouped0_late")
-        group_y(0, nc.vector.tensor_copy, GPSIMD_GROUP, M, y_late[:])
+        y_late = place(TAB_AT + 12 * KB, [P, M - SCALAR_GROUP, PACK], BF16, "y_grouped0_late")
+        group_y(0, nc.vector.tensor_copy, SCALAR_GROUP, M, y_late[:])
         quantise_last(1)
         multiply(7, halves, [0, 1], [1])
         store_y(6, whole)
         y_words0 = place(EARLY_AT + 4 * KB, [P, M], I32, "y_words0")
-        for grouped, m0, m1 in ((y_early, 0, GPSIMD_GROUP), (y_late, GPSIMD_GROUP, M)):
+        for grouped, m0, m1 in ((y_early, 0, SCALAR_GROUP), (y_late, SCALAR_GROUP, M)):
             nc.vector.quantize_mx(
                 out=y_words0[:, m0:m1].bitcast(FP8X4), scales=y_planes[:, 0, m0:m1], in_=grouped[:].rearrange("p m t -> p (m t)")
             )

@@ -115,18 +115,15 @@ def tile_list_leaky_event_layer_kernel(
             )
         load_tab(1)
         nc.sync.dma_start(out=x_sb[:].bitcast(I32), in_=x_words.rearrange("a p n -> p a n").bitcast(I32))
-        for q in range(QUADS):
+        for r in range(4):
             nc.sync.dma_start(
-                out=x_planes[32 * q : 32 * q + 4, :, :].bitcast(I32),
-                in_=x_scales[:, 4 * q : 4 * q + 4, :].rearrange("a r m -> r a m").bitcast(I32),
+                out=x_planes[r:P:32, :, :].bitcast(I32),
+                in_=x_scales[:, r:16:4, :].rearrange("a q m -> q a m").bitcast(I32),
             )
         load_tab(2)
-        vecs = [keep.tile([P, J_PASSES * PACK], F32, name="vec%d" % v) for v in range(3)]
+        vecs = [keep.tile([P, J_PASSES, 2 * PACK], F32, name="vec%d" % v) for v in range(3)]
         for vec_sb, vec in zip(vecs, (thr, g, leak)):
-            nc.sync.dma_start(
-                out=vec_sb[:].rearrange("p (b t) -> p b t", t=PACK),
-                in_=vec.rearrange("(b p t) -> p b t", b=J_PASSES, t=PACK),
-            )
+            nc.sync.dma_start(out=vec_sb[:, :, :PACK], in_=vec.rearrange("(b p t) -> p b t", b=J_PASSES, t=PACK))
         load_prev(0, 0)
 
         nc.vector.tensor_copy(whole_words[0][:].rearrange("p t c -> p c t"), tab_sb[0][:].bitcast(U32).indirect(offsets[:]))
@@ -136,12 +133,12 @@ def tile_list_leaky_event_layer_kernel(
                 out=v_planes[a][0:MOVED_ROWS, :].bitcast(I32),
                 in_=v_planes[0][4 * a : 4 * a + MOVED_ROWS, :].bitcast(I32),
             )
-        thresholds, gain, leaks = [vec_sb[:] for vec_sb in vecs]
-        gain_leak = keep.tile([P, J_PASSES * PACK], F32, name="gain_leak")
-        minus_thr = keep.tile([P, J_PASSES * PACK], F32, name="minus_thr")
-        minus_gain_thr = keep.tile([P, J_PASSES * PACK], F32, name="minus_gain_thr")
-        upper = keep.tile([P, J_PASSES * PACK], F32, name="upper")
-        lower = keep.tile([P, J_PASSES * PACK], F32, name="lower")
+        thresholds, gain, leaks = [vec_sb[:, :, :PACK] for vec_sb in vecs]
+        gain_leak = keep.tile([P, J_PASSES, PACK], F32, name="gain_leak")
+        minus_thr = keep.tile([P, J_PASSES, PACK], F32, name="minus_thr")
+        minus_gain_thr = keep.tile([P, J_PASSES, PACK], F32, name="minus_gain_thr")
+        upper = keep.tile([P, J_PASSES, PACK], F32, name="upper")
+        lower = keep.tile([P, J_PASSES, PACK], F32, name="lower")
         nc.gpsimd.tensor_tensor(gain_leak[:], gain, leaks, ALU.mult)
         nc.scalar.activation(minus_thr[:], thresholds, ACT.Identity, scale=-1.0)
         nc.gpsimd.tensor_tensor(minus_gain_thr[:], gain, minus_thr[:], ALU.mult)
@@ -195,25 +192,22 @@ def tile_list_leaky_event_layer_kernel(
 
         def make_rests(b):
             for t in range(PACK):
-                bt = slice(b * PACK + t, b * PACK + t + 1)
                 rest = place(TAB_AT + b * WINDOW_BYTES + 2 * KB * t, [P, M], F32, "rest%d_%d" % (b, t))
                 rows = prev_sb[b][t // 2][:, t % 2, :]
-                nc.scalar.activation(rest[:], rows, ACT.Identity, bias=minus_gain_thr[:, bt], scale=gain_leak[:, bt])
+                nc.scalar.activation(rest[:], rows, ACT.Identity, bias=minus_gain_thr[:, b, t : t + 1], scale=gain_leak[:, b, t : t + 1])
                 rests[b, t] = rest
 
         rounded = [keep.tile([P, PACK, M], BF16, name="rounded%d" % b) for b in range(J_PASSES)]
 
         def add_current(b):
             for t in range(PACK):
-                bt = slice(b * PACK + t, b * PACK + t + 1)
-                nc.vector.scalar_tensor_tensor(rounded[b][:, t, :], currents[b][t][:], gain[:, bt], rests[b, t][:], ALU.mult, ALU.add)
+                nc.vector.scalar_tensor_tensor(rounded[b][:, t, :], currents[b][t][:], gain[:, b, t : t + 1], rests[b, t][:], ALU.mult, ALU.add)
 
         def clamp(b):
             at = prev_at[b][1] - 64 * b
             h_rows = place(at, [P, PACK, M], BF16, "h_rows%d" % b)
             for t in range(PACK):
-                bt = slice(b * PACK + t, b * PACK + t + 1)
-                nc.vector.tensor_scalar(h_rows[:, t, :], rounded[b][:, t, :], upper[:, bt], lower[:, bt], ALU.min, ALU.max)
+                nc.vector.tensor_scalar(h_rows[:, t, :], rounded[b][:, t, :], upper[:, b, t : t + 1], lower[:, b, t : t + 1], ALU.min, ALU.max)
             clamped[b] = h_rows
 
         h_grouped = {}
@@ -432,9 +426,9 @@ def tile_list_leaky_event_layer_kernel(
             grouped = keep.tile([P, m1 - m0, PACK], BF16, name="y_grouped1_%d" % m0, align_bytes=64)
             group_y(1, copy, m0, m1, grouped[:])
             quantise_y(1, m0, m1, grouped, words, queue)
-        for q in range(QUADS):
-            queue = nc.scalar if q % 2 else nc.sync
+        for r in range(4):
+            queue = nc.scalar if r % 2 else nc.sync
             queue.dma_start(
-                out=out_2[:, 4 * q : 4 * q + 4, :].rearrange("c r m -> r c m").bitcast(I32),
-                in_=y_planes[32 * q : 32 * q + 4, :, :].bitcast(I32),
+                out=out_2[:, r:16:4, :].rearrange("c q m -> q c m").bitcast(I32),
+                in_=y_planes[r:P:32, :, :].bitcast(I32),
             )

from contextlib import ExitStack

import concourse.mybir as mybir
from concourse.masks import make_identity

K, T, S, N, M = 1536, 2048, 1024, 1024, 512
FLOPS = 2 * K * S * M + 2 * S * N * M

F32 = mybir.dt.float32
BF16 = mybir.dt.bfloat16
I32 = mybir.dt.int32
U32 = mybir.dt.uint32
U16 = mybir.dt.uint16
U8 = mybir.dt.uint8
FP8X4 = mybir.dt.float8_e4m3fn_x4
FP4X4 = mybir.dt.float4_e2m1fn_x4
ALU = mybir.AluOpType
ACT = mybir.ActivationFunctionType

P = 128
PACK = 4
PASS = P * PACK
K_PASSES = K // PASS
J_PASSES = S // PASS
N_GROUPS = N // PASS
N_SLICES = N_GROUPS * PACK
QUADS = 4
BANKS = 8
MOVED_ROWS = 100
BIG = 3.0e38
KB = 1024
WINDOW_BYTES = 4 * T
UNITS = [(0,), (1,), (2,), (3,), (4, 5), (6,), (7,)]
PAIR = 4
LAST = len(UNITS) - 1
PAIR_CUTS = (0, 512, 1024, 1536, T)
SCALAR_GROUP = 256

TAB_AT = 0
PREV_AT = TAB_AT + K_PASSES * WINDOW_BYTES
ROWS_AT = PREV_AT + 24 * KB
EARLY_AT = ROWS_AT + 24 * KB
SINGLES_AT = EARLY_AT + 4 * WINDOW_BYTES
WINDOW_AT = [SINGLES_AT + WINDOW_BYTES * k for k in range(len(UNITS))]
LATE_PICKS_AT = [(64 - 2 * KB, 256), (192 - 2 * KB, 192 - KB)]
LAST_PART_AT = ROWS_AT + 8 * PAIR_CUTS[-2]


def tile_list_leaky_event_layer_kernel(
    tc, tab_words, tab_scales, x_words, x_scales, offs, prev, leak, thr, g, wdT, out_0, out_1, out_2
):
    nc = tc.nc
    with ExitStack() as ctx:
        keep = ctx.enter_context(tc.tile_pool(name="keep", bufs=1))
        placed = ctx.enter_context(tc.tile_pool(name="placed", bufs=1))
        psum = ctx.enter_context(tc.psum_pool(name="psum", bufs=1))

        def place(at, shape, dtype, name):
            return placed.tile(shape, dtype, name=name, align_bytes=64, offset=at)

        def bank(n, shape):
            return psum.tile(shape, F32, name="bank%d" % n)

        offsets = keep.tile([P, S // 16], U16, name="offsets")
        nc.sync.dma_start(offsets[:], offs)

        tab_planes = keep.tile([P, T], U8, name="tab_planes", align_bytes=64)
        nc.vector.memset(tab_planes[:].bitcast(I32), 0)
        x_planes = keep.tile([P, K_PASSES, M], U8, name="x_planes", align_bytes=64)
        identity = keep.tile([P, P], F32, name="identity")
        make_identity(nc, identity[:])
        tab_sb = [place(TAB_AT + a * WINDOW_BYTES, [P, T], I32, "tab_sb%d" % a) for a in range(K_PASSES)]
        windows = [place(WINDOW_AT[k], [P, T], F32 if len(unit) == 1 else U32, "window%d" % k) for k, unit in enumerate(UNITS)]
        x_sb = keep.tile([P, K_PASSES, 2 * M], U8, name="x_sb", align_bytes=64)
        prev_at = [[PREV_AT + 4 * KB * (2 * b + u) for u in range(2)] for b in range(J_PASSES)]
        prev_sb = [[place(prev_at[b][u], [P, 2, M], F32, "prev_sb%d_%d" % (b, u)) for u in range(2)] for b in range(J_PASSES)]
        prev_rows = prev.rearrange("(b p t) m -> b p t m", b=J_PASSES, t=PACK)
        wd_rows = wdT.rearrange("(c p t) j -> c p t j", c=N_GROUPS, t=PACK)

        def load_tab(a):
            nc.sync.dma_start(out=tab_sb[a][:], in_=tab_words[a].rearrange("p n t -> p (n t)").bitcast(I32))

        def load_prev(b, u):
            nc.sync.dma_start(out=prev_sb[b][u][:], in_=prev_rows[b, :, 2 * u : 2 * u + 2, :])

        staged = []

        def load_unit(k):
            c, t = divmod(UNITS[k][0], PACK)
            if len(UNITS[k]) == 1:
                nc.sync.dma_start(out=windows[k][:], in_=wd_rows[c, :, t, :])
                return
            for j0, j1 in zip(PAIR_CUTS, PAIR_CUTS[1:]):
                two_rows = place(ROWS_AT + 8 * j0, [P, 2, j1 - j0], F32, "two_rows%d" % j0)
                nc.sync.dma_start(out=two_rows[:], in_=wd_rows[c, :, t : t + 2, j0:j1])
                staged.append(two_rows)

        def cast_part(n):
            nc.scalar.copy(
                windows[PAIR][:, PAIR_CUTS[n] : PAIR_CUTS[n + 1]].bitcast(BF16).rearrange("p (j e) -> p j e", e=2),
                staged[n][:].rearrange("p e j -> p j e"),
            )

        def list_half(b):
            return offsets[:, b * PASS // 16 : (b + 1) * PASS // 16]

        whole_words = [keep.tile([P, PACK, J_PASSES * P], U32, name="v_words%d" % a, align_bytes=64) for a in range(K_PASSES - 1)]
        half_words = [keep.tile([P, PACK, P], U32, name="v_words_half%d" % b, align_bytes=64) for b in range(J_PASSES)]
        v_planes = [keep.tile([P, S], U8, name="v_planes%d" % a, align_bytes=64) for a in range(K_PASSES)]
        load_tab(0)
        for q in range(QUADS):
            (nc.sync if q < 2 else nc.scalar).dma_start(
                out=tab_planes[32 * q : 32 * q + 4 * K_PASSES, :].bitcast(I32),
                in_=tab_scales[:, 4 * q : 4 * q + 4, :].bitcast(I32),
            )
        load_tab(1)
        nc.sync.dma_start(out=x_sb[:].bitcast(I32), in_=x_words.rearrange("a p n -> p a n").bitcast(I32))
        for r in range(4):
            nc.sync.dma_start(
                out=x_planes[r:P:32, :, :].bitcast(I32),
                in_=x_scales[:, r:16:4, :].rearrange("a q m -> q a m").bitcast(I32),
            )
        load_tab(2)
        vecs = [keep.tile([P, J_PASSES, 2 * PACK], F32, name="vec%d" % v) for v in range(3)]
        for vec_sb, vec in zip(vecs, (thr, g, leak)):
            nc.sync.dma_start(out=vec_sb[:, :, :PACK], in_=vec.rearrange("(b p t) -> p b t", b=J_PASSES, t=PACK))
        load_prev(0, 0)

        nc.vector.tensor_copy(whole_words[0][:].rearrange("p t c -> p c t"), tab_sb[0][:].bitcast(U32).indirect(offsets[:]))
        nc.vector.tensor_copy(v_planes[0][:].rearrange("p (t c) -> p c t", t=PACK), tab_planes[:].indirect(offsets[:]))
        for a in range(1, K_PASSES):
            nc.sync.dma_start(
                out=v_planes[a][0:MOVED_ROWS, :].bitcast(I32),
                in_=v_planes[0][4 * a : 4 * a + MOVED_ROWS, :].bitcast(I32),
            )
        thresholds, gain, leaks = [vec_sb[:, :, :PACK] for vec_sb in vecs]
        gain_leak = keep.tile([P, J_PASSES, PACK], F32, name="gain_leak")
        minus_thr = keep.tile([P, J_PASSES, PACK], F32, name="minus_thr")
        minus_gain_thr = keep.tile([P, J_PASSES, PACK], F32, name="minus_gain_thr")
        upper = keep.tile([P, J_PASSES, PACK], F32, name="upper")
        lower = keep.tile([P, J_PASSES, PACK], F32, name="lower")
        nc.gpsimd.tensor_tensor(gain_leak[:], gain, leaks, ALU.mult)
        nc.scalar.activation(minus_thr[:], thresholds, ACT.Identity, scale=-1.0)
        nc.gpsimd.tensor_tensor(minus_gain_thr[:], gain, minus_thr[:], ALU.mult)
        nc.gpsimd.tensor_scalar(upper[:], gain, 0.0, BIG, ALU.is_ge, ALU.mult)
        nc.gpsimd.tensor_scalar(lower[:], gain, 0.0, -BIG, ALU.is_lt, ALU.mult)

        load_prev(0, 1)
        load_prev(1, 0)
        load_prev(1, 1)
        for k in range(len(UNITS)):
            load_unit(k)

        nc.vector.tensor_copy(whole_words[1][:].rearrange("p t c -> p c t"), tab_sb[1][:].bitcast(U32).indirect(offsets[:]))
        for b in range(J_PASSES):
            nc.vector.tensor_copy(half_words[b][:].rearrange("p t c -> p c t"), tab_sb[2][:].bitcast(U32).indirect(list_half(b)))

        currents = [[bank(b * PACK + t, [P, M]) for t in range(PACK)] for b in range(J_PASSES)]

        def first_pass(a, b, t):
            if a < K_PASSES - 1:
                words = whole_words[a][:, t, b * P : (b + 1) * P]
            else:
                words = half_words[b][:, t, :]
            at = (t * J_PASSES + b) * P
            nc.tensor.matmul_mx(
                out=currents[b][t][:],
                lhsT=words.bitcast(FP8X4),
                lhsT_scale=v_planes[a][:, at : at + P],
                rhs=x_sb[:, a, :].bitcast(FP4X4),
                rhs_scale=x_planes[:, a, :],
                start=(a == 0),
                stop=(a == K_PASSES - 1),
            )

        for b in range(J_PASSES):
            for t in range(PACK):
                first_pass(0, b, t)
        for b in range(J_PASSES):
            for t in range(PACK):
                for a in range(1, K_PASSES):
                    first_pass(a, b, t)

        h_codes = {}
        clamped = {}
        rests = {}

        def slot(k):
            if k < 3:
                return EARLY_AT + (k + 1) * WINDOW_BYTES
            return WINDOW_AT[k - 2]

        def make_rests(b):
            for t in range(PACK):
                rest = place(TAB_AT + b * WINDOW_BYTES + 2 * KB * t, [P, M], F32, "rest%d_%d" % (b, t))
                rows = prev_sb[b][t // 2][:, t % 2, :]
                nc.scalar.activation(rest[:], rows, ACT.Identity, bias=minus_gain_thr[:, b, t : t + 1], scale=gain_leak[:, b, t : t + 1])
                rests[b, t] = rest

        rounded = [keep.tile([P, PACK, M], BF16, name="rounded%d" % b) for b in range(J_PASSES)]

        def add_current(b):
            for t in range(PACK):
                nc.vector.scalar_tensor_tensor(rounded[b][:, t, :], currents[b][t][:], gain[:, b, t : t + 1], rests[b, t][:], ALU.mult, ALU.add)

        def clamp(b):
            at = prev_at[b][1] - 64 * b
            h_rows = place(at, [P, PACK, M], BF16, "h_rows%d" % b)
            for t in range(PACK):
                nc.vector.tensor_scalar(h_rows[:, t, :], rounded[b][:, t, :], upper[:, b, t : t + 1], lower[:, b, t : t + 1], ALU.min, ALU.max)
            clamped[b] = h_rows

        h_grouped = {}

        def group_h(b):
            h_grouped[b] = place(prev_at[1][1] + 4 * KB * (b + 1) - 64, [P, M, PACK], BF16, "h_grouped%d" % b)
            nc.scalar.copy(
                h_grouped[b][:].rearrange("p (c i) t -> p c t i", i=4),
                clamped[b][:].rearrange("p t (c i) -> p c t i", i=4),
            )

        def quantise_h(b):
            if b == 0:
                words = keep.tile([P, M], U32, name="h_words0", align_bytes=64)
            else:
                words = place(behind_turn(0), [P, M], U32, "h_words1")
            planes = keep.tile([P, M], U8, name="h_planes%d" % b, align_bytes=64)
            nc.vector.quantize_mx(out=words[:].bitcast(FP8X4), scales=planes[:], in_=h_grouped[b][:].rearrange("p m t -> p (m t)"))
            h_codes[b] = (words, planes)

        picks = {}
        wd_codes = {}
        turned = {}
        wd_grouped = {}

        def pick(k, b):
            size = len(UNITS[k]) * KB
            at = slot(k) + (2 * KB - size if b == 0 else 4 * KB)
            if k > PAIR:
                at = slot(PAIR) + LATE_PICKS_AT[k - PAIR - 1][b]
            if len(UNITS[k]) == 1:
                room = 2 * PASS if (k, b) == (PAIR + 1, 0) else PASS
                picked = place(at, [P, room], BF16, "picked%d_%d" % (k, b))
                dealt = picked[:, :PASS]
            else:
                picked = place(at, [P, PACK, P], U32, "picked%d_%d" % (k, b))
                dealt = picked[:].rearrange("p t c -> p c t")
            nc.vector.tensor_copy(dealt, windows[k][:].indirect(list_half(b)))
            picks[k, b] = picked

        def turn(k, b, n):
            if len(UNITS[k]) == 2 or k == LAST:
                turned[k, b] = bank(n, [P, 2 * len(UNITS[k]), P])[:]
            else:
                if b == 0:
                    turned[k] = bank(n, [P, J_PASSES, 2, P])
                turned[k, b] = turned[k][:, b, :, :]
            for u in range(2 * len(UNITS[k])):
                words = picks[k, b][:, u, :].bitcast(F32) if k == PAIR else picks[k, b][:, :PASS].bitcast(F32)[:, u::2]
                nc.tensor.transpose(turned[k, b][:, u, :], words, identity[:])

        def group_single(k, grouped):
            nc.scalar.copy(
                grouped.bitcast(F32).rearrange("p (b c u) -> p b c u", b=J_PASSES, u=2),
                turned[k][:].rearrange("p b u c -> p b c u"),
            )

        def group_pair(b, grouped):
            by_row = grouped.rearrange("p (e b c t) -> p e b c t", e=2, b=J_PASSES, t=PACK)
            nc.scalar.copy(by_row[:, :, b, :, :], turned[PAIR, b].bitcast(BF16).rearrange("p t (c e) -> p e c t", e=2))

        def quantise_wd(slices, grouped, at):
            columns = len(slices) * J_PASSES * P
            words = place(at, [P, columns], U32, "wd_words%d" % slices[0])
            planes = keep.tile([P, columns], U8, name="wd_planes%d" % slices[0], align_bytes=64)
            nc.vector.quantize_mx(out=words[:].bitcast(FP8X4), scales=planes[:], in_=grouped)
            for n, i in enumerate(slices):
                for b in range(J_PASSES):
                    at = (n * J_PASSES + b) * P
                    wd_codes[i, b] = (words[:, at : at + P], planes[:, at : at + P])

        def group_last(b):
            wd_grouped[LAST, b] = place(EARLY_AT + b * 4 * KB, [P, PASS], BF16, "last_grouped%d" % b)
            nc.scalar.copy(
                wd_grouped[LAST, b][:].bitcast(F32).rearrange("p (c u) -> p c u", u=2), turned[LAST, b].rearrange("p u c -> p c u")
            )

        def quantise_last(b):
            words = keep.tile([P, P], U32, name="last_words%d" % b, align_bytes=64)
            planes = keep.tile([P, P], U8, name="last_planes%d" % b, align_bytes=64)
            nc.vector.quantize_mx(out=words[:].bitcast(FP8X4), scales=planes[:], in_=wd_grouped[LAST, b][:])
            wd_codes[UNITS[LAST][0], b] = (words[:], planes[:])

        y_rows = out_0.rearrange("(c p t) m -> c p t m", c=N_GROUPS, t=PACK)
        y_sb = [place(LAST_PART_AT + 4 * KB - 64, [P, PACK, M], F32, "y_sb0"), keep.tile([P, PACK, M], F32, name="y_sb1")]
        y_planes = keep.tile([P, N_GROUPS, M], U8, name="y_planes", align_bytes=64)
        whole = [(nc.scalar.copy, 0, M)]
        halves = [(nc.vector.tensor_copy, 0, M // 2), (nc.scalar.copy, M // 2, M)]

        sums = {}

        def multiply(i, shares, banks, passes):
            if passes[0] == 0:
                sums[i] = [bank(n, [P, m1 - m0]) for n, (copy, m0, m1) in zip(banks, shares)]
            accs = sums[i]
            for b in passes:
                words, planes = wd_codes[i, b]
                h_words, h_planes = h_codes[b]
                for acc, (copy, m0, m1) in zip(accs, shares):
                    nc.tensor.matmul_mx(
                        out=acc[:],
                        lhsT=words.bitcast(FP8X4),
                        lhsT_scale=planes,
                        rhs=h_words[:, m0:m1].bitcast(FP8X4),
                        rhs_scale=h_planes[:, m0:m1],
                        start=(b == 0),
                        stop=(b == J_PASSES - 1),
                    )

        def store_y(i, shares):
            c, t = divmod(i, PACK)
            for acc, (copy, m0, m1) in zip(sums[i], shares):
                copy(y_sb[c][:, t, m0:m1], acc[:])
            nc.sync.dma_start(out=y_rows[c, :, t, :], in_=y_sb[c][:, t, :])

        def group_y(c, copy, m0, m1, grouped):
            copy(
                grouped.rearrange("p (c i) t -> p c t i", i=4),
                y_sb[c][:, :, m0:m1].rearrange("p t (c i) -> p c t i", i=4),
            )

        def quantise_y(c, m0, m1, grouped, words, queue):
            nc.vector.quantize_mx(
                out=words[:].bitcast(FP8X4), scales=y_planes[:, c, m0:m1], in_=grouped[:].rearrange("p m t -> p (m t)")
            )
            queue.dma_start(out=out_1[c, :, m0:m1, :].rearrange("p m t -> p (m t)").bitcast(I32), in_=words[:])

        both = [0, 1]

        def unit(k, n0, n1):
            pick(k, 0)
            turn(k, 0, n0)
            pick(k, 1)
            turn(k, 1, n1)

        def make_y(i, n):
            multiply(i, whole, [n], both)
            store_y(i, whole)

        def behind_turn(k):
            return slot(k) + 2 * KB - 64

        def single(k, at):
            wd_grouped[k] = place(at, [P, S], BF16, "wd_grouped%d" % k)
            group_single(k, wd_grouped[k][:])

        make_rests(0)
        make_rests(1)
        add_current(0)
        clamp(0)
        add_current(1)
        clamp(1)
        group_h(0)
        group_h(1)
        quantise_h(0)
        unit(0, 0, 0)
        single(0, TAB_AT)
        quantise_h(1)
        cast_part(0)
        unit(1, 1, 1)
        quantise_wd([0], wd_grouped[0][:], behind_turn(1))
        multiply(0, whole, [3], both)
        single(1, ROWS_AT)
        cast_part(1)
        cast_part(2)
        unit(2, 2, 2)
        quantise_wd([1], wd_grouped[1][:], behind_turn(2))
        multiply(1, whole, [4], both)
        cast_part(3)
        single(2, LAST_PART_AT + 64 - 2 * KB)
        unit(3, 5, 5)
        single(3, LAST_PART_AT + 64)
        store_y(0, whole)
        store_y(1, whole)
        unit(PAIR, 5, 3)
        quantise_wd([2], wd_grouped[2][:], TAB_AT + 4 * KB)
        quantise_wd([3], wd_grouped[3][:], behind_turn(PAIR))
        multiply(2, whole, [4], both)
        multiply(3, whole, [1], both)
        paired = place(TAB_AT + 8 * KB, [P, 2 * S], BF16, "wd_grouped45")
        group_pair(0, paired[:])
        group_pair(1, paired[:])
        store_y(2, whole)
        store_y(3, whole)
        y_early = keep.tile([P, SCALAR_GROUP, PACK], BF16, name="y_grouped0_early", align_bytes=64)
        group_y(0, nc.scalar.copy, 0, SCALAR_GROUP, y_early[:])
        unit(5, 3, 3)
        quantise_wd([4, 5], paired[:], TAB_AT + 16 * KB)
        single(5, TAB_AT + 12 * KB)
        make_y(4, 0)
        make_y(5, 6)
        pick(LAST, 0)
        turn(LAST, 0, 5)
        pick(LAST, 1)
        turn(LAST, 1, 2)
        group_last(0)
        group_last(1)
        quantise_wd([6], wd_grouped[5][:], TAB_AT + 20 * KB)
        quantise_last(0)
        multiply(6, whole, [7], both)
        multiply(7, halves, [0, 1], [0])
        y_late = place(TAB_AT + 12 * KB, [P, M - SCALAR_GROUP, PACK], BF16, "y_grouped0_late")
        group_y(0, nc.vector.tensor_copy, SCALAR_GROUP, M, y_late[:])
        quantise_last(1)
        multiply(7, halves, [0, 1], [1])
        store_y(6, whole)
        y_words0 = place(EARLY_AT + 4 * KB, [P, M], I32, "y_words0")
        for grouped, m0, m1 in ((y_early, 0, SCALAR_GROUP), (y_late, SCALAR_GROUP, M)):
            nc.vector.quantize_mx(
                out=y_words0[:, m0:m1].bitcast(FP8X4), scales=y_planes[:, 0, m0:m1], in_=grouped[:].rearrange("p m t -> p (m t)")
            )
        nc.sync.dma_start(out=out_1[0].rearrange("p m t -> p (m t)").bitcast(I32), in_=y_words0[:])
        store_y(7, halves)
        for (copy, m0, m1), queue in zip(halves, (nc.sync, nc.scalar)):
            words = keep.tile([P, m1 - m0], I32, name="y_words1_%d" % m0, align_bytes=64)
            grouped = keep.tile([P, m1 - m0, PACK], BF16, name="y_grouped1_%d" % m0, align_bytes=64)
            group_y(1, copy, m0, m1, grouped[:])
            quantise_y(1, m0, m1, grouped, words, queue)
        for r in range(4):
            queue = nc.scalar if r % 2 else nc.sync
            queue.dma_start(
                out=out_2[:, r:16:4, :].rearrange("c q m -> q c m").bitcast(I32),
                in_=y_planes[r:P:32, :, :].bitcast(I32),
            )
